import numpy as np, ml_dtypes
CORES = [36,164,52,180,100,228,116,244]
N = 8
BF = ml_dtypes.bfloat16
def gentries(a):
    return np.ascontiguousarray(a.reshape(8, 16, -1).transpose(0, 2, 1)).reshape(8, -1)
def gtable(e):
    e = np.asarray(e); return np.ascontiguousarray(e.reshape(8, -1, 16).transpose(0, 2, 1)).reshape(128, -1).astype(np.int32)
P, M, B, R, VI, HO, NEED = 4096, 4096, 128, 16, 3, 3, 12
F, C, TM = B // 2, M // (B // 2), R // 2
HALF = (16 - NEED) // 2
def stock(rng):
    mem = np.stack([rng.permutation(M) for g in range(8)]); fo = np.zeros((8, M), np.int64)
    np.put_along_axis(fo, mem, np.tile(np.repeat(np.arange(F), C), (8, 1)), 1)
    ml = rng.choice(np.array([1, 1, 2, 2, 3, 3, 4, 5, 6, TM]), (8, F))
    st = rng.integers(1, F, (8, F, TM)); st[:, :, 0] = np.arange(F)
    return mem.reshape(8, F, C), fo, ml, np.add.accumulate(st, axis=2) % F
def runs(rng, st, fam, same):
    mem, fo, ml, mot = st; sh = fam.shape + (R,); gi = np.arange(8)[:, None]; gj = np.arange(8)[:, None, None]; s = np.arange(R)
    n = ml[gi, fam]; ln = np.minimum(n + rng.integers(0, n + 2), R)
    key = rng.random(sh); key[..., 0] = -1.0; key = np.where(s < ln[..., None], key, 2.0)
    k = np.add.accumulate((np.argsort(np.argsort(key, axis=-1), axis=-1) < n[..., None]).astype(np.int64), axis=-1) - 1
    k = np.minimum(k, TM - 1); fs = mot[gi, fam]; nm = mem[gj, fs, rng.integers(0, C, fs.shape)]
    t = np.take_along_axis(nm, k, -1); alike = mem[gj, np.take_along_axis(fs, k, -1), rng.integers(0, C, sh)]
    hit = (s == ln[..., None] - 1) | (rng.random(sh) < 0.06)
    return ln, np.where(hit, np.where(rng.random(sh) < same, t, alike), rng.integers(0, M, sh)), t
def voices(rng, st, base, alts, mode):
    x = base[:, np.arange(8)[:, None], st[1]]; pool = np.argsort(rng.random((256, 16)), axis=-1)
    m = pool[rng.integers(0, 256, (N, 8, M))] < rng.choice(np.array(alts), (N, 8, M))[..., None]
    if mode == "flip": y = -x
    elif mode == "near": y = np.where(x == 15, 14, x + 1)
    else: y = (x + 15 + rng.integers(1, 31, x.shape)) % 31 - 15
    return np.where(m, y, x)
def parts(rng, same=0.3, lo=F, mode="any", alts=(0, 1, HALF, HALF, HALF + 1), base=None, skew=1):
    st = stock(rng); fo = st[1]; gi = np.arange(8)[:, None]; s = np.arange(R)
    if base is None: base = rng.integers(-15, 16, (N, 8, F, 16))
    d = {"fo": fo, "x": voices(rng, st, base, alts, mode)}
    cf = np.argsort(rng.random((N, 8, B)), axis=-1) // 2; own = np.argsort(cf, axis=-1, kind="stable").reshape(N, 8, F, 2)
    ln, u, t = runs(rng, st, cf, same); d["cf"] = cf
    d["bl"] = np.where(rng.random(ln.shape) < 0.15, np.maximum(ln - 1, 1), ln); d["bu"] = u; d["bt"] = t
    bk = own[np.arange(N)[:, None, None], gi, fo[None], rng.integers(0, 2, (N, 8, M))]; v = rng.random(bk.shape)
    d["bk"] = np.where(v < 0.1, -1, np.where(v < 0.16, rng.integers(0, B, bk.shape), bk))
    ln, u, t = runs(rng, st, (lo * rng.random((N, 8, P // 2)) ** skew).astype(np.int64), same); m = s < ln[..., None]
    d["pu"] = np.stack([np.stack([np.resize(u[q, g][m[q, g]], P) for g in range(8)]) for q in range(N)])
    d["pt"] = np.stack([np.stack([np.resize(t[q, g][m[q, g]], P) for g in range(8)]) for q in range(N)])
    d["pn"] = np.where(rng.random((N, 8)) < 0.3, P, rng.integers(3 * P // 4, P + 1, (N, 8)))
    d["th"] = rng.integers(550, 850, (N, 8))
    return d
def pack(d):
    i = lambda a, *sh: np.ascontiguousarray(np.reshape(a, (N, 8) + sh)).astype(np.int32)
    return {"tones": np.ascontiguousarray(d["x"].transpose(0, 1, 3, 2)).reshape(N, 128, M).astype(np.float32).astype(BF),
            "pu": np.stack([gtable(a) for a in d["pu"]]), "pt": np.stack([gtable(a) for a in d["pt"]]), "pn": i(d["pn"], 1),
            "bu": i(d["bu"], B * R), "bt": i(d["bt"], B * R), "bl": i(d["bl"], B), "bk": i(d["bk"], M), "th": i(d["th"], 1)}
def signs(rng, *sh):
    return 15 * (2 * rng.integers(0, 2, sh) - 1)
def setup_inputs(rng):
    return pack(parts(rng))
def setup_inputs_spread(rng):
    b = rng.integers(-15, 16, (N, 8, F, 16)); b = np.sign(b) * (np.abs(b) >> rng.choice(np.array([0, 0, 0, 1, 2, 3]), (N, 8, F, 1)))
    d = parts(rng, same=0.5, base=b, skew=3)
    w = (2 * rng.integers(0, 2, (N, 8)) - 1) * np.minimum(np.exp2(12 * rng.random((N, 8))).astype(np.int64), 3600)
    d["th"] = np.where(rng.random((N, 8)) < 0.4, w, rng.integers(150, 900, (N, 8)))
    d["pn"] = np.where(rng.random((N, 8)) < 0.3, np.minimum(np.exp2(12 * rng.random((N, 8))).astype(np.int64), P), rng.integers(1, P + 1, (N, 8)))
    d["bk"] = np.where(rng.random((N, 8, M)) < 0.25, rng.integers(-1, B, (N, 8, M)), d["bk"])
    return pack(d)
def poles(rng, sh):
    mt = rng.integers(0, 3, sh + (1,)); mu = rng.integers(0, 3, sh + (1,)); a = rng.integers(0, 2, sh + (R,))
    t = np.where(mt == 0, a, np.where(mt == 1, a[..., :1], np.arange(R) % 2)); u = np.where(mu == 0, rng.integers(0, 2, sh + (R,)), np.where(mu == 1, t, 1 - t))
    return u * (M - 1), t * (M - 1)
def setup_inputs_ends(rng):
    lo = F // 4; d = parts(rng, same=0.8, lo=lo, mode="flip", base=signs(rng, N, 8, F, 16)); x = d["x"]
    v = signs(rng, N, 8, 16); x[:, :, 0] = v; x[:, :, M - 1] = -v
    m = rng.random((N, 8, P // R, 1)) < 0.75; u, t = poles(rng, (N, 8, P // R))
    d["pu"] = np.where(m, u, d["pu"].reshape(u.shape)).reshape(N, 8, P); d["pt"] = np.where(m, t, d["pt"].reshape(u.shape)).reshape(N, 8, P)
    dead = d["cf"] >= lo; u, t = poles(rng, (N, 8, B)); one = np.where(rng.random((N, 8, B)) < 0.5, 1, R)
    dead[..., 0] = True; dead[..., B - 1] = True
    d["bl"] = np.where(dead, one, d["bl"]); d["bu"] = np.where(dead[..., None], u, d["bu"]); d["bt"] = np.where(dead[..., None], t, d["bt"])
    d["bk"] = np.where(d["fo"][None] < lo, d["bk"], np.where(rng.random((N, 8, M)) < 0.5, -1, B - 1)); d["bk"][..., 0] = 0; d["bk"][..., M - 1] = B - 1
    d["bt"][:, :, 0] = 0; d["bt"][:, :, B - 1] = M - 1; turn = np.where(np.arange(R) % 2 == 0, M - 1, 0)
    for q in range(N):
        d["th"][q, rng.permutation(7)] = np.array([3600, 3600, -3600, -3600, -3600, 3151, 3150]); d["th"][q, 7] = 3600
        d["pn"][q, rng.permutation(7)] = np.array([1, 1, P, P, P, P - 1 - int(rng.integers(0, R)), P // 2 + int(rng.integers(0, R))]); d["pn"][q, 7] = P
        d["pt"][q, 7, P - R:] = turn; d["pu"][q, 7, P - R:] = M - 1 - turn; d["pu"][q, 7, P - 1] = turn[R - 1]
        for g in range(8):
            if d["th"][q, g] == 3600: d["bt"][q, g, B - 1] = turn; d["bl"][q, g, B - 1] = R
    return pack(d)
def setup_inputs_corners(rng):
    d = parts(rng); x = d["x"]; sh = int(rng.integers(0, 8)); s = np.arange(R)
    for g in range(8):
        kind = (g + sh) % 8; nm = rng.permutation(M); e, z, rest = nm[:12], nm[12], nm[13:]; lx = rng.integers(2, R + 1, 12); grow = int(np.sum(lx - 1))
        if kind == 7:
            d["bk"][::2, g] = -1; d["pn"][:, g] = P; continue
        for q in range(N):
            x[q, g, nm[:13]] = signs(rng, 13, 16); d["th"][q, g] = 3600; cs = rng.permutation(B)[:12]
            d["bk"][q, g] = -1; d["bk"][q, g, e] = cs; ln = lx
            a = rest[rng.integers(0, len(rest), P)]; b = rest[rng.integers(0, len(rest), P)]; at = R * (1 + rng.permutation(P // (2 * R) - 1)[:12])
            if kind == 4: at[0] = P - R
            ix = at[:, None] + s
            n = P; bt = np.repeat(e[:, None], R, axis=1)
            if kind == 0:
                n = 1; a[0] = e[0]; b[0] = e[0]; ln = np.full(12, 1 + q % 3)
            elif kind <= 4:
                a[at] = e; b[at] = e; a[at - 1] = z; b[at - 1] = z
                if kind == 4: ln = np.full(12, R)
                else: n = P - grow + (0, 0, -1, 1)[kind]
            elif kind == 5:
                a[ix] = e[:, None]; b[ix] = e[:, None]; ln = rng.choice(np.array([1, 2, 3]), 12)
            else:
                bt = np.where(s % 2 == 0, e[:, None], z); a[ix] = bt; ln = R - np.arange(12) % 2
            d["pt"][q, g] = a; d["pu"][q, g] = b; d["pn"][q, g] = n
            d["bl"][q, g, cs] = ln; d["bt"][q, g, cs] = bt; d["bu"][q, g, cs] = rest[rng.integers(0, len(rest), (12, R))]; d["bu"][q, g, cs, ln - 1] = e
    return pack(d)
def setup_inputs_crowd(rng):
    d = parts(rng); x = d["x"]; sh = int(rng.integers(0, 8)); nb = P // R
    full = min(nb, B); at = R * (np.arange(full) * (nb - 1) // (full - 1)); ix = at[:, None] + np.arange(R)
    for g in range(8):
        kind = (g + sh) % 8
        if kind == 3: continue
        if kind >= 4:
            nm = rng.permutation(M); e, rest = nm[:full], nm[full:]
            lo = 1 if kind == 6 or P - full * R + 3 * full // 2 > 280 else 3
            for q in range(N):
                x[q, g, e] = signs(rng, full, 16); d["th"][q, g] = 3600
                cs = rng.permutation(np.append(1 + rng.permutation(B - 2)[:full - 2], [0, B - 1]))
                d["bk"][q, g] = -1; d["bk"][q, g, e] = cs
                a = rest[rng.integers(0, len(rest), P)]; b = rest[rng.integers(0, len(rest), P)]
                if kind <= 5:
                    a[at] = e; b[at] = e; ln = np.full(full, R)
                else:
                    a[ix] = e[:, None]; b[ix] = e[:, None]; ln = lo + np.arange(full) % 2
                d["pt"][q, g] = a; d["pu"][q, g] = b; d["pn"][q, g] = P
                d["bl"][q, g, cs] = ln; d["bt"][q, g, cs] = e[:, None]; d["bu"][q, g, cs] = rest[rng.integers(0, len(rest), (full, R))]; d["bu"][q, g, cs, ln - 1] = e
            continue
        nm = rng.permutation(M)[:4]
        for q in range(N):
            x[q, g, nm] = signs(rng, 4, 16); cs = rng.permutation(B)[:3]; ln = rng.choice(np.array([2, 3, R - 1, R]), 3)
            d["bk"][q, g, nm] = np.append(cs, -1); d["bl"][q, g, cs] = ln; d["bt"][q, g, cs] = nm[:3, None]; d["bu"][q, g, cs, ln - 1] = nm[:3]
            w = np.zeros(nb, np.int64)
            if kind == 1: w[int(rng.choice(np.array([0, nb - 1, int(rng.integers(0, nb))])))] = 1
            if kind == 2: w = rng.integers(0, 3, nb)
            t = np.where(np.arange(P) % 2 == 0, nm[np.repeat(w, R)], nm[3])
            d["pt"][q, g] = t; d["pu"][q, g] = t; d["pn"][q, g] = P
    return pack(d)
def filler(rng, d, q, g, th, rest):
    d["th"][q, g] = th; d["pn"][q, g] = P; d["bk"][q, g] = -1
    d["pu"][q, g] = rest[rng.integers(0, len(rest), P)]; d["pt"][q, g] = rest[np.add.accumulate(rng.integers(1, len(rest), P)) % len(rest)]
def near(rng, a, n):
    i = rng.permutation(16)[:n]; y = np.array(a); y[i] = np.where(a[i] == 15, 14, a[i] + 1)
    return y
def lay(rng, n):
    s = np.arange(R); n = n[:, None]
    return np.sort(np.where(s < n, s, rng.integers(0, R, (len(n), R)) % n), axis=1)
def clones(rng, d, g):
    nm = rng.permutation(M); a = nm[:12 * R].reshape(12, R); b = nm[12 * R:24 * R].reshape(12, R); rest = nm[24 * R:]
    h = [int(v) for v in rng.integers(9, R + 1, 4)]; late = int(rng.integers(8, h[3]))
    na = np.array([3, 3, 2, h[0], h[1], R, h[2], R, h[3], 2, 1, 3]); nb = np.array([3, 2, 3, h[0], h[1], R, h[2], R, h[3], 1, 2, 3])
    for q in range(N):
        filler(rng, d, q, g, 3600, rest)
        x = rng.integers(-15, 16, (12, R, 16)); x[:3, 1] = x[:3, 0]; x[3, h[0] - 1] = x[3, h[0] - 2]; x[11, 1:3] = 0; y = np.array(x)
        y[1, 1] = x[1, 2]; x[2, 1] = y[2, 2]; x[9, 1] = 0; y[10, 1] = 0
        y[6, h[2] - 1] = near(rng, x[6, h[2] - 1], 17 - NEED); y[7, R - 1] = near(rng, x[7, R - 1], 16 - NEED); y[8, late] = near(rng, x[8, late], 17 - NEED)
        d["x"][q, g, a] = x; d["x"][q, g, b] = y; cs = rng.permutation(B)[:12]
        d["bk"][q, g, a[:, 0]] = cs; d["bk"][q, g, b[:, 0]] = cs
        ix = R * rng.permutation(P // R)[:12][:, None] + np.arange(R)
        d["pt"][q, g, ix] = np.take_along_axis(a, lay(rng, na), 1)
        d["bt"][q, g, cs] = np.take_along_axis(b, lay(rng, nb), 1); d["bu"][q, g, cs] = rest[rng.integers(0, len(rest), (12, R))]; d["bl"][q, g, cs] = R
def bound(rng, d, g, sg, ths):
    nm = rng.permutation(M); e, z, w, l, rest = nm[:16], nm[16:32], nm[32:96], nm[96:160], nm[160:]
    i = np.arange(16); pc = i & 1; bc = (i >> 1) & 1; s = np.arange(R); o = int(rng.integers(0, 4))
    for q in range(N):
        th = ths[(q + o) % 4]; filler(rng, d, q, g, th, rest)
        k = int(rng.integers(0, 16)); v = signs(rng, 16); v[k] = 1; up = sg * v; up[k] = th - sg * 3375; lo = np.array(up); lo[k] = up[k] - 1
        d["x"][q, g, e] = v; d["x"][q, g, w] = up; d["x"][q, g, l] = lo
        cs = rng.permutation(B)[:16]; d["bk"][q, g, e] = cs; at = R * rng.permutation(P // R)[:16]; t = np.where(s == 0, e[:, None], z[:, None])
        d["pt"][q, g, at[:, None] + s] = t; d["pu"][q, g, at] = np.where(pc == 1, l[rng.integers(0, 64, 16)], w[rng.integers(0, 64, 16)])
        d["bt"][q, g, cs] = t; d["bl"][q, g, cs] = np.where(bc == 1, R, 1)
        u = rest[rng.integers(0, len(rest), (16, R))]; u[:, 0] = np.where(bc == 1, l[rng.integers(0, 64, 16)], w[rng.integers(0, 64, 16)]); d["bu"][q, g, cs] = u
def singles(rng, d, g):
    pr = rng.permutation(M // 2); side = rng.integers(0, 2, 12); e = 2 * pr[:12] + side; y = 2 * pr[:12] + 1 - side
    rest = (2 * pr[12:, None] + np.arange(2)).reshape(-1)
    for q in range(N):
        filler(rng, d, q, g, -3600, rest)
        at = R * np.append(P // R - 1, rng.permutation(P // R - 1)[:11]) + R - 1; cs = rng.permutation(B)[:12]
        d["pt"][q, g, at] = e; d["pt"][q, g, at - 1] = y; d["pu"][q, g, at - 1] = y
        d["bk"][q, g, e] = cs; d["bl"][q, g, cs] = 1; d["bt"][q, g, cs, 0] = e; d["bu"][q, g, cs, 0] = rest[rng.integers(0, len(rest), 12)]
def setup_inputs_edge(rng):
    d = parts(rng, mode="near", alts=(HALF, HALF, HALF, HALF + 1)); x = d["x"]; sh = int(rng.integers(0, 8))
    m = rng.random((N, 8, P)) < 0.04; m[..., 0] = False; d["pt"] = np.where(m, np.roll(d["pt"], 1, axis=-1), d["pt"])
    for q in range(N):
        for g in range(8):
            if (g + sh) % 8 >= 4: continue
            u, t = d["pu"][q, g], d["pt"][q, g]; v = np.add.reduce(x[q, g][u] * x[q, g][t], axis=1)[:-1]
            v = np.unique(v[t[1:] != t[:-1]]); v = v[(v > 1026) & (v < 1300)]; w = v[np.isin(v - 1, v)]
            if len(w): d["th"][q, g] = rng.choice(w)
            elif len(v): d["th"][q, g] = rng.choice(v)
    for g in range(8):
        kind = (g + sh) % 8
        if kind == 4: clones(rng, d, g)
        elif kind == 5: bound(rng, d, g, -1, (-3375, -3371, -3372, -3378))
        elif kind == 6: bound(rng, d, g, 1, (3376, 3372, 3373, 3377))
        elif kind == 7: singles(rng, d, g)
    return pack(d)
def check_inputs(d):
    bad = []
    for k, lo, hi in (("tones", -15, 15), ("pu", 0, M - 1), ("pt", 0, M - 1), ("pn", 1, P), ("bu", 0, M - 1), ("bt", 0, M - 1), ("bl", 1, R), ("bk", -1, B - 1), ("th", -3600, 3600)):
        a = np.asarray(d[k]).astype(np.float32)
        if not np.all((a >= lo) & (a <= hi)): bad.append("range of " + k)
        elif k == "tones" and np.any(a != np.rint(a)): bad.append("whole numbers in tones")
        elif k == "tones" and np.any((a == 0) & np.signbit(a)): bad.append("-0.0 in tones")
    return bad
def tone_numbers(t, head):
    new = np.array(head); new[1:] |= t[1:] != t[:-1]; cnt = np.add.accumulate(new.astype(np.int64))
    return cnt - cnt[np.maximum.accumulate(np.where(head, np.arange(len(t)), 0))]
def visit(x, u, t, bu, bt, bl, bk, th):
    n = len(t); j = np.arange(n); s = np.arange(R)
    score = np.add.reduce(x[u] * x[t], axis=1)
    end = (j % R == R - 1) | (j == n - 1); end[:-1] |= (t[1:] != t[:-1]) & (score[:-1] >= th)
    head = np.ones(n, bool); head[1:] = end[:-1]
    first = np.flatnonzero(head); last = np.flatnonzero(end); size = last - first + 1
    k = tone_numbers(t, head)
    bh = np.zeros((B, R), bool); bh[:, 0] = True; kb = tone_numbers(bt.reshape(-1), bh.reshape(-1)).reshape(B, R)
    ci, si = np.nonzero(s < bl[:, None]); key = np.zeros((B, R), np.int64); key[ci, kb[ci, si]] = bt[ci, si]
    tones_of = kb[np.arange(B), bl - 1] + 1
    c = bk[t[first]]; c0 = np.maximum(c, 0)
    agree = np.add.reduce((x[t] == x[key[np.repeat(c0, size), k]]).astype(np.int64), axis=1) >= NEED
    match = (c >= 0) & (k[last] + 1 == tones_of[c0]) & (np.minimum.reduceat(agree.astype(np.int64), first) == 1)
    o = np.flatnonzero(match); o = o[np.unique(first[o] // R, return_index=True)[1]]
    o = o[np.unique(c[o], return_index=True)[1]]
    begin = np.array(first); length = np.array(size); begin[o] = n + c[o] * R; length[o] = bl[c[o]]
    before = np.add.accumulate(length) - length; src = (np.repeat(begin - before, length) + np.arange(np.sum(length)))[:P]
    nu = np.concatenate([u, bu.reshape(-1)])[src]; nt = np.concatenate([t, bt.reshape(-1)])[src]
    ix = np.minimum(first[o][:, None] + s, n - 1); bu, bt, bl = np.array(bu), np.array(bt), np.array(bl)
    bu[c[o]] = u[ix]; bt[c[o]] = t[ix]; bl[c[o]] = size[o]
    return nu, nt, bu, bt, bl
def reference(tones, pu, pt, pn, bu, bt, bl, bk, th):
    x = np.ascontiguousarray(tones.astype(np.float32).reshape(N, 8, 16, M).transpose(0, 1, 3, 2)).astype(np.int64)
    lu = np.stack([gentries(a) for a in pu]).astype(np.int64); lt = np.stack([gentries(a) for a in pt]).astype(np.int64)
    piece = {(r, g): (lu[r, g, :pn[r, g, 0]], lt[r, g, :pn[r, g, 0]]) for r in range(N) for g in range(8)}
    u = bu.astype(np.int64).reshape(N, 8, B, R); t = bt.astype(np.int64).reshape(N, 8, B, R); ln = bl.astype(np.int64); pt_ = bk.astype(np.int64)
    for v in range(VI):
        for q in range(N):
            r = (q - HO * v) % N
            for g in range(8):
                a, b, u[q, g], t[q, g], ln[q, g] = visit(x[q, g], piece[r, g][0], piece[r, g][1], u[q, g], t[q, g], ln[q, g], pt_[q, g], int(th[q, g, 0]))
                piece[r, g] = (a, b)
    fu = np.full((N, 8, P), -1, np.int64); ft = np.full((N, 8, P), -1, np.int64)
    for q in range(N):
        for g in range(8):
            a, b = piece[(q - HO * (VI - 1)) % N, g]; fu[q, g, :len(a)] = a; ft[q, g, :len(b)] = b
    live = np.arange(R) < ln[..., None]
    return {"yu": np.stack([gtable(a) for a in fu]).astype(np.float32), "yt": np.stack([gtable(a) for a in ft]).astype(np.float32),
            "zu": np.where(live, u, -1).reshape(N, 8, B * R).astype(np.float32), "zt": np.where(live, t, -1).reshape(N, 8, B * R).astype(np.float32)}

@@ -1,0 +1,750 @@
+from concourse.mybir import AluOpType, AxisListType, ActivationFunctionType
+
+BF, F32, I32, U16 = "bfloat16", "float32", "int32", "uint16"
+BOOK = 6144
+OPT = {"ES": 0, "XS": 96, "E0": 1, "E1": 1}
+
+
+def _s(n, d):
+    return ("sbuf", [128] + (list(n) if isinstance(n, (list, tuple)) else [n]), d)
+
+
+SCRATCH = {
+    "TN": _s(4112, BF), "W": _s(8192, BF), "SCW": _s(6432, BF), "XT": _s(8192, BF), "PR": _s(4096, BF), "CO": _s(4096, BF),
+    "EQ": _s(4096, BF), "EO": _s(4096, BF), "FO": _s(2048, BF), "XB": _s(2064, BF), "TB": _s(4128, BF), "N99": _s(2064, BF),
+    "OFF0": _s(512, U16), "OFF1": _s(512, U16), "OFF2": _s(512, U16), "OUT0": _s(512, U16), "OUT1": _s(512, U16),
+    "LND1": _s(1024, BF), "LND2": _s(1024, BF), "STG0": ("dram", [128, 1024], BF), "STG1": ("dram", [128, 1024], BF),
+    "PI": _s(512, I32), "JI": _s(256, F32), "Y0": _s(512, F32), "DG": _s(1024, BF), "BKI": _s(256, I32), "RW": _s([4, 256], BF),
+    "BI": _s([2, 128], I32), "BX": _s([2, 128], F32), "BD": _s([4, 128], BF), "SM": _s(144, I32), "SMF": _s(16, F32), "BLF": _s(256, F32),
+    "PMI": _s(2, I32), "COL": _s(8, F32), "J16": _s(256, F32),
+    "ONE": _s(256, F32), "ONEB": _s(128, BF), "ID": _s(128, BF), "IDF": _s(128, F32), "ID16": _s(128, BF), "ID129": _s(128, BF),
+    "M15": _s(128, F32), "MK8": _s(128, F32), "THX": _s(128, F32), "THT": _s(128, F32),
+    "EQF": _s(64, BF), "SEL": _s([4, 24], BF), "GS": _s([2, 32], BF), "UZ": _s(144, BF), "UU": _s([3, 160], BF), "UTRI": _s([16, 128], BF),
+    "S128": _s([8, 128], BF), "V1": _s(240, BF), "BS": _s([8, 128], BF), "ZL": _s([8, 128], BF), "ZA": _s(136, F32), "RT": _s(256, BF),
+    "DGM": _s(256, F32), "DM": _s(256, F32), "CONT16": _s(256, F32), "BARC": _s(128, F32), "C16R": _s(128, BF), "NTC": _s(8, F32),
+    "NEQ": _s([2, 144], BF), "END": _s([2, 144], BF), "CNT": _s([2, 144], BF), "GEQ": _s([2, 128], BF), "K16": _s([2, 128], BF),
+    "AC": _s([2, 128], BF), "C16": _s([2, 128], BF), "RR": _s([2, 128], BF), "ZT": _s([2, 128], BF), "IDX": _s(256, U16),
+    "PC": _s([2, 256], BF), "MN": _s(128, BF), "MT": _s(128, BF), "ST": _s(128, F32), "FI": _s(128, BF), "YC": _s(256, BF),
+    "FB": _s([2, 8], F32), "TI": _s([4, 8], I32), "TF": _s([8, 8], F32), "X1": _s(128, BF), "X2": _s(128, BF), "X3": _s(128, BF),
+    "YS": _s(256, BF), "Y3": _s(128, BF), "MG": _s([8, 128], BF), "LRS": _s(256, F32), "LV": _s(256, F32), "LS": _s(256, F32),
+    "EL": _s(16, U16), "FL": _s(128, U16), "LOC": _s(272, F32), "C16F": _s(128, F32), "SRC": _s(256, F32), "SRU": _s(256, U16),
+    "ETS": _s([2, 512], BF), "YO": _s([2, 256], F32), "ZO": _s(256, F32), "RS": _s([8, 16, 16], BF),
+    "BL": _s(128, U16), "NEWB": _s(128, BF), "CN": _s(128, BF), "CM": _s([16, 128], BF), "PL": _s(128, U16), "NL": _s(128, BF),
+    "NTF": _s(8, F32), "NTL": _s(8, U16), "XL": _s(128, BF), "XK": _s(1024, BF), "IDN": _s(128, BF),
+    "B0": ("psum", [128, 512], F32), "B1": ("psum", [128, 512], F32), "B2": ("psum", [128, 512], F32), "B3": ("psum", [128, 512], F32),
+    "B4": ("psum", [128, 512], F32), "B5": ("psum", [128, 512], F32), "B6": ("psum", [128, 16, 2, 16], F32), "B7": ("psum", [128, 16, 2, 16], F32),
+}
+GROUPS = ["small", "bl", "pp", "bk", "bb", "tn", "wr", "wb", "rc", "stg0", "stg1", "rows1", "rows2", "fo0", "fo1", "yo", "zo",
+          "arr10", "arr11", "arr20", "arr21", "arw1", "arw2", "sent", "t0", "t1", "t2", "xb0", "xb1", "dum", "dum2", "zs0", "zs1"]
+SEMAPHORES = ["cg", "cv", "cs", "ct"] + GROUPS
+SIZE = {BF: 2, F32: 4, I32: 4, U16: 2}
+AL = AluOpType
+AF = ActivationFunctionType
+
+
+def rank_program(g, core, T, topo):
+    rank = T.rank_of(core)
+    if rank is None:
+        return
+    ES, XS = OPT["ES"], OPT["XS"]
+    n_ranks = len(T.cores)
+    nxt = T.cores[(rank + 3) % n_ranks]
+    rid, pid = topo.addr(nxt, core)
+    mask = topo.mask(core, nxt)
+    n_eng = len(topo.engines(core, nxt))
+    n_in = len(topo.engines(T.cores[(rank - 3) % n_ranks], core))
+    Q = {"g": g, "v": g.vector, "s": g.scalar, "t": g.tensor, "y": g.sync}
+    ops, acc, grp = [], {}, {}
+
+    def A(name, *ix):
+        where, shape, d = SCRATCH[name]
+        ix = list(ix) + [slice(None)] * (len(shape) - len(ix))
+        pm = 0
+        for i in range(*ix[0].indices(128)):
+            pm |= 1 << i
+        lo = hi = 0
+        stride, em = 1, 1
+        for k in range(len(shape) - 1, 0, -1):
+            r = range(ix[k], ix[k] + 1) if isinstance(ix[k], int) else range(*ix[k].indices(shape[k]))
+            lo += r[0] * stride
+            hi += r[-1] * stride
+            if stride == 1 and r.step == 1:
+                em = ((1 << len(r)) - 1) << r[0]
+            else:
+                em = sum(em << (i * stride) for i in r)
+            stride *= shape[k]
+        z = SIZE[d]
+        return (T[name][tuple(ix)], [(name, pm, lo * z, (hi + 1) * z, em)])
+
+    def C(name, a, b=None, st=None):
+        return A(name, slice(None), slice(a, b, st))
+
+    def P(name, p0, p1, a=None, b=None, st=None):
+        return A(name, slice(p0, p1), slice(a, b, st))
+
+    def col(j):
+        return C("COL", j, j + 1)
+
+    def IND(win, off):
+        return (win[0].indirect(off[0]), win[1], off[1])
+
+    def X(ap):
+        return (ap, [])
+
+    def rec(eng, fn, outs, ins, group=None, inc=16):
+        rd, wr = [], []
+        for o in outs:
+            wr += o[1]
+            if len(o) > 2:
+                rd += o[2]
+        for i in ins:
+            if isinstance(i, tuple):
+                rd += i[1]
+                if len(i) > 2:
+                    rd += i[2]
+        me = len(ops)
+        deps = set()
+        for lst, w in ((rd, False), (wr, True)):
+            for (nm, pm, lo, hi, em) in lst:
+                ps = SCRATCH[nm][0] == "psum"
+                for (o, pm2, lo2, hi2, w2, em2) in acc.setdefault(nm, []):
+                    e2, g2 = ops[o]["eng"], ops[o]["grp"]
+                    same = e2 == eng and g2 is None and group is None
+                    if ps and not same:
+                        deps.add(o)
+                        continue
+                    if not (w or w2) or not (pm & pm2):
+                        continue
+                    if same and eng == "t":
+                        continue
+                    if (g2 is None) != (group is None):
+                        hit = lo // 16 <= (hi2 - 1) // 16 and lo2 // 16 <= (hi - 1) // 16
+                    else:
+                        hit = (em & em2) != 0
+                    if hit and not (group is not None and g2 == group):
+                        deps.add(o)
+        for lst, w in ((rd, False), (wr, True)):
+            for (nm, pm, lo, hi, em) in lst:
+                acc[nm].append((me, pm, lo, hi, w, em))
+        ops.append({"eng": eng, "fn": fn, "deps": deps, "grp": group, "inc": inc})
+        if group is not None:
+            grp.setdefault(group, []).append(me)
+
+    def ap(x):
+        return x[0] if isinstance(x, tuple) else x
+
+    def ts(out, in0, s1, op0, s2=None, op1=None):
+        if op1 is None:
+            rec("v", lambda: g.vector.tensor_scalar(out[0], in0[0], ap(s1), None, op0), [out], [in0, s1])
+        else:
+            rec("v", lambda: g.vector.tensor_scalar(out[0], in0[0], ap(s1), ap(s2), op0, op1), [out], [in0, s1, s2])
+
+    def tt(out, a, b, op):
+        rec("v", lambda: g.vector.tensor_tensor(out[0], a[0], b[0], op), [out], [a, b])
+
+    def cp(out, a):
+        rec("v", lambda: g.vector.tensor_copy(out[0], a[0]), [out], [a])
+
+    def ms(out, val):
+        rec("v", lambda: g.vector.memset(out[0], val), [out], [])
+
+    def scan(out, d0, d1, init, op0, op1):
+        rec("v", lambda: g.vector.tensor_tensor_scan(out[0], d0[0], d1[0], ap(init), op0, op1), [out], [d0, d1, init])
+
+    def red(out, a):
+        rec("v", lambda: g.vector.tensor_reduce(out[0], a[0], AxisListType.X, AL.min, apply_absolute_value=True), [out], [a])
+
+    def act(out, a, scale=None, bias=0.0):
+        if scale is None:
+            rec("s", lambda: g.scalar.activation(out[0], a[0], AF.Copy), [out], [a])
+        else:
+            rec("s", lambda: g.scalar.activation(out[0], a[0], AF.Identity, bias=ap(bias), scale=scale), [out], [a, bias])
+
+    def gat(eng, out, win, off):
+        (cp if eng == "v" else act)(out, IND(win, off))
+
+    def mm(out, l, r, start=True, stop=True):
+        rec("t", lambda: g.tensor.matmul(out[0], l[0], r[0], start, stop), [out], [l, r])
+
+    def width(x):
+        n = 1
+        for k in x[0].shape[1:]:
+            n *= k
+        return n
+
+    def iota(out, pat, base, cm, integer=False):
+        if integer:
+            rec("g", lambda: g.iota(out[0], pat, base, cm), [out], [])
+        else:
+            rec("g", lambda: g.iota(out[0], pat, base, cm, allow_small_or_imprecise_dtypes=True), [out], [])
+
+    def fill(out, val):
+        iota(out, [[0, width(out)]], val, 0)
+
+    def asel(out, a, pat, op, val, base, cm):
+        rec("g", lambda: g.affine_select(out[0], a[0], pat, op, val, base, cm), [out], [a])
+
+    def dma(eng, group, out, a, slow=False):
+        if slow:
+            rec(eng, lambda: g.dma_start(out[0], a[0], allow_slow_non_contiguous=True), [out], [a], group)
+        else:
+            rec(eng, lambda: Q[eng].dma_start(out[0], a[0]), [out], [a], group)
+
+    def send(out, a, sem):
+        rec("g", lambda: g.remote_dma(out[0], a[0], T.sem[sem], T.sem["sent"], pid, rid, mask), [], [a], "sent", 0)
+
+    def arrive(out, sem):
+        rec("x", None, [out], [], sem, n_in)
+
+    mult, add, sub, amax, amin = AL.mult, AL.add, AL.subtract, AL.max, AL.min
+    ge, gt, le, lt, eq, ne = AL.is_ge, AL.is_gt, AL.is_le, AL.is_lt, AL.is_equal, AL.not_equal
+    al = slice(None)
+    PM, PM16, PM17, INI, C16C, C16N = range(6)
+    BLK, TRI, SPOS, SF, SL, SLE, SE, UB = range(8)
+    UBT, UDF, USEL = range(3)
+
+    def B(k, a, b, p1=128, st=None):
+        if k < 6:
+            return P("B%d" % k, 0, p1, a, b, st)
+        return A("B%d" % k, slice(0, p1), slice(a // 32, b // 32))
+
+    def S128(k):
+        return A("S128", al, k)
+
+    def slide(k, s):
+        return A("UU", al, k, slice(16 - s, 144 - s))
+
+    def row(view, f, val):
+        asel(view, view, [[-16, 8]], ne, val, -f, 1)
+
+    def rows(out, src, lo, hi, n):
+        asel(out, src, [[-16, 8], [0, n]], ge, 0.0, -lo, 1)
+        asel(out, out, [[16, 8], [0, n]], ge, 0.0, hi, -1)
+
+    def xk(nm, f):
+        return C(nm, f, 128, 16)
+
+    def book_compact(k, out, src, c0):
+        for s in range(16):
+            mm(out, slide(UBT if s == 15 else k, s), C(src, c0 + s, c0 + 2048, 16), s == 0, s == 15)
+
+    for v in (1, 2):
+        for h in (0, 1):
+            arrive(C("OFF%d" % v, 256 * h, 256 * h + 256), "arr%d%d" % (v, h))
+        arrive(A("LND%d" % v), "arw%d" % v)
+    dma("y", "small", P("SM", 0, 8, 0, 1), X(T.pn[:]))
+    dma("y", "small", P("SM", 0, 8, 1, 2), X(T.th[:]))
+    dma("y", "pp", C("PI", 256, 512), X(T.pt[:]))
+    dma("y", "pp", C("PI", 0, 256), X(T.pu[:]))
+    dma("y", "bk", A("BKI"), X(T.bk[:]))
+    dma("s", "bb", A("BI", al, 0), X(T.bu[:]))
+    dma("s", "bb", A("BI", al, 1), X(T.bt[:]))
+    dma("s", "tn", C("TN", 16, 4112), X(T.tones[:]))
+    dma("y", "bl", P("SM", 0, 8, 16, 144), X(T.bl[:]))
+    ms(A("ONE"), 1.0)
+    ms(C("W", BOOK - 16, 8192), 0.0)
+    ms(C("W", 0, 2064), 0.0)
+    ms(C("TN", 0, 16), 0.0)
+    act(A("N99"), C("W", BOOK - 16, 8192), 0.0, 99.0)
+    ts(A("BX"), A("BI"), 1.0, add)
+    cp(A("BD", al, slice(0, 4, 2)), A("BX"))
+    tt(A("BD", al, slice(1, 4, 2)), A("BX"), A("BD", al, slice(0, 4, 2)), sub)
+    for f in range(4):
+        dma("y", "wb", A("W", slice(4 + f, 128, 16), slice(BOOK, 8192)), A("BD", al, f))
+    ms(C("W", 2064, 4112), 0.0)
+    iota(A("RW", al, 1), [[0, 256]], 256, 256)
+    iota(A("RW", al, 2), [[1, 256]], 0, 0)
+    fill(A("RW", al, 3), 1)
+    iota(P("SMF", 0, 32, 2, 3), [[0, 1]], 0, 16)
+    asel(P("MK8", 0, 32), P("ONE", 0, 32, 0, 128), [[1, 128]], ge, 0.0, 0, -16)
+    asel(P("MK8", 0, 32), P("MK8", 0, 32), [[-1, 128]], ge, 0.0, 15, 16)
+    iota(A("JI"), [[16, 256]], 0, 1)
+    iota(C("PMI", 0, 1), [[0, 1]], 0, 1, True)
+    ts(A("RW", al, 0), A("BKI"), 1.0, add)
+    for f in range(4):
+        dma("y", "wr", A("W", slice(f, 128, 16), slice(16, 4112)), A("RW", al, f))
+    cp(P("SMF", 0, 8, 0, 2), P("SM", 0, 8, 0, 2))
+    mm(B(0, 0, 1), P("MK8", 0, 8), P("SMF", 0, 8, 0, 1), True, False)
+    mm(B(0, 0, 1), P("MK8", 0, 8), P("SMF", 0, 8, 2, 3), False, True)
+    ts(C("OFF0", 0, 256), C("PI", 0, 256), 16.0, add)
+    ts(A("JI"), A("JI"), B(0, 0, 1), ge, -8192.0, mult)
+    tt(C("Y0", 256, 512), C("PI", 256, 512), A("JI"), add)
+    ts(C("OFF0", 256, 512), C("Y0", 256, 512), -1.0, amax, 16.0, add)
+    dma("y", "t0", C("TB", 2064, 4128), A("N99"))
+    fill(A("UU"), 0)
+    for k in (UBT, UDF):
+        for f in (6, 7):
+            row(A("UU", al, k, slice(16, 144, 16)), f, 1.0)
+    for f in (6, 7):
+        row(A("UU", al, UDF, slice(17, 145, 16)), f, -1.0)
+    book_compact(UBT, B(6, 0, 128), "W", BOOK)
+    book_compact(UDF, B(7, 0, 128), "W", BOOK)
+    asel(A("IDF"), C("ONE", 0, 128), [[-1, 128]], eq, 0.0, 0, 1)
+    asel(S128(TRI), C("ONE", 0, 128), [[-16, 8], [0, 16]], ge, 0.0, 0, 1)
+    asel(S128(TRI), S128(TRI), [[16, 8], [1, 16]], ge, 0.0, 0, -1)
+    asel(S128(TRI), S128(TRI), [[16, 8], [0, 16]], ge, 0.0, 15, -1)
+    fill(A("SEL"), 0)
+    row(A("SEL", al, 0, slice(0, 8)), 0, 1.0)
+    for f in (1, 2):
+        row(A("SEL", al, 0, slice(8, 16)), f, -1.0)
+        row(A("SEL", al, 2, slice(8, 16)), f, 1.0)
+    row(A("SEL", al, 2, slice(16, 24)), 3, -8192.0)
+    fill(A("SEL", al, 1, slice(8, 16)), -1)
+    rows(A("SEL", al, 3, slice(16, 24)), C("ONE", 0, 8), 0, 15, 1)
+    rows(A("UU", al, USEL, slice(16, 144, 16)), C("ONE", 0, 8), 0, 15, 1)
+    rows(S128(BLK), C("ONE", 0, 128), 0, 15, 16)
+    iota(A("J16"), [[0, 16], [1, 16]], 0, 0)
+    iota(A("C16R"), [[16, 128]], 0, 0)
+    iota(A("NTC"), [[256, 8]], 15, 0)
+    fill(C("XB", 2048, 2064), 0)
+    fill(C("TB", 0, 16), 99)
+    fill(A("ONEB"), 1)
+    for nm, val in (("NEQ", 16), ("END", 16), ("CNT", 0)):
+        fill(A(nm, al, al, 0), val)
+    asel(A("CONT16"), A("ONE"), [[0, 16], [1, 16]], gt, 0.0, 0, 0)
+    LM1, ONEL, TK, NTK, TMP = [A("TF", al, k) for k in range(5)]
+    ts(P("THX", 0, 8), P("MK8", 0, 8), P("SMF", 0, 8, 1, 2), mult)
+    mm(B(1, 0, 128), P("ONE", 0, 8, 0, 128), P("THX", 0, 8))
+    ts(P("BLF", 0, 8, 0, 128), P("SM", 0, 8, 16, 144), -1.0, add)
+    ts(P("BLF", 0, 8, 128, 256), P("SM", 0, 8, 16, 144), 1.0, eq, 16384.0, mult)
+    ts(C("PMI", 1, 2), C("PMI", 0, 1), 15, AL.bitwise_and)
+    tt(P("BLF", 0, 8, 128, 256), P("BLF", 0, 8, 128, 256), P("BLF", 0, 8, 0, 128), add)
+    cp(col(PM), C("PMI", 1, 2))
+    mm(B(3, 128, 384), P("MK8", 0, 8), P("BLF", 0, 8))
+    mm(B(2, 0, 8), P("BLF", 0, 8, 0, 128), P("IDF", 0, 8, 0, 8))
+
+    def small_constants():
+        act(A("THT"), B(1, 0, 128), 1.0, -8192.0)
+        act(C("THT", 15, 128, 16), C("ONE", 0, 8), -1000000.0)
+        act(A("LRS"), B(3, 128, 384))
+        act(LM1, B(2, 0, 8))
+        act(A("ID16"), A("IDF"), 1.0 / 16)
+        act(A("ID129"), A("IDF"), 129.0)
+        act(A("IDN"), A("IDF"), -1.0)
+        act(col(PM16), col(PM), 16.0)
+        act(col(PM17), col(PM), 17.0)
+        act(col(INI), col(PM), 1.0, -16.0)
+
+    asel(A("EQF"), C("ONE", 0, 64), [[-1, 8], [-16, 8]], eq, 0.0, 0, 1)
+    iota(A("DM"), [[1, 256]], BOOK, 0)
+    fill(A("BARC"), 2)
+    fill(C("BARC", 0, 128, 16), 0)
+    fill(A("GS"), 0)
+    rows(A("GS", al, 0, slice(0, 8)), C("ONE", 0, 8), 0, 15, 1)
+    rows(A("GS", al, 1, slice(8, 16)), C("ONE", 0, 8), 0, 15, 1)
+    iota(P("RT", 0, 32), [[0, 2], [1, 128]], 0, 0)
+    asel(P("RT", 0, 32), P("RT", 0, 32), [[0, 256]], ne, -65536.0, -17, 1)
+    Z0, Z1 = P("ZA", 0, 32, 0, 128), P("ZA", 0, 32, 128, 136)
+    iota(Z0, [[1, 128]], 1, 0)
+    asel(Z0, Z0, [[0, 128]], eq, 0.0, -17, 1)
+    asel(Z0, Z0, [[0, 128]], ne, 256.0, -16, 1)
+    fill(Z1, 0)
+    asel(Z1, Z1, [[-1, 8]], ne, 65536.0, 0, 1)
+    asel(Z1, Z1, [[-1, 8]], ne, 1.0, -8, 1)
+    for nm in ("X1", "X2", "X3"):
+        fill(A(nm), 0)
+    iota(xk("X1", 0), [[0, 8]], 0, 16)
+    fill(xk("X1", 1), BOOK)
+    iota(xk("X2", 5), [[0, 8]], 0, -16)
+    fill(xk("X2", 8), -BOOK)
+    iota(col(C16C), [[0, 1]], 0, 16)
+    iota(col(C16N), [[0, 1]], 0, -16)
+    fill(S128(SPOS), -1)
+    rows(S128(SPOS), S128(SPOS), 2, 4, 16)
+    for k, lo, hi in ((SF, 0, 3), (SL, 4, 4), (SLE, 4, 5), (SE, 5, 8), (UB, 0, 8)):
+        rows(S128(k), C("ONE", 0, 128), lo, hi, 16)
+    fill(A("V1"), 0)
+    fill(C("V1", 112, 128), 1)
+    for s in range(16):
+        asel(A("UTRI", al, s), S128(UB), [[16, 8], [9, 16]], ge, 0.0, 4 - 9 * s, -1)
+    rows(A("M15"), C("ONE", 0, 128), 15, 15, 16)
+    asel(A("M15"), A("M15"), [[-1, 128]], ne, -1.0, 0, 1)
+    row(C("M15", 15, 128, 16), 15, 0.0)
+    fill(A("C16F"), 16)
+    fill(C("LOC", 0, 1), 0)
+    fill(A("UZ"), 0)
+    for k in (0, 1):
+        for f in (4, 5):
+            row(C("UZ", 8 + 64 * k, 72 + 64 * k, 8), f + 2 * k, 1.0)
+
+    def clear_steps(group):
+        for f in range(9):
+            dma("y", group, A("SCW", slice(f, 128, 16), slice(16, 4112)), A("W", slice(9, 128, 16), slice(0, 4096)))
+
+    dma("y", "dum", C("SCW", 0, 4112), A("TN"))
+    dma("y", "dum", C("W", 4112, BOOK - 16), C("TN", 0, BOOK - 4128))
+    dma("y", "dum", C("XT", 4096, BOOK), C("TN", 0, 2048))
+    clear_steps("dum2")
+    for f in range(4):
+        dma("y", "dum2", A("W", slice(4 + f, 128, 16), slice(4112, BOOK - 16)), A("W", slice(9, 128, 16), slice(0, BOOK - 4128)))
+
+    def pickers():
+        for gi in range(8):
+            act(A("ZL", slice(0, 32), gi), Z0, 1.0, P("ZA", 0, 32, 128 + gi, 129 + gi))
+        for gi in range(8):
+            act(A("BS", al, gi), C("ONE", 0, 128), 0.0, C("EQF", 16 + gi, 17 + gi))
+
+    def single_items():
+        ts(ONEL, LM1, 0.0, eq)
+        ts(xk("X1", 5), ONEL, col(C16N), mult)
+        ts(xk("X1", 8), ONEL, -float(BOOK), mult)
+
+    def book_new():
+        ts(A("NEWB"), B(7, 0, 128), 0.0, ne)
+        mm(B(6, 0, 128), S128(TRI), A("NEWB"))
+
+    def book_places(k0, k1):
+        for k in range(k0, k1):
+            ts(A("CM", al, k), A("CN"), float(k), le)
+            mm(B(7, 0, 128), slide(USEL, k), A("CM", al, k), k == 0, False)
+        if k1 == 16:
+            mm(B(7, 0, 128), A("ID"), A("C16R"), False, True)
+
+    def book_live():
+        ts(A("NL"), C("LRS", 0, 128), col(PM), ge)
+        tt(A("NL"), A("NL"), A("NEWB"), mult)
+        mm(B(1, 0, 128), S128(BLK), A("NL"))
+
+    def book_counts():
+        tt(C("LV", 0, 128), B(1, 0, 128), C("DGM", 0, 128), mult)
+        scan(C("LS", 0, 128), C("CONT16", 0, 128), C("LV", 0, 128), 0.0, mult, add)
+        tt(A("NTF"), C("LS", 15, 128, 16), A("NTC"), add)
+        cp(A("NTL"), A("NTF"))
+
+    def book_list():
+        cp(A("PL"), B(7, 0, 128))
+
+    def table1(eng, i, n):
+        w = 128 // n
+        gat(eng, C("TB", 16 + 16 * w * i, 16 + 16 * w * (i + 1)), A("XB"), C("PL", w * i, w * (i + 1)))
+
+    def table2():
+        cp(A("XL"), IND(C("TB", 0, 2064), A("NTL")))
+        cp(IND(C("TB", 2064, 4128), A("NTL")), A("XL"))
+
+    def natural_rows(step):
+        if step == 0:
+            tt(C("Y0", 0, 256), C("PI", 0, 256), A("JI"), add)
+            ts(A("Y0"), A("Y0"), -1.0, amax, 1.0, add)
+            for k in (0, 1):
+                act(C("DG", 512 * k, 512 * k + 256), C("Y0", 256 * k, 256 * k + 256))
+            return
+        if step == 1:
+            for k in (0, 1):
+                tt(C("DG", 512 * k + 256, 512 * k + 512), C("Y0", 256 * k, 256 * k + 256), C("DG", 512 * k, 512 * k + 256), sub)
+            return
+        for gp in (2 * step - 4, 2 * step - 3):
+            bank = "B%d" % (6 + gp % 2)
+            for bl in range(16):
+                mm(A(bank, slice(0, 64), bl), C("DG", bl, 1024, 16), C("ID", 32 * gp, 32 * gp + 32))
+            for k in (0, 1):
+                act(A("RS", slice(0, 64), 2 * gp + k), A(bank, slice(0, 64), al, k))
+
+    def visit(v):
+        off = "OFF%d" % v
+
+        def names(kind, q, lo, n):
+            c0 = lo + (256 * kind + 64 * q if v == 0 else 256 * (q // 2) + 128 * kind + 64 * (q % 2))
+            return C(off, c0, c0 + n)
+
+        def part(nm, q, lo, n):
+            return C(nm, 1024 * q + 16 * lo, 1024 * q + 16 * (lo + n))
+
+        def a(q, lo=0, n=64):
+            gat("s", part("XT", q, lo, n), A("TN"), names(1, q, lo, n))
+
+        def b(q, lo=0, n=64):
+            tt(part("PR", q, lo, n), IND(A("TN"), names(0, q, lo, n)), part("XT", q, lo, n), mult)
+
+        def c(q, eng):
+            gat(eng, part("CO", q, 0, 64), C("W", 0, 4112), names(1, q, 0, 64))
+
+        def H(nm, h, a0=0, n=128):
+            return A(nm, al, h, slice(a0, a0 + n))
+
+        def far(c0):
+            k = (c0 // 32) % 2
+            gat("s", C("XK", 512 * k, 512 * k + 512), A("TB"), C("IDX", c0, c0 + 32))
+            mm(A("B%d" % (6 + k)), A("IDN"), C("XT", 16 * c0, 16 * c0 + 512), True, False)
+            mm(A("B%d" % (6 + k)), A("ID"), C("XK", 512 * k, 512 * k + 512), False, True)
+
+        def same(c0):
+            out, ps = C("EQ", 16 * c0, 16 * c0 + 512), A("B%d" % (6 + (c0 // 32) % 2))
+            rec("s", lambda: g.scalar.activation(out[0], ps[0], AF.Abs), [out], [ps])
+            rec("s", lambda: g.scalar.activation(out[0], out[0], AF.Relu, bias=1.0, scale=-1.0), [out], [out])
+
+        def scores(h, s0=0, s1=16):
+            o = 2048 * h
+            for s in range(s0, s1):
+                out = B(h, s, 384, 128, 16)
+                mm(out, C("CO", o + s, o + 2048, 16), A("SEL", al, 0), True, False)
+                if s < 15:
+                    mm(out, C("CO", o + s + 1, o + 2048, 16), A("SEL", al, 2), False, False)
+                else:
+                    mm(out, A("ONEB"), A("SEL", al, 1), False, False)
+                mm(out, C("PR", o + s, o + 2048, 16), A("SEL", al, 3), False, True)
+
+        def passages(h):
+            ts(H("NEQ", h, 1), B(h, 128, 256), 0.0, ne, 16.0, mult)
+            tt(H("GEQ", h), B(h, 256, 384), A("THT"), ge)
+            tt(H("END", h, 1), H("NEQ", h, 1), H("GEQ", h), mult)
+            ts(H("CNT", h, 1), H("END", h, 1), 0.0, eq)
+            tt(H("AC", h), B(h, 0, 128), H("END", h), mult)
+            scan(H("K16", h), H("NEQ", h), H("CNT", h), 0.0, add, mult)
+            scan(H("C16", h), H("CNT", h), H("AC", h), 0.0, mult, add)
+            mm(B(h, 384, 512), H("K16", h), A("ID16"), True, False)
+            mm(B(h, 384, 512), H("END", h, 1), A("ID129"), False, False)
+            mm(B(h, 384, 512), H("C16", h), A("ID"), False, True)
+            scan(H("RR", h), A("ONEB"), H("CNT", h), 0.0, add, mult)
+            ts(H("ZT", h), H("CNT", h, 1), 87.0, mult, 12.0, add)
+            mm(B(2 + h, 0, 128), H("C16", h), A("ID"))
+            mm(B(2 + h, 128, 256), H("RR", h), A("ID"))
+
+        def index(h):
+            cp(C("IDX", 128 * h, 128 * h + 128), B(h, 384, 512))
+
+        def payload(h):
+            act(H("PC", h), B(2 + h, 0, 128), 1.0 / 16)
+            act(H("PC", h, 128), B(2 + h, 128, 256), -16.0, col(PM17))
+
+        def d(c0, n):
+            tt(C("EQ", 16 * c0, 16 * (c0 + n)), IND(A("TB"), C("IDX", c0, c0 + n)), C("XT", 16 * c0, 16 * (c0 + n)), eq)
+
+        def counts(h):
+            for s in range(16):
+                mm(B(2 + h, 256 + s, 384, 128, 16), C("EQ", 2048 * h + s, 2048 * h + 2048, 16), A("SEL", al, 3, slice(16, 24)))
+
+        def offers(h):
+            scan(A("MN"), H("END", h), B(2 + h, 256, 384), 0.0, amax, amin)
+            tt(A("MT"), A("MN"), H("ZT", h), ge)
+            scan(A("ST"), A("BARC"), A("MT"), 0.0, mult, add)
+            ts(A("FI"), A("ST"), 1.0, eq)
+            mm(B(2 + h, 384, 512), A("FI"), A("ID"))
+
+        def offer_rows(h, step):
+            if step == 0:
+                tt(C("YC", 0, 128), B(2 + h, 384, 512), H("PC", h), mult)
+                tt(C("YC", 128, 256), B(2 + h, 384, 512), H("PC", h, 128), mult)
+                mm(B(4, 0, 128, 32), A("GS", al, 0), C("YC", 0, 128), True, False)
+                mm(B(4, 0, 128, 32), A("GS", al, 1), C("YC", 128, 256), False, True)
+                return
+            act(P("RT", 0, 16, 128 * h, 128 * h + 128), B(4, 0, 128, 16))
+            for gi in range(8):
+                mm(B(4 + gi // 4, 128 * (gi % 4), 128 * (gi % 4) + 128), A("ZL", slice(0, 18), gi), P("RT", 0, 18, 128 * h, 128 * h + 128))
+
+        def lowest(h, k):
+            for gi in range(4 * k, 4 * k + 4):
+                red(A("FB", al, h, slice(gi, gi + 1)), B(4 + k, 128 * (gi % 4), 128 * (gi % 4) + 128))
+
+        if v == 0:
+            ts(A("BL"), B(6, 0, 128), 15.0, add)
+            c(0, "v"), book_new(), a(0), a(1), act(A("ID"), A("IDF"))
+            gat("s", C("XB", 0, 2048), A("TN"), A("BL"))
+            small_constants(), b(0)
+            dma("y", "xb0", C("XT", BOOK, 8192), C("XB", 0, 2048))
+            cp(A("CN"), B(6, 0, 128))
+            book_places(0, 16)
+            c(1, "v"), book_list(), b(1), scores(0), book_live()
+            table1("s", 0, 1), natural_rows(0), a(2), a(3), c(2, "s"), c(3, "s")
+            ts(A("DGM"), A("J16"), col(PM), eq)
+            ts(A("NTC"), A("NTC"), col(PM16), add)
+            passages(0), book_counts()
+            table2(), index(0), d(0, 128), counts(0), natural_rows(1), payload(0), pickers(), b(2)
+            natural_rows(2), offers(0), b(3), natural_rows(3), scores(1)
+            for gi in range(8):
+                dma("y", "rc", P("W", 16 * gi + 4, 16 * gi + 8, 0, 4096), A("RS", slice(0, 64), gi))
+            tt(A("DM"), A("DM"), A("DGM"), mult)
+            single_items()
+            offer_rows(0, 0), offer_rows(0, 1), passages(1), index(1), far(224), payload(1), d(128, 96)
+            same(224), counts(1), lowest(0, 0)
+        else:
+            c(0, "v"), a(0), a(1), c(1, "s"), a(2), a(3), c(2, "s"), c(3, "s")
+            b(0), table2(), b(1), scores(0), b(2), passages(0), b(3), index(0)
+            scores(1), far(96), d(0, 96), payload(0), same(96)
+            for f in range(4):
+                dma("y", "rows%d" % v, A("W", slice(4 + f, 128, 16), slice(0, 4096)), P("LND%d" % v, 32 * f, 32 * f + 32))
+            passages(1), counts(0), index(1), far(224), payload(1), d(128, 32), offers(0), same(224), d(160, 32), offer_rows(0, 0)
+            d(192, 32), offer_rows(0, 1), counts(1), lowest(0, 0)
+        if v < 2:
+            dma("y", "t%d" % (v + 1), C("TB", 2064, 4128), A("N99"))
+        F0, F1 = A("FB", al, 0), A("FB", al, 1)
+        offers(1), offer_rows(1, 0), lowest(0, 1), offer_rows(1, 1)
+        ts(TMP, F0, 32768.0, ge, 1048576.0, mult)
+        ts(F0, F0, -32768.0, add)
+        tt(F0, F0, TMP, add)
+        mm(B(6, 0, 128), A("IDF"), C("LRS", 128, 256), True, False)
+        lowest(1, 0), lowest(1, 1)
+        DL = xk("X3", 9)
+        VI, BB, FS, SEE = [A("TI", al, k) for k in range(4)]
+        tt(VI, F0, F1, amin)
+        ts(BB, VI, 8, AL.arith_shift_right)
+        ts(FS, VI, 4, AL.arith_shift_right, 15, AL.bitwise_and)
+        ts(SEE, VI, 15, AL.bitwise_and)
+        ts(xk("X2", 6), BB, 16.0, mult, 2048.0, add)
+        ts(xk("X1", 2), BB, -16.0, mult, -2048.0, add)
+        ts(xk("X1", 3), FS, -1.0, mult)
+        tt(xk("X2", 7), SEE, LM1, sub)
+        ts(xk("X1", 4), BB, 128.0, ge, -16384.0, mult)
+        tt(xk("X1", 6), xk("X2", 6), ONEL, mult)
+        tt(xk("X1", 7), xk("X2", 7), ONEL, mult)
+        mm(B(0, 0, 128), A("X1"), A("ID"))
+        mm(B(0, 128, 256), A("X2"), A("ID"))
+        act(A("YS"), B(0, 0, 256))
+        for gi in range(8):
+            mm(B(4 + gi // 4, 128 * (gi % 4), 128 * (gi % 4) + 128), A("BS", al, gi), C("YS", 0, 128))
+        ts(TK, BB, 128.0, lt)
+        ts(NTK, BB, 128.0, ge)
+        tt(DL, FS, xk("X2", 7), sub)
+        tt(xk("X3", 0), xk("X2", 6), TK, mult)
+        tt(xk("X3", 1), FS, TK, mult)
+        tt(TMP, DL, TK, mult)
+        ts(xk("X3", 2), NTK, col(C16C), mult)
+        ts(xk("X3", 3), NTK, float(BOOK), mult)
+        tt(xk("X3", 4), LM1, TMP, sub)
+        tt(LM1, LM1, TMP, sub)
+        ts(xk("X3", 5), xk("X3", 4), 0.0, eq, 16384.0, mult)
+        mm(B(1, 0, 128), A("X3"), A("ID"))
+        act(A("Y3"), B(1, 0, 128))
+        mm(B(2, 0, 128), S128(SPOS), C("YS", 0, 128), True, False)
+        mm(B(6, 0, 128), S128(SPOS), C("YS", 0, 128), False, False)
+        for gi in range(8):
+            ts(A("MG", al, gi), B(4 + gi // 4, 128 * (gi % 4), 128 * (gi % 4) + 128), C("X1", 16 * gi + 2, 16 * gi + 3), lt, C("X3", 16 * gi + 9, 16 * gi + 10), mult)
+            for k in (2, 6):
+                mm(B(k, 0, 128), C("V1", 112 - 16 * gi, 240 - 16 * gi), A("MG", al, gi), False, gi == 7)
+            if gi == 3:
+                for i, k in enumerate((SF, SL, SLE)):
+                    mm(B(3, 128 * i, 128 * i + 128), S128(k), A("Y3"))
+        if v < 2:
+            ts(A("FL"), B(3, 0, 128), col(PM), add)
+        else:
+            ts(C("SRC", 0, 128), B(3, 128, 256), col(PM), ge)
+            ts(C("SRC", 128, 256), B(3, 0, 128), col(PM), add, -4096.0, add)
+            tt(C("SRC", 0, 128), C("SRC", 0, 128), C("SRC", 128, 256), mult)
+            ts(A("FL"), C("SRC", 0, 128), 4096.0, add)
+        gat("s", A("FO"), A("W"), A("FL"))
+        if v < 2:
+            gat("s", C("XB", 0, 16 * XS), A("XT"), C("FL", 0, XS))
+        tt(C("LV", 0, 128), B(2, 0, 128), C("DM", 0, 128), amin)
+        tt(C("LV", 128, 256), B(6, 0, 128), C("DM", 128, 256), amin)
+        scan(A("LS"), A("CONT16"), A("LV"), 0.0, mult, add)
+        ts(A("EL"), C("LS", 15, 256, 16), 16.0, add)
+        cp(IND(A("SCW"), A("EL")), A("YS"))
+        if v < 2:
+            single_items()
+        for h in (0, 1):
+            o = 2048 * h
+            for s in range(16):
+                mm(B(6 + h, 0, 128), A("UTRI", al, s), C("SCW", 16 + o + s, 16 + o + 2048, 16), s == 0, s == 15)
+            cp(C("LOC", 1 + 128 * h, 129 + 128 * h), B(6 + h, 0, 128))
+        for h in (0, 1):
+            o = 2048 * h
+            mm(B(h, 0, 128), S128(SE), C("SCW", o + 15, o + 2048, 16), True, False)
+            mm(B(h, 0, 128), A("M15"), C("LOC", 128 * h, 128 * h + 128), False, False)
+            mm(B(h, 0, 128), A("IDF"), C("LOC", 1 + 128 * h, 129 + 128 * h), False, True)
+            scan(C("SRC", 128 * h, 128 * h + 128), A("C16F"), B(h, 0, 128), col(INI) if h == 0 else C("SRC", 127, 128), add, add)
+            cp(C("SRU", 128 * h, 128 * h + 128), C("SRC", 128 * h, 128 * h + 128))
+            for eng, lo, hi in ((("s", 0, 128),), (("s", 128, 128 + ES), ("v", 128 + ES, 256)))[h]:
+                if hi > lo:
+                    gat(eng, C("EO", 16 * lo, 16 * hi), A("W"), C("SRU", lo, hi))
+        if v < 2:
+            gat("s", C("XB", 16 * XS, 2048), A("XT"), C("FL", XS, 128))
+            if v == 0:
+                dma("y", "xb1", C("XT", BOOK, 8192), C("XB", 0, 2048))
+            book_compact(UDF, B(7, 0, 128), "FO", 0)
+        else:
+            for q in range(8):
+                mm(B(6, 0, 256), C("UZ", 8 - q, 136 - q), C("FO", 256 * q, 256 * q + 256), q == 0, q == 7)
+        for h in (0, 1):
+            for s in range(16):
+                mm(B(4 + h, s, 512, 128, 16), C("EO", 2048 * h + s, 2048 * h + 2048, 16), C("EQF", 32, 64))
+        if v < 2:
+            book_new()
+        for h in (0, 1):
+            (cp if v == 2 and h == 1 else act)(A("ETS", al, h), B(4 + h, 0, 512))
+            bk = 2 * h
+            for f in range(4):
+                mm(B(bk, 128 * (f // 2), 128 * (f // 2) + 128), H("ETS", h, 128 * f), A("ID"), f % 2 == 0, f % 2 == 1)
+            if v < 2:
+                if h == 0:
+                    cp(A("CN"), B(6, 0, 128))
+                else:
+                    act(A("LRS"), B(3, 128, 384))
+                    book_places(0, 6)
+                o = C("OUT%d" % v, 256 * h, 256 * h + 256)
+                ts(o, B(bk, 0, 256), 15.0, add)
+                send(C("OFF%d" % (v + 1), 256 * h, 256 * h + 256), o, "arr%d%d" % (v + 1, h))
+            else:
+                ts(A("YO", al, h), B(bk, 0, 256), -1.0, add)
+                dma("y", "yo", X(T.yu[:, 128 * h:128 * h + 128]), H("YO", h))
+                dma("y", "yo", X(T.yt[:, 128 * h:128 * h + 128]), H("YO", h, 128))
+        if v < 2:
+            for f in range(4):
+                dma("y", "stg%d" % v, A("STG%d" % v, slice(32 * f, 32 * f + 32)), A("EO", slice(4 + f, 128, 16)))
+            send(A("LND%d" % (v + 1)), A("STG%d" % v), "arw%d" % (v + 1))
+            for f in range(4):
+                dma("y", "fo%d" % v, A("W", slice(4 + f, 128, 16), slice(BOOK, 8192)), A("FO", slice(4 + f, 128, 16)))
+            clear_steps("zs%d" % v)
+            book_places(6, 16), book_live(), book_list(), table1("s", 1, 2), book_counts(), table1("v", 0, 2)
+        else:
+            act(A("ZO"), B(6, 0, 256), 1.0, -1.0)
+            dma("s", "zo", X(T.zu[:]), P("ZO", 0, 64))
+            dma("s", "zo", X(T.zt[:]), P("ZO", 64, 128))
+
+    for v in range(3):
+        visit(v)
+
+    know = {e: {} for e in Q}
+    seen, need, pos, cnt = [], set(), [], {e: 0 for e in Q}
+    for i, o in enumerate(ops):
+        e = o["eng"]
+        o["waits"] = []
+        if e == "x":
+            seen.append({}), pos.append(0)
+            continue
+        k = know[e]
+        for j in sorted(o["deps"], reverse=True):
+            gj = ops[j]["grp"]
+            key, val = (gj, 1) if gj is not None else (ops[j]["eng"], pos[j])
+            if k.get(key, 0) >= val:
+                continue
+            members = grp[gj] if gj is not None else [j]
+            assert max(members) < i
+            o["waits"].append(j)
+            need.add(j)
+            k[key] = val
+            for m in members:
+                for kk, vv in seen[m].items():
+                    if k.get(kk, 0) < vv:
+                        k[kk] = vv
+        cnt[e] += 1
+        pos.append(cnt[e])
+        seen.append(dict(k))
+    total = {e: 0 for e in Q}
+    val = {}
+    for i, o in enumerate(ops):
+        if o["grp"] is None and i in need:
+            total[o["eng"]] += 1
+            val[i] = total[o["eng"]]
+    gsum = {k: sum(ops[m]["inc"] for m in members) for k, members in grp.items()}
+    gsum["sent"] = n_eng * len(grp["sent"])
+    for i, o in enumerate(ops):
+        e = o["eng"]
+        if e == "x":
+            continue
+        for j in o["waits"]:
+            gj = ops[j]["grp"]
+            if gj is not None:
+                Q[e].wait_ge(T.sem[gj], gsum[gj])
+            else:
+                Q[e].wait_ge(T.sem["c" + ops[j]["eng"]], val[j])
+        ins = o["fn"]()
+        if o["grp"] is not None:
+            if o["inc"]:
+                ins.then_inc(T.sem[o["grp"]], 16)
+        elif i in need:
+            ins.then_inc(T.sem["c" + e], 1)
+    for e in "vstg":
+        if total[e]:
+            g.wait_ge(T.sem["c" + e], total[e])
+    for k in gsum:
+        g.wait_ge(T.sem[k], gsum[k])

@@ -1,64 +1,74 @@
 from concourse.mybir import AluOpType, AxisListType, ActivationFunctionType
 
-BF, F32, I32, U16 = "bfloat16", "float32", "int32", "uint16"
-BOOK = 6144
-OPT = {"ES": 0, "XS": 96, "E0": 1, "E1": 1}
+BF, F32, I32, U16, F16 = "bfloat16", "float32", "int32", "uint16", "float16"
+PB = 2048
+T2, XO = 2064, 4128
+DUMMY = 6048
+EO = 4112
+OPT = {"shy": 3000.0, "slack": 100.0, "XT": "f", "CNT": "s", "TK1": "s", "FO": "ff", "TB": "ff", "XL": "f", "CO": "ffff", "CB": "ff", "XB": "ff", "EO": "ffff", "XC": "f", "ZS": "f", "LT": "s", "YS": "f", "NQ": 4, "NE": 4, "look": 10.0, "lead": 6500.0}
 
 
 def _s(n, d):
     return ("sbuf", [128] + (list(n) if isinstance(n, (list, tuple)) else [n]), d)
 
 
-SCRATCH = {
-    "TN": _s(4112, BF), "W": _s(8192, BF), "SCW": _s(6432, BF), "XT": _s(8192, BF), "PR": _s(4096, BF), "CO": _s(4096, BF),
-    "EQ": _s(4096, BF), "EO": _s(4096, BF), "FO": _s(2048, BF), "XB": _s(2064, BF), "TB": _s(4128, BF), "N99": _s(2064, BF),
-    "OFF0": _s(512, U16), "OFF1": _s(512, U16), "OFF2": _s(512, U16), "OUT0": _s(512, U16), "OUT1": _s(512, U16),
-    "LND1": _s(1024, BF), "LND2": _s(1024, BF), "STG0": ("dram", [128, 1024], BF), "STG1": ("dram", [128, 1024], BF),
-    "PI": _s(512, I32), "JI": _s(256, F32), "Y0": _s(512, F32), "DG": _s(1024, BF), "BKI": _s(256, I32), "RW": _s([4, 256], BF),
-    "BI": _s([2, 128], I32), "BX": _s([2, 128], F32), "BD": _s([4, 128], BF), "SM": _s(144, I32), "SMF": _s(16, F32), "BLF": _s(256, F32),
-    "PMI": _s(2, I32), "COL": _s(8, F32), "J16": _s(256, F32),
-    "ONE": _s(256, F32), "ONEB": _s(128, BF), "ID": _s(128, BF), "IDF": _s(128, F32), "ID16": _s(128, BF), "ID129": _s(128, BF),
-    "M15": _s(128, F32), "MK8": _s(128, F32), "THX": _s(128, F32), "THT": _s(128, F32),
-    "EQF": _s(64, BF), "SEL": _s([4, 24], BF), "GS": _s([2, 32], BF), "UZ": _s(144, BF), "UU": _s([3, 160], BF), "UTRI": _s([16, 128], BF),
-    "S128": _s([8, 128], BF), "V1": _s(240, BF), "BS": _s([8, 128], BF), "ZL": _s([8, 128], BF), "ZA": _s(136, F32), "RT": _s(256, BF),
-    "DGM": _s(256, F32), "DM": _s(256, F32), "CONT16": _s(256, F32), "BARC": _s(128, F32), "C16R": _s(128, BF), "NTC": _s(8, F32),
-    "NEQ": _s([2, 144], BF), "END": _s([2, 144], BF), "CNT": _s([2, 144], BF), "GEQ": _s([2, 128], BF), "K16": _s([2, 128], BF),
-    "AC": _s([2, 128], BF), "C16": _s([2, 128], BF), "RR": _s([2, 128], BF), "ZT": _s([2, 128], BF), "IDX": _s(256, U16),
-    "PC": _s([2, 256], BF), "MN": _s(128, BF), "MT": _s(128, BF), "ST": _s(128, F32), "FI": _s(128, BF), "YC": _s(256, BF),
-    "FB": _s([2, 8], F32), "TI": _s([4, 8], I32), "TF": _s([8, 8], F32), "X1": _s(128, BF), "X2": _s(128, BF), "X3": _s(128, BF),
-    "YS": _s(256, BF), "Y3": _s(128, BF), "MG": _s([8, 128], BF), "LRS": _s(256, F32), "LV": _s(256, F32), "LS": _s(256, F32),
-    "EL": _s(16, U16), "FL": _s(128, U16), "LOC": _s(272, F32), "C16F": _s(128, F32), "SRC": _s(256, F32), "SRU": _s(256, U16),
-    "ETS": _s([2, 512], BF), "YO": _s([2, 256], F32), "ZO": _s(256, F32), "RS": _s([8, 16, 16], BF),
-    "BL": _s(128, U16), "NEWB": _s(128, BF), "CN": _s(128, BF), "CM": _s([16, 128], BF), "PL": _s(128, U16), "NL": _s(128, BF),
-    "NTF": _s(8, F32), "NTL": _s(8, U16), "XL": _s(128, BF), "XK": _s(1024, BF), "IDN": _s(128, BF),
-    "B0": ("psum", [128, 512], F32), "B1": ("psum", [128, 512], F32), "B2": ("psum", [128, 512], F32), "B3": ("psum", [128, 512], F32),
-    "B4": ("psum", [128, 512], F32), "B5": ("psum", [128, 512], F32), "B6": ("psum", [128, 16, 2, 16], F32), "B7": ("psum", [128, 16, 2, 16], F32),
+SHARED = {
+    "WR": _s([13, 128], BF), "WC": _s(16, F32), "BLK": _s(128, F32), "CO": _s(2048, BF), "CB": _s(1024, BF), "XB": _s(1040, BF), "SG": _s([16, 64], BF), "OH": _s(1024, BF),
+    "BKI": _s(256, I32), "RW": _s([3, 256], BF), "LP1": _s(256, BF), "LP2": _s(256, BF),
+    "BI": _s(128, I32), "BX": _s(128, F32), "BD": _s([2, 128], BF), "BT": _s(128, I32), "BTF": _s(144, F32),
+    "SM": _s(144, I32), "SMF": _s(144, F32), "PMI": _s(2, I32), "COL": _s(8, F32), "JI": _s(128, F32), "SI": _s(128, F32),
+    "NEB": _s([2, 128], BF), "CN": _s(128, BF), "NTC": _s(8, F32), "NTA": _s(128, F32), "E16": _s(128, BF), "DG": _s(16, F32),
+    "ONE": _s(128, F32), "ONEB": _s(256, BF), "NEG": _s(128, BF), "IDF": _s(128, F32), "IDS": _s([7, 128], BF),
+    "TRI": _s(128, BF), "SEL": _s([2, 8], BF), "SELT": _s([5, 8], BF), "IOC": _s(128, BF),
+    "CONT": _s(128, F32), "DM": _s(128, F32), "BARX": _s([2, 128], BF), "IDH": _s(128, F16), "V1": _s(176, BF), "ROWS": _s([6, 128], BF), "UP": _s(128, F32), "KR": _s(1024, BF),
+    "SY": _s([7, 64], BF), "SELI": _s([4, 48], BF), "USEL": _s(160, BF), "UZ": _s(144, BF), "MK8": _s(128, F32), "RS": _s([8, 4, 16], BF),
 }
-GROUPS = ["small", "bl", "pp", "bk", "bb", "tn", "wr", "wb", "rc", "stg0", "stg1", "rows1", "rows2", "fo0", "fo1", "yo", "zo",
-          "arr10", "arr11", "arr20", "arr21", "arw1", "arw2", "sent", "t0", "t1", "t2", "xb0", "xb1", "dum", "dum2", "zs0", "zs1"]
-SEMAPHORES = ["cg", "cv", "cs", "ct"] + GROUPS
-SIZE = {BF: 2, F32: 4, I32: 4, U16: 2}
+EACH = {
+    "TN": _s(4112, BF), "W": _s(8192, BF), "XW": _s(XO + 4112, BF), "U": _s(6208, BF), "EQ": _s(2048, BF),
+    "FO": _s(1024, BF), "TBN": _s(1024, BF), "TK": _s(1024, BF), "MG": _s([4, 128], BF), "ZP": _s([8, 112], BF),
+    "OFF": _s([3, 256], U16), "ATT": _s([3, 384], BF), "OUT": _s([2, 256], U16), "ATO": _s([2, 384], BF), "STG": _s([2, 640], BF), "LND": _s([2, 640], BF),
+    "PI": _s(256, I32), "Y0": _s(256, F32), "DU": _s(256, BF), "JM": _s(128, F32), "MK": _s(128, F32), "THX": _s(128, F32),
+    "TF": _s([6, 144], BF), "IDX": _s(128, U16), "FS": _s([4, 128], F32), "TI": _s([4, 8], F32), "PAY": _s([8, 8], BF), "X": _s([4, 16], BF),
+    "YS": _s(128, BF), "EL": _s(8, U16), "LS": _s([4, 64], U16), "LT": _s(192, F32), "SRU": _s(128, U16), "TS": _s(272, F16), "THB": _s([2, 128], BF), "NTL": _s(8, U16), "XL": _s(128, BF),
+}
+ONCE = ("XL", "MG", "DU", "EL", "THX", "LT", "SRU", "TBN")
+SCRATCH = dict(SHARED)
+for _b in (0, 1):
+    SCRATCH.update({k + str(_b): v for k, v in EACH.items() if _b == 0 or k not in ONCE})
+    SCRATCH.update({"P%s%d" % (k, _b): ("psum", [128, 512], F32) for k in "ad"})
+    SCRATCH["Pb%d" % _b] = ("psum", [128, 32, 16], F32)
+    SCRATCH["Pc%d" % _b] = ("psum", [128, 4, 8, 16], F32)
+SEMAPHORES = ["cg", "cv", "cs", "ct", "sent"] + ["d%d" % i for i in range(140)]
+SIZE = {F16: 2, BF: 2, F32: 4, I32: 4, U16: 2}
 AL = AluOpType
 AF = ActivationFunctionType
+PLAN = {}
+COST = {"act": 100.0, "cyc": 0.9, "gr": 1.5, "sr": 3.5, "pe": 0.5, "sem": 120.0, "dma": 1900.0, "rem": 3000.0, "bw": 250.0, "rbw": 60.0, "iy": 100.0, "ig": 900.0}
 
 
 def rank_program(g, core, T, topo):
     rank = T.rank_of(core)
     if rank is None:
         return
-    ES, XS = OPT["ES"], OPT["XS"]
     n_ranks = len(T.cores)
-    nxt = T.cores[(rank + 3) % n_ranks]
-    rid, pid = topo.addr(nxt, core)
-    mask = topo.mask(core, nxt)
-    n_eng = len(topo.engines(core, nxt))
-    n_in = len(topo.engines(T.cores[(rank - 3) % n_ranks], core))
     Q = {"g": g, "v": g.vector, "s": g.scalar, "t": g.tensor, "y": g.sync}
-    ops, acc, grp = [], {}, {}
+    ops, acc, grp, sems = [], {}, {}, {}
+    planned = "order" in PLAN
+    now = [0]
+    cyc = COST["cyc"]
+
+    def sem_of(group):
+        if group not in sems:
+            sems[group] = "d%d" % len(sems)
+        return T.sem[sems[group]]
 
     def A(name, *ix):
+        if name[:-1] in ONCE:
+            name = name[:-1] + "0"
         where, shape, d = SCRATCH[name]
         ix = list(ix) + [slice(None)] * (len(shape) - len(ix))
+        if planned:
+            return (T[name][tuple(ix)], [])
         pm = 0
         for i in range(*ix[0].indices(128)):
             pm |= 1 << i
@@ -76,22 +86,50 @@ def rank_program(g, core, T, topo):
         z = SIZE[d]
         return (T[name][tuple(ix)], [(name, pm, lo * z, (hi + 1) * z, em)])
 
-    def C(name, a, b=None, st=None):
-        return A(name, slice(None), slice(a, b, st))
+    al = slice(None)
 
     def P(name, p0, p1, a=None, b=None, st=None):
+        if name[:2] == "Pb":
+            return A(name, slice(p0, p1), slice(a // 16, b // 16))
         return A(name, slice(p0, p1), slice(a, b, st))
 
-    def col(j):
-        return C("COL", j, j + 1)
+    def C(name, a, b=None, st=None):
+        return P(name, 0, 128, a, b, st)
+
+    def col(j, p1=128):
+        return P("COL", 0, p1, j, j + 1)
 
     def IND(win, off):
-        return (win[0].indirect(off[0]), win[1], off[1])
+        return (win[0].indirect(off[0]), win[1], off[1], 16 * width(off))
 
     def X(ap):
         return (ap, [])
 
-    def rec(eng, fn, outs, ins, group=None, inc=16):
+    def width(x):
+        if len(x) > 3:
+            return x[3]
+        n = 1
+        for k in x[0].shape[1:]:
+            n *= k
+        return n
+
+    def size(x):
+        return SIZE[SCRATCH[x[1][0][0]][2]] if x[1] else 4
+
+    def narrow(*xs):
+        return all(x[1] and size(x) == 2 for x in xs)
+
+    def in_psum(x):
+        return bool(x[1]) and SCRATCH[x[1][0][0]][0] == "psum"
+
+    def rec(eng, fn, outs, ins, dur, group=None, inc=16, lat=0.0):
+        me = len(ops)
+        op = {"eng": eng, "fn": fn, "deps": set(), "soft": set(), "grp": group, "inc": inc, "dur": dur, "lat": lat, "batch": now[0]}
+        ops.append(op)
+        if group is not None:
+            grp.setdefault(group, []).append(me)
+        if planned:
+            return me
         rd, wr = [], []
         for o in outs:
             wr += o[1]
@@ -102,649 +140,669 @@ def rank_program(g, core, T, topo):
                 rd += i[1]
                 if len(i) > 2:
                     rd += i[2]
-        me = len(ops)
-        deps = set()
         for lst, w in ((rd, False), (wr, True)):
             for (nm, pm, lo, hi, em) in lst:
                 ps = SCRATCH[nm][0] == "psum"
                 for (o, pm2, lo2, hi2, w2, em2) in acc.setdefault(nm, []):
                     e2, g2 = ops[o]["eng"], ops[o]["grp"]
-                    same = e2 == eng and g2 is None and group is None
-                    if ps and not same:
-                        deps.add(o)
+                    same = e2 == eng != "f" and g2 is None and group is None
+                    if ps:
+                        if not same:
+                            op["deps"].add(o)
+                        elif eng == "t":
+                            op["soft"].add(o)
                         continue
                     if not (w or w2) or not (pm & pm2):
-                        continue
-                    if same and eng == "t":
                         continue
                     if (g2 is None) != (group is None):
                         hit = lo // 16 <= (hi2 - 1) // 16 and lo2 // 16 <= (hi - 1) // 16
                     else:
                         hit = (em & em2) != 0
                     if hit and not (group is not None and g2 == group):
-                        deps.add(o)
+                        op["deps"].add(o)
         for lst, w in ((rd, False), (wr, True)):
             for (nm, pm, lo, hi, em) in lst:
+                if SCRATCH[nm][0] == "psum":
+                    acc[nm] = [a for a in acc[nm] if ops[a[0]]["eng"] != "t" or eng != "t"]
                 acc[nm].append((me, pm, lo, hi, w, em))
-        ops.append({"eng": eng, "fn": fn, "deps": deps, "grp": group, "inc": inc})
-        if group is not None:
-            grp.setdefault(group, []).append(me)
+        return me
 
     def ap(x):
         return x[0] if isinstance(x, tuple) else x
 
+    def vec(n, fast=False):
+        return max(64, n * (0.5 if fast else 1)) * cyc
+
     def ts(out, in0, s1, op0, s2=None, op1=None):
+        dur = vec(width(in0), narrow(out, in0))
         if op1 is None:
-            rec("v", lambda: g.vector.tensor_scalar(out[0], in0[0], ap(s1), None, op0), [out], [in0, s1])
+            rec("v", lambda: g.vector.tensor_scalar(out[0], in0[0], ap(s1), None, op0), [out], [in0, s1], dur)
         else:
-            rec("v", lambda: g.vector.tensor_scalar(out[0], in0[0], ap(s1), ap(s2), op0, op1), [out], [in0, s1, s2])
+            rec("v", lambda: g.vector.tensor_scalar(out[0], in0[0], ap(s1), ap(s2), op0, op1), [out], [in0, s1, s2], dur)
 
     def tt(out, a, b, op):
-        rec("v", lambda: g.vector.tensor_tensor(out[0], a[0], b[0], op), [out], [a, b])
+        dur = 50 + width(a) * COST["gr"] * cyc if len(a) > 2 else vec(width(a) * (1 if in_psum(a) or in_psum(b) else 2))
+        rec("v", lambda: g.vector.tensor_tensor(out[0], a[0], b[0], op), [out], [a, b], dur)
 
     def cp(out, a):
-        rec("v", lambda: g.vector.tensor_copy(out[0], a[0]), [out], [a])
+        dur = 50 + width(a) * COST["gr" if len(a) > 2 else "sr"] * cyc if len(a) > 2 or len(out) > 2 else vec(width(a), narrow(out, a))
+        rec("v", lambda: g.vector.tensor_copy(out[0], a[0]), [out], [a], dur)
 
     def ms(out, val):
-        rec("v", lambda: g.vector.memset(out[0], val), [out], [])
+        rec("v", lambda: g.vector.memset(out[0], val), [out], [], vec(width(out), narrow(out)))
 
-    def scan(out, d0, d1, init, op0, op1):
-        rec("v", lambda: g.vector.tensor_tensor_scan(out[0], d0[0], d1[0], ap(init), op0, op1), [out], [d0, d1, init])
+    def scan(out, d0, d1, op0, op1):
+        rec("v", lambda: g.vector.tensor_tensor_scan(out[0], d0[0], d1[0], 0.0, op0, op1), [out], [d0, d1], vec(width(out), narrow(out, d0, d1)))
 
-    def red(out, a):
-        rec("v", lambda: g.vector.tensor_reduce(out[0], a[0], AxisListType.X, AL.min, apply_absolute_value=True), [out], [a])
-
-    def act(out, a, scale=None, bias=0.0):
-        if scale is None:
-            rec("s", lambda: g.scalar.activation(out[0], a[0], AF.Copy), [out], [a])
+    def act(out, a, scale=None, bias=0.0, func=AF.Identity, either=True):
+        dur = 65 + width(a) * COST["gr"] * cyc if len(a) > 2 else COST["act"] + vec(width(a))
+        if func == AF.Sign or not either:
+            eng = "s"
         else:
-            rec("s", lambda: g.scalar.activation(out[0], a[0], AF.Identity, bias=ap(bias), scale=scale), [out], [a, bias])
+            eng, dur = "f", {"s": dur, "v": dur - 15 if len(a) > 2 else vec(width(a), narrow(out, a))}
+        if scale is None:
+            fn = {"s": lambda: g.scalar.activation(out[0], a[0], AF.Copy), "v": lambda: g.vector.tensor_copy(out[0], a[0])}
+        else:
+            fn = {"s": lambda: g.scalar.activation(out[0], a[0], func, bias=ap(bias), scale=ap(scale)),
+                  "v": lambda: g.vector.tensor_scalar(out[0], a[0], ap(scale), ap(bias), AL.mult, AL.add if func == AF.Identity else AL.max)}
+        rec(eng, fn if eng == "f" else fn["s"], [out], [a, bias, scale], dur)
+
+    def move(eng, out, a):
+        if eng == "v":
+            cp(out, a)
+        else:
+            act(out, a, either=eng == "f")
 
     def gat(eng, out, win, off):
-        (cp if eng == "v" else act)(out, IND(win, off))
+        move(eng, out, IND(win, off))
+
+    def gats(engs, out, win, off, n, c0=0):
+        w = n // len(engs)
+        for q, eng in enumerate(engs):
+            gat(eng, C(out, c0 + 16 * w * q, c0 + 16 * w * (q + 1)), win, off(w * q, w * (q + 1)))
 
     def mm(out, l, r, start=True, stop=True):
-        rec("t", lambda: g.tensor.matmul(out[0], l[0], r[0], start, stop), [out], [l, r])
+        dur = max(min(64, width(l)), width(r)) * COST["pe"] * (4 if size(l) == 4 else 1)
+        rec("t", lambda: g.tensor.matmul(out[0], l[0], r[0], start, stop), [out], [l, r], dur)
 
-    def width(x):
-        n = 1
-        for k in x[0].shape[1:]:
-            n *= k
-        return n
+    def mms(items):
+        for i, (out, l, r) in enumerate(items):
+            mm(out, l, r, i == 0, i == len(items) - 1)
 
     def iota(out, pat, base, cm, integer=False):
+        dur = 130 + 2 * width(out) * cyc
         if integer:
-            rec("g", lambda: g.iota(out[0], pat, base, cm), [out], [])
+            rec("g", lambda: g.iota(out[0], pat, base, cm), [out], [], dur)
         else:
-            rec("g", lambda: g.iota(out[0], pat, base, cm, allow_small_or_imprecise_dtypes=True), [out], [])
+            rec("g", lambda: g.iota(out[0], pat, base, cm, allow_small_or_imprecise_dtypes=True), [out], [], dur)
 
     def fill(out, val):
         iota(out, [[0, width(out)]], val, 0)
 
+    def fills(name, a, e, val):
+        for x in range(a, e, 512):
+            fill(C(name, x, min(e, x + 512)), val)
+
     def asel(out, a, pat, op, val, base, cm):
-        rec("g", lambda: g.affine_select(out[0], a[0], pat, op, val, base, cm), [out], [a])
+        rec("g", lambda: g.affine_select(out[0], a[0], pat, op, val, base, cm), [out], [a], 170 + 2 * width(out) * cyc)
 
-    def dma(eng, group, out, a, slow=False):
-        if slow:
-            rec(eng, lambda: g.dma_start(out[0], a[0], allow_slow_non_contiguous=True), [out], [a], group)
-        else:
-            rec(eng, lambda: Q[eng].dma_start(out[0], a[0]), [out], [a], group)
+    def dma(group, out, a, eng="y"):
+        sem_of(group)
+        move_ns = out[0].shape[0] * width(out) * size(out) / COST["bw"]
+        rec(eng, lambda: Q[eng].dma_start(out[0], a[0]), [out], [a], max(COST["iy"], move_ns) if eng == "y" else COST["iy"], group, 16, COST["dma"] + (0.0 if eng == "y" else move_ns))
 
-    def send(out, a, sem):
-        rec("g", lambda: g.remote_dma(out[0], a[0], T.sem[sem], T.sem["sent"], pid, rid, mask), [], [a], "sent", 0)
+    sends = {}
 
-    def arrive(out, sem):
-        rec("x", None, [out], [], sem, n_in)
+    def arrive(out, group, step):
+        sem_of(group)
+        sends[group] = [rec("x", None, [out], [], 0.0, group, len(topo.engines(T.cores[(rank - step) % n_ranks], core)))]
+
+    def send(out, a, group, step, after=None):
+        to = T.cores[(rank + step) % n_ranks]
+        rid, pid = topo.addr(to, core)
+        mask = topo.mask(core, to)
+        sends[group].append(rec("g", lambda: g.remote_dma(out[0], a[0], sem_of(group), T.sem["sent"], pid, rid, mask), [], [a], COST["ig"], "sent",
+                                len(topo.engines(core, to)), COST["rem"] + 128 * width(a) * 2 / COST["rbw"]))
+        if after is not None:
+            ops[-1]["soft"].add(sends[after][1])
 
     mult, add, sub, amax, amin = AL.mult, AL.add, AL.subtract, AL.max, AL.min
     ge, gt, le, lt, eq, ne = AL.is_ge, AL.is_gt, AL.is_le, AL.is_lt, AL.is_equal, AL.not_equal
-    al = slice(None)
-    PM, PM16, PM17, INI, C16C, C16N = range(6)
-    BLK, TRI, SPOS, SF, SL, SLE, SE, UB = range(8)
-    UBT, UDF, USEL = range(3)
+    PM, PM256, SRC0, KIND, C16, PMH = range(6)
+    BAR, RR, TKN, EE, HB, DL, CC, UNO, LM, CT, LN, CU = range(12)
+    SPOS, SZC, SFL, SPB, SLN = 5, 1, 4, 3, 0
 
-    def B(k, a, b, p1=128, st=None):
-        if k < 6:
-            return P("B%d" % k, 0, p1, a, b, st)
-        return A("B%d" % k, slice(0, p1), slice(a // 32, b // 32))
+    def every(name, hh, st, a, e):
+        return A(name, slice(64 * hh, 64 * hh + 64, st), slice(a, e))
 
-    def S128(k):
-        return A("S128", al, k)
+    WEIGHTS = [1.0, 8192.0, 2.0 ** -14, 129.0 / 1024, 1.0 / 16, 1.0 / 32, -16.0]
+    ID1, ID8K, IDM14, ID129, ID16, ID32, IDN16 = [A("IDS", al, k) for k in range(7)]
 
-    def slide(k, s):
-        return A("UU", al, k, slice(16 - s, 144 - s))
+    def rows4(name, hh, f, a, b):
+        return A(name, slice(64 * hh + f, 64 * hh + 64, 16), slice(a, b))
 
-    def row(view, f, val):
-        asel(view, view, [[-16, 8]], ne, val, -f, 1)
+    arrive(A("LP1"), "lp1", -3)
+    arrive(A("LP2"), "lp2", -6)
+    for b in (0, 1):
+        for v in (1, 2):
+            arrive(A("OFF%d" % b, al, v), "off%d%d" % (v, b), 3)
+            arrive(A("ATT%d" % b, al, v), "att%d%d" % (v, b), 3)
+            arrive(A("LND%d" % b, al, v - 1, slice(0, 128 * (6 - v))), "lnd%d%d" % (v, b), 3)
+    dma("bk", A("BKI"), X(T.bk[:]))
+    dma("small", P("SM", 0, 8, 0, 1), X(T.pn[:]))
+    dma("small", P("SM", 0, 8, 1, 2), X(T.th[:]))
+    dma("small", P("SM", 0, 8, 16, 144), X(T.bl[:]))
+    for b in (0, 1):
+        for hh in (0, 1):
+            for k, src in enumerate((T.pu, T.pt)):
+                dma("pp%d" % b, P("PI%d" % b, 64 * hh, 64 * hh + 64, 128 * k, 128 * k + 128), X(src[64 * b:64 * b + 64, 128 * hh:128 * hh + 128]))
+            dma("tn%d" % b, P("TN%d" % b, 64 * hh, 64 * hh + 64, 16, 4112), X(T.tones[64 * b:64 * b + 64]))
+    for gi in range(8):
+        dma("bt", C("BT", 16 * gi, 16 * gi + 16), X(T.bt[gi]), "s")
+    dma("bb", A("BI"), X(T.bu[:]))
 
-    def rows(out, src, lo, hi, n):
-        asel(out, src, [[-16, 8], [0, n]], ge, 0.0, -lo, 1)
-        asel(out, out, [[16, 8], [0, n]], ge, 0.0, hi, -1)
+    ms(A("ONE"), 1.0), ms(A("ONEB"), 1.0), ms(A("NEG"), -1.0)
 
-    def xk(nm, f):
-        return C(nm, f, 128, 16)
+    def put(out, val):
+        act(out, A("ONE", slice(0, out[0].shape[0]), slice(0, width(out))), 0.0, val)
 
-    def book_compact(k, out, src, c0):
-        for s in range(16):
-            mm(out, slide(UBT if s == 15 else k, s), C(src, c0 + s, c0 + 2048, 16), s == 0, s == 15)
-
-    for v in (1, 2):
-        for h in (0, 1):
-            arrive(C("OFF%d" % v, 256 * h, 256 * h + 256), "arr%d%d" % (v, h))
-        arrive(A("LND%d" % v), "arw%d" % v)
-    dma("y", "small", P("SM", 0, 8, 0, 1), X(T.pn[:]))
-    dma("y", "small", P("SM", 0, 8, 1, 2), X(T.th[:]))
-    dma("y", "pp", C("PI", 256, 512), X(T.pt[:]))
-    dma("y", "pp", C("PI", 0, 256), X(T.pu[:]))
-    dma("y", "bk", A("BKI"), X(T.bk[:]))
-    dma("s", "bb", A("BI", al, 0), X(T.bu[:]))
-    dma("s", "bb", A("BI", al, 1), X(T.bt[:]))
-    dma("s", "tn", C("TN", 16, 4112), X(T.tones[:]))
-    dma("y", "bl", P("SM", 0, 8, 16, 144), X(T.bl[:]))
-    ms(A("ONE"), 1.0)
-    ms(C("W", BOOK - 16, 8192), 0.0)
-    ms(C("W", 0, 2064), 0.0)
-    ms(C("TN", 0, 16), 0.0)
-    act(A("N99"), C("W", BOOK - 16, 8192), 0.0, 99.0)
-    ts(A("BX"), A("BI"), 1.0, add)
-    cp(A("BD", al, slice(0, 4, 2)), A("BX"))
-    tt(A("BD", al, slice(1, 4, 2)), A("BX"), A("BD", al, slice(0, 4, 2)), sub)
-    for f in range(4):
-        dma("y", "wb", A("W", slice(4 + f, 128, 16), slice(BOOK, 8192)), A("BD", al, f))
-    ms(C("W", 2064, 4112), 0.0)
-    iota(A("RW", al, 1), [[0, 256]], 256, 256)
-    iota(A("RW", al, 2), [[1, 256]], 0, 0)
-    fill(A("RW", al, 3), 1)
-    iota(P("SMF", 0, 32, 2, 3), [[0, 1]], 0, 16)
-    asel(P("MK8", 0, 32), P("ONE", 0, 32, 0, 128), [[1, 128]], ge, 0.0, 0, -16)
-    asel(P("MK8", 0, 32), P("MK8", 0, 32), [[-1, 128]], ge, 0.0, 15, 16)
-    iota(A("JI"), [[16, 256]], 0, 1)
     iota(C("PMI", 0, 1), [[0, 1]], 0, 1, True)
-    ts(A("RW", al, 0), A("BKI"), 1.0, add)
-    for f in range(4):
-        dma("y", "wr", A("W", slice(f, 128, 16), slice(16, 4112)), A("RW", al, f))
-    cp(P("SMF", 0, 8, 0, 2), P("SM", 0, 8, 0, 2))
-    mm(B(0, 0, 1), P("MK8", 0, 8), P("SMF", 0, 8, 0, 1), True, False)
-    mm(B(0, 0, 1), P("MK8", 0, 8), P("SMF", 0, 8, 2, 3), False, True)
-    ts(C("OFF0", 0, 256), C("PI", 0, 256), 16.0, add)
-    ts(A("JI"), A("JI"), B(0, 0, 1), ge, -8192.0, mult)
-    tt(C("Y0", 256, 512), C("PI", 256, 512), A("JI"), add)
-    ts(C("OFF0", 256, 512), C("Y0", 256, 512), -1.0, amax, 16.0, add)
-    dma("y", "t0", C("TB", 2064, 4128), A("N99"))
-    fill(A("UU"), 0)
-    for k in (UBT, UDF):
-        for f in (6, 7):
-            row(A("UU", al, k, slice(16, 144, 16)), f, 1.0)
-    for f in (6, 7):
-        row(A("UU", al, UDF, slice(17, 145, 16)), f, -1.0)
-    book_compact(UBT, B(6, 0, 128), "W", BOOK)
-    book_compact(UDF, B(7, 0, 128), "W", BOOK)
-    asel(A("IDF"), C("ONE", 0, 128), [[-1, 128]], eq, 0.0, 0, 1)
-    asel(S128(TRI), C("ONE", 0, 128), [[-16, 8], [0, 16]], ge, 0.0, 0, 1)
-    asel(S128(TRI), S128(TRI), [[16, 8], [1, 16]], ge, 0.0, 0, -1)
-    asel(S128(TRI), S128(TRI), [[16, 8], [0, 16]], ge, 0.0, 15, -1)
-    fill(A("SEL"), 0)
-    row(A("SEL", al, 0, slice(0, 8)), 0, 1.0)
-    for f in (1, 2):
-        row(A("SEL", al, 0, slice(8, 16)), f, -1.0)
-        row(A("SEL", al, 2, slice(8, 16)), f, 1.0)
-    row(A("SEL", al, 2, slice(16, 24)), 3, -8192.0)
-    fill(A("SEL", al, 1, slice(8, 16)), -1)
-    rows(A("SEL", al, 3, slice(16, 24)), C("ONE", 0, 8), 0, 15, 1)
-    rows(A("UU", al, USEL, slice(16, 144, 16)), C("ONE", 0, 8), 0, 15, 1)
-    rows(S128(BLK), C("ONE", 0, 128), 0, 15, 16)
-    iota(A("J16"), [[0, 16], [1, 16]], 0, 0)
-    iota(A("C16R"), [[16, 128]], 0, 0)
-    iota(A("NTC"), [[256, 8]], 15, 0)
-    fill(C("XB", 2048, 2064), 0)
-    fill(C("TB", 0, 16), 99)
-    fill(A("ONEB"), 1)
-    for nm, val in (("NEQ", 16), ("END", 16), ("CNT", 0)):
-        fill(A(nm, al, al, 0), val)
-    asel(A("CONT16"), A("ONE"), [[0, 16], [1, 16]], gt, 0.0, 0, 0)
-    LM1, ONEL, TK, NTK, TMP = [A("TF", al, k) for k in range(5)]
-    ts(P("THX", 0, 8), P("MK8", 0, 8), P("SMF", 0, 8, 1, 2), mult)
-    mm(B(1, 0, 128), P("ONE", 0, 8, 0, 128), P("THX", 0, 8))
-    ts(P("BLF", 0, 8, 0, 128), P("SM", 0, 8, 16, 144), -1.0, add)
-    ts(P("BLF", 0, 8, 128, 256), P("SM", 0, 8, 16, 144), 1.0, eq, 16384.0, mult)
     ts(C("PMI", 1, 2), C("PMI", 0, 1), 15, AL.bitwise_and)
-    tt(P("BLF", 0, 8, 128, 256), P("BLF", 0, 8, 128, 256), P("BLF", 0, 8, 0, 128), add)
     cp(col(PM), C("PMI", 1, 2))
-    mm(B(3, 128, 384), P("MK8", 0, 8), P("BLF", 0, 8))
-    mm(B(2, 0, 8), P("BLF", 0, 8, 0, 128), P("IDF", 0, 8, 0, 8))
-
-    def small_constants():
-        act(A("THT"), B(1, 0, 128), 1.0, -8192.0)
-        act(C("THT", 15, 128, 16), C("ONE", 0, 8), -1000000.0)
-        act(A("LRS"), B(3, 128, 384))
-        act(LM1, B(2, 0, 8))
-        act(A("ID16"), A("IDF"), 1.0 / 16)
-        act(A("ID129"), A("IDF"), 129.0)
-        act(A("IDN"), A("IDF"), -1.0)
-        act(col(PM16), col(PM), 16.0)
-        act(col(PM17), col(PM), 17.0)
-        act(col(INI), col(PM), 1.0, -16.0)
-
-    asel(A("EQF"), C("ONE", 0, 64), [[-1, 8], [-16, 8]], eq, 0.0, 0, 1)
-    iota(A("DM"), [[1, 256]], BOOK, 0)
-    fill(A("BARC"), 2)
-    fill(C("BARC", 0, 128, 16), 0)
-    fill(A("GS"), 0)
-    rows(A("GS", al, 0, slice(0, 8)), C("ONE", 0, 8), 0, 15, 1)
-    rows(A("GS", al, 1, slice(8, 16)), C("ONE", 0, 8), 0, 15, 1)
-    iota(P("RT", 0, 32), [[0, 2], [1, 128]], 0, 0)
-    asel(P("RT", 0, 32), P("RT", 0, 32), [[0, 256]], ne, -65536.0, -17, 1)
-    Z0, Z1 = P("ZA", 0, 32, 0, 128), P("ZA", 0, 32, 128, 136)
-    iota(Z0, [[1, 128]], 1, 0)
-    asel(Z0, Z0, [[0, 128]], eq, 0.0, -17, 1)
-    asel(Z0, Z0, [[0, 128]], ne, 256.0, -16, 1)
-    fill(Z1, 0)
-    asel(Z1, Z1, [[-1, 8]], ne, 65536.0, 0, 1)
-    asel(Z1, Z1, [[-1, 8]], ne, 1.0, -8, 1)
-    for nm in ("X1", "X2", "X3"):
-        fill(A(nm), 0)
-    iota(xk("X1", 0), [[0, 8]], 0, 16)
-    fill(xk("X1", 1), BOOK)
-    iota(xk("X2", 5), [[0, 8]], 0, -16)
-    fill(xk("X2", 8), -BOOK)
-    iota(col(C16C), [[0, 1]], 0, 16)
-    iota(col(C16N), [[0, 1]], 0, -16)
-    fill(S128(SPOS), -1)
-    rows(S128(SPOS), S128(SPOS), 2, 4, 16)
-    for k, lo, hi in ((SF, 0, 3), (SL, 4, 4), (SLE, 4, 5), (SE, 5, 8), (UB, 0, 8)):
-        rows(S128(k), C("ONE", 0, 128), lo, hi, 16)
-    fill(A("V1"), 0)
-    fill(C("V1", 112, 128), 1)
-    for s in range(16):
-        asel(A("UTRI", al, s), S128(UB), [[16, 8], [9, 16]], ge, 0.0, 4 - 9 * s, -1)
-    rows(A("M15"), C("ONE", 0, 128), 15, 15, 16)
-    asel(A("M15"), A("M15"), [[-1, 128]], ne, -1.0, 0, 1)
-    row(C("M15", 15, 128, 16), 15, 0.0)
-    fill(A("C16F"), 16)
-    fill(C("LOC", 0, 1), 0)
-    fill(A("UZ"), 0)
-    for k in (0, 1):
-        for f in (4, 5):
-            row(C("UZ", 8 + 64 * k, 72 + 64 * k, 8), f + 2 * k, 1.0)
-
-    def clear_steps(group):
-        for f in range(9):
-            dma("y", group, A("SCW", slice(f, 128, 16), slice(16, 4112)), A("W", slice(9, 128, 16), slice(0, 4096)))
-
-    dma("y", "dum", C("SCW", 0, 4112), A("TN"))
-    dma("y", "dum", C("W", 4112, BOOK - 16), C("TN", 0, BOOK - 4128))
-    dma("y", "dum", C("XT", 4096, BOOK), C("TN", 0, 2048))
-    clear_steps("dum2")
-    for f in range(4):
-        dma("y", "dum2", A("W", slice(4 + f, 128, 16), slice(4112, BOOK - 16)), A("W", slice(9, 128, 16), slice(0, BOOK - 4128)))
-
-    def pickers():
-        for gi in range(8):
-            act(A("ZL", slice(0, 32), gi), Z0, 1.0, P("ZA", 0, 32, 128 + gi, 129 + gi))
-        for gi in range(8):
-            act(A("BS", al, gi), C("ONE", 0, 128), 0.0, C("EQF", 16 + gi, 17 + gi))
-
-    def single_items():
-        ts(ONEL, LM1, 0.0, eq)
-        ts(xk("X1", 5), ONEL, col(C16N), mult)
-        ts(xk("X1", 8), ONEL, -float(BOOK), mult)
-
-    def book_new():
-        ts(A("NEWB"), B(7, 0, 128), 0.0, ne)
-        mm(B(6, 0, 128), S128(TRI), A("NEWB"))
-
-    def book_places(k0, k1):
+    act(col(PM256), col(PM), 256.0)
+    act(col(SRC0), col(PM), 1.0, float(PB - 16))
+    iota(col(C16), [[0, 1]], 16, 16)
+    for hh in (0, 1):
+        act(P("COL", 64 * hh, 64 * hh + 64, KIND, KIND + 1), P("ONE", 64 * hh, 64 * hh + 64, 0, 1), 16.0 + hh)
+        act(P("COL", 64 * hh, 64 * hh + 64, PMH, PMH + 1), P("COL", 64 * hh, 64 * hh + 64, PM, PM + 1), 1.0, 2048.0 * hh)
+    iota(A("JI"), [[16, 128]], 0, 0)
+    asel(A("IDF"), A("ONE"), [[-1, 128]], eq, 0.0, 0, 1)
+    iota(A("BARX"), [[128, 2], [0, 128]], 1, 1)
+    cp(A("IDH"), A("IDF"))
+    for k, w in enumerate(WEIGHTS):
+        act(A("IDS", al, k), A("IDF"), w)
+    asel(A("UP"), A("ONE"), [[1, 128]], ge, 0.0, 0, -1)
+    asel(A("TRI"), A("NEG"), [[1, 128]], ge, 0.0, 0, -1)
+    asel(A("TRI"), A("TRI"), [[1, 128]], ne, 1.0, 0, -1)
+    asel(A("BLK"), A("ONE"), [[-16, 8], [0, 16]], ge, 0.0, 0, 1)
+    asel(A("BLK"), A("BLK"), [[16, 8], [0, 16]], ge, 0.0, 15, -1)
+    SELF = C("BLK", 0, 128, 16)
+    act(A("SEL", al, 0), SELF)
+    act(A("SEL", al, 1), SELF, 32768.0)
+    iota(A("IOC"), [[1, 128]], 1, 0)
+    iota(A("SI"), [[0, 8], [1, 16]], 0, 0)
+    asel(A("CONT"), A("ONE"), [[0, 8], [1, 16]], gt, 0.0, 0, 0)
+    for k, (scale, bias) in enumerate(((-512.0, -8192.0), (0.0, -188416.0), (15.0, 0.0), (1.0, 0.0))):
+        act(A("ROWS", slice(0, 1), k), P("SI", 0, 1), scale, bias)
+    act(A("ROWS", slice(0, 1), 4), P("JI", 0, 1))
+    asel(P("E16", 0, 32), P("ONEB", 0, 32, 0, 128), [[0, 8], [-1, 16]], eq, 0.0, 0, 1)
+    mm(C("Pb1", 0, 128), P("E16", 0, 16), P("E16", 0, 16))
+    iota(A("DM"), [[1, 128]], DUMMY, 0)
+    tt(A("DM"), C("Pb1", 0, 128), A("DM"), mult)
+    cp(A("DG"), C("Pb1", 0, 16))
+    ms(A("V1"), 0.0), put(C("V1", 48, 64), 32.0), put(C("V1", 112, 128), 32.0)
+    ms(A("USEL"), 0.0)
+    act(C("USEL", 16, 144, 16), SELF, 0.5)
+    asel(P("MK8", 0, 32), P("ONE", 0, 32), [[-1, 8], [0, 16]], eq, 0.0, 0, 1)
+    place = {BAR: 16.0, EE: -1.0 / 512, RR: -32.0}
+    step = {BAR: -16.0, EE: 1.0 / 512, RR: 32.0, CU: 1.0}
+    base = {BAR: 16.0, CC: 1.0, CT: -1.0, UNO: 24.0}
+    start = {**place, UNO: 8192.0, TKN: -8192.0}
+    slots = [{0: 1.0, 8: 1.0}, {4: 1.0, 12: 1.0}, {6: 1.0}, {2: 1.0},
+             {LN: 32.0}, {EE: 1.0 / 32, RR: 512.0, TKN: -256.0}, {**base, TKN: XO - 32.0 + 2048, HB: -4096.0}, {**base, TKN: XO - 32.0},
+             {**place, TKN: float(PB), CC: 1.0, CT: -1.0}, start, {**start, LM: 32.0},
+             {**{f: -w for f, w in step.items()}, DL: -32.0}, step]
+    iota(P("KR", 0, 32), [[8, 16], [0, 64]], -4, 0)
+    for k0, k1 in ((0, 4), (4, 13)):
+        ms(A("WR", slice(0, 1), slice(k0, k1)), 0.0)
+    for k, ws in enumerate(slots):
+        for f, w in ws.items():
+            if k == 0 or slots[k - 1].get(f) != w:
+                e = k + 1
+                while e < len(slots) and slots[e].get(f) == w:
+                    e += 1
+                ms(A("WR", slice(0, 1), slice(k, e), slice(f, 128, 16)), w)
+    for k0, k1 in ((0, 4), (4, 13)):
         for k in range(k0, k1):
-            ts(A("CM", al, k), A("CN"), float(k), le)
-            mm(B(7, 0, 128), slide(USEL, k), A("CM", al, k), k == 0, False)
-        if k1 == 16:
-            mm(B(7, 0, 128), A("ID"), A("C16R"), False, True)
+            mm(C("Pd0", k, k + 1), A("WR", slice(0, 1), k), P("ONEB", 0, 1, 0, 1))
+        act(C("WC", k0, k1), C("Pd0", k0, k1))
+    for j, k in enumerate((0, 1, 2, 1, 3)):
+        act(A("SELT", al, j), SELF, C("WC", k, k + 1))
+    ms(A("UZ"), 0.0)
+    for k in (0, 1):
+        for hh in (0, 1):
+            act(C("UZ", 8 + 64 * k + 8 * hh, 72 + 64 * k, 16), C("BLK", 64 * hh, 64 * hh + 64, 16), C("WC", k, k + 1))
+    for k in range(4, 11):
+        act(A("SY", slice(0, 64), k - 4), P("BLK", 0, 64, 0, 64), P("WC", 0, 64, k, k + 1))
+    ms(A("SELI"), 0.0)
+    for kind in (0, 1):
+        act(A("SELI", slice(64 * kind, 64 * kind + 64), al, slice(16, 32)), P("BLK", 64 * kind, 64 * kind + 64, 64 * kind, 64 * kind + 64), P("WC", 64 * kind, 64 * kind + 64, 12 - kind, 13 - kind))
+    for b in (0, 1):
+        for a in range(PB - 16, PB + 4096, 1028):
+            ms(C("W%d" % b, a, a + 1028), 0.0)
+        for a in (T2, T2 + 1032):
+            act(C("XW%d" % b, a, a + 1032), C("W0", PB - 16, PB + 1016), 0.0, 99.0)
+        now[0] = b
+        fills("W%d" % b, 0, PB - 16, 0), fills("W%d" % b, PB + 4096, 8192, 0), fills("U%d" % b, 2064, 4112, 0)
+    now[0] = 0
+    fill(C("XB", 1024, 1040), 0), fill(C("BTF", 0, 16), 0)
+    for b in (0, 1):
+        n = str(b)
+        fill(C("TN" + n, 0, 16), 0), fill(C("XW" + n, 0, 16), 99), fill(C("XW" + n, XO + 4096, XO + 4112), 0), fill(C("U" + n, 0, 16), 0)
+        ms(A("ZP" + n), 0.0), fill(C("LT" + n, 0, 64), 0), cp(C("TS" + n, 256, 272), C("ONE", 0, 16))
+        fill(A("TF" + n, al, 0, slice(0, 1)), 16384)
+        fill(A("X" + n), 0), fill(A("X" + n, al, al, UNO), 1)
+        iota(A("X" + n, al, al, CC), [[0, 4]], 0, 16)
+        iota(A("X" + n, al, al, CU), [[0, 4]], -PB, 16)
+        fill(A("PAY" + n), 1)
+        iota(A("PAY" + n, al, al, BAR), [[128, 2], [0, 4]], 1, 1)
+        iota(A("PAY" + n, al, al, HB), [[1, 2], [0, 4]], 0, 0)
+        asel(P("MK" + n, 0, 32), P("ONE", 0, 32), [[0, 2], [-1, 4], [0, 16]], eq, 0.0, -4 * b, 1)
 
-    def book_live():
-        ts(A("NL"), C("LRS", 0, 128), col(PM), ge)
-        tt(A("NL"), A("NL"), A("NEWB"), mult)
-        mm(B(1, 0, 128), S128(BLK), A("NL"))
+    ts(A("RW", al, 0), A("BKI"), 1.0, add, 16.0, mult)
+    send(A("LP1"), A("RW", al, 0), "lp1", -3)
+    send(A("LP2"), A("RW", al, 0), "lp2", -6)
+    ts(A("RW", al, 1), A("ONEB"), col(PM256), mult)
+    iota(A("RW", al, 2), [[1, 256]], 1, 0)
+    for b in (0, 1):
+        now[0] = b
+        for f, src in enumerate((A("RW", slice(64 * b, 64 * b + 64), 0), P("LP1", 64 * b, 64 * b + 64), P("LP2", 64 * b, 64 * b + 64))):
+            for hh in (0, 1):
+                dma("tab%d" % b, rows4("W%d" % b, hh, 2 + 4 * f, PB, PB + 4096), src)
+        for k in (1, 2):
+            dma("tab%d" % b, A("W%d" % b, slice(8 * k - 4, 128, 16), slice(PB, PB + 4096)), A("RW", al, k))
+    now[0] = 0
+    ts(A("BX"), A("BI"), 1.0, add)
+    act(A("BD", al, 0), A("BX"))
+    tt(A("BD", al, 1), A("BX"), A("BD", al, 0), sub)
+    cp(P("SMF", 0, 8, 0, 2), P("SM", 0, 8, 0, 2))
+    cp(P("SMF", 0, 8, 16, 144), P("SM", 0, 8, 16, 144))
+    cp(C("BTF", 16, 144), A("BT"))
+    LB = C("Pd1", 0, 128)
+    mm(LB, P("SMF", 0, 8, 16, 144), P("MK8", 0, 8))
+    tt(A("NEB", al, 0), LB, A("SI"), gt)
+    for b in (0, 1):
+        ts(A("X%d" % b, al, al, LM), C("Pd1", 64 * b, 64 * b + 64, 16), -1.0, add, 1.0 / 32, mult)
+    tt(A("NEB", al, 1), C("BTF", 16, 144), C("BTF", 15, 143), ne)
+    tt(A("NEB", al, 0), A("NEB", al, 0), A("NEB", al, 1), mult)
+    scan(A("CN"), A("NEB", al, 0), A("CONT"), add, mult)
+    ts(A("NTC"), C("CN", 15, 128, 16), col(C16), add)
+    for gi in range(8):
+        ts(C("NTA", 16 * gi, 16 * gi + 16), A("DG"), C("NTC", gi, gi + 1), mult)
 
-    def book_counts():
-        tt(C("LV", 0, 128), B(1, 0, 128), C("DGM", 0, 128), mult)
-        scan(C("LS", 0, 128), C("CONT16", 0, 128), C("LV", 0, 128), 0.0, mult, add)
-        tt(A("NTF"), C("LS", 15, 128, 16), A("NTC"), add)
-        cp(A("NTL"), A("NTF"))
-
-    def book_list():
-        cp(A("PL"), B(7, 0, 128))
-
-    def table1(eng, i, n):
-        w = 128 // n
-        gat(eng, C("TB", 16 + 16 * w * i, 16 + 16 * w * (i + 1)), A("XB"), C("PL", w * i, w * (i + 1)))
-
-    def table2():
-        cp(A("XL"), IND(C("TB", 0, 2064), A("NTL")))
-        cp(IND(C("TB", 2064, 4128), A("NTL")), A("XL"))
-
-    def natural_rows(step):
-        if step == 0:
-            tt(C("Y0", 0, 256), C("PI", 0, 256), A("JI"), add)
-            ts(A("Y0"), A("Y0"), -1.0, amax, 1.0, add)
-            for k in (0, 1):
-                act(C("DG", 512 * k, 512 * k + 256), C("Y0", 256 * k, 256 * k + 256))
-            return
-        if step == 1:
-            for k in (0, 1):
-                tt(C("DG", 512 * k + 256, 512 * k + 512), C("Y0", 256 * k, 256 * k + 256), C("DG", 512 * k, 512 * k + 256), sub)
-            return
-        for gp in (2 * step - 4, 2 * step - 3):
-            bank = "B%d" % (6 + gp % 2)
-            for bl in range(16):
-                mm(A(bank, slice(0, 64), bl), C("DG", bl, 1024, 16), C("ID", 32 * gp, 32 * gp + 32))
-            for k in (0, 1):
-                act(A("RS", slice(0, 64), 2 * gp + k), A(bank, slice(0, 64), al, k))
-
-    def visit(v):
-        off = "OFF%d" % v
-
-        def names(kind, q, lo, n):
-            c0 = lo + (256 * kind + 64 * q if v == 0 else 256 * (q // 2) + 128 * kind + 64 * (q % 2))
-            return C(off, c0, c0 + n)
-
-        def part(nm, q, lo, n):
-            return C(nm, 1024 * q + 16 * lo, 1024 * q + 16 * (lo + n))
-
-        def a(q, lo=0, n=64):
-            gat("s", part("XT", q, lo, n), A("TN"), names(1, q, lo, n))
-
-        def b(q, lo=0, n=64):
-            tt(part("PR", q, lo, n), IND(A("TN"), names(0, q, lo, n)), part("XT", q, lo, n), mult)
-
-        def c(q, eng):
-            gat(eng, part("CO", q, 0, 64), C("W", 0, 4112), names(1, q, 0, 64))
-
-        def H(nm, h, a0=0, n=128):
-            return A(nm, al, h, slice(a0, a0 + n))
-
-        def far(c0):
-            k = (c0 // 32) % 2
-            gat("s", C("XK", 512 * k, 512 * k + 512), A("TB"), C("IDX", c0, c0 + 32))
-            mm(A("B%d" % (6 + k)), A("IDN"), C("XT", 16 * c0, 16 * c0 + 512), True, False)
-            mm(A("B%d" % (6 + k)), A("ID"), C("XK", 512 * k, 512 * k + 512), False, True)
-
-        def same(c0):
-            out, ps = C("EQ", 16 * c0, 16 * c0 + 512), A("B%d" % (6 + (c0 // 32) % 2))
-            rec("s", lambda: g.scalar.activation(out[0], ps[0], AF.Abs), [out], [ps])
-            rec("s", lambda: g.scalar.activation(out[0], out[0], AF.Relu, bias=1.0, scale=-1.0), [out], [out])
-
-        def scores(h, s0=0, s1=16):
-            o = 2048 * h
-            for s in range(s0, s1):
-                out = B(h, s, 384, 128, 16)
-                mm(out, C("CO", o + s, o + 2048, 16), A("SEL", al, 0), True, False)
-                if s < 15:
-                    mm(out, C("CO", o + s + 1, o + 2048, 16), A("SEL", al, 2), False, False)
-                else:
-                    mm(out, A("ONEB"), A("SEL", al, 1), False, False)
-                mm(out, C("PR", o + s, o + 2048, 16), A("SEL", al, 3), False, True)
-
-        def passages(h):
-            ts(H("NEQ", h, 1), B(h, 128, 256), 0.0, ne, 16.0, mult)
-            tt(H("GEQ", h), B(h, 256, 384), A("THT"), ge)
-            tt(H("END", h, 1), H("NEQ", h, 1), H("GEQ", h), mult)
-            ts(H("CNT", h, 1), H("END", h, 1), 0.0, eq)
-            tt(H("AC", h), B(h, 0, 128), H("END", h), mult)
-            scan(H("K16", h), H("NEQ", h), H("CNT", h), 0.0, add, mult)
-            scan(H("C16", h), H("CNT", h), H("AC", h), 0.0, mult, add)
-            mm(B(h, 384, 512), H("K16", h), A("ID16"), True, False)
-            mm(B(h, 384, 512), H("END", h, 1), A("ID129"), False, False)
-            mm(B(h, 384, 512), H("C16", h), A("ID"), False, True)
-            scan(H("RR", h), A("ONEB"), H("CNT", h), 0.0, add, mult)
-            ts(H("ZT", h), H("CNT", h, 1), 87.0, mult, 12.0, add)
-            mm(B(2 + h, 0, 128), H("C16", h), A("ID"))
-            mm(B(2 + h, 128, 256), H("RR", h), A("ID"))
-
-        def index(h):
-            cp(C("IDX", 128 * h, 128 * h + 128), B(h, 384, 512))
-
-        def payload(h):
-            act(H("PC", h), B(2 + h, 0, 128), 1.0 / 16)
-            act(H("PC", h, 128), B(2 + h, 128, 256), -16.0, col(PM17))
-
-        def d(c0, n):
-            tt(C("EQ", 16 * c0, 16 * (c0 + n)), IND(A("TB"), C("IDX", c0, c0 + n)), C("XT", 16 * c0, 16 * (c0 + n)), eq)
-
-        def counts(h):
-            for s in range(16):
-                mm(B(2 + h, 256 + s, 384, 128, 16), C("EQ", 2048 * h + s, 2048 * h + 2048, 16), A("SEL", al, 3, slice(16, 24)))
-
-        def offers(h):
-            scan(A("MN"), H("END", h), B(2 + h, 256, 384), 0.0, amax, amin)
-            tt(A("MT"), A("MN"), H("ZT", h), ge)
-            scan(A("ST"), A("BARC"), A("MT"), 0.0, mult, add)
-            ts(A("FI"), A("ST"), 1.0, eq)
-            mm(B(2 + h, 384, 512), A("FI"), A("ID"))
-
-        def offer_rows(h, step):
-            if step == 0:
-                tt(C("YC", 0, 128), B(2 + h, 384, 512), H("PC", h), mult)
-                tt(C("YC", 128, 256), B(2 + h, 384, 512), H("PC", h, 128), mult)
-                mm(B(4, 0, 128, 32), A("GS", al, 0), C("YC", 0, 128), True, False)
-                mm(B(4, 0, 128, 32), A("GS", al, 1), C("YC", 128, 256), False, True)
-                return
-            act(P("RT", 0, 16, 128 * h, 128 * h + 128), B(4, 0, 128, 16))
-            for gi in range(8):
-                mm(B(4 + gi // 4, 128 * (gi % 4), 128 * (gi % 4) + 128), A("ZL", slice(0, 18), gi), P("RT", 0, 18, 128 * h, 128 * h + 128))
-
-        def lowest(h, k):
-            for gi in range(4 * k, 4 * k + 4):
-                red(A("FB", al, h, slice(gi, gi + 1)), B(4 + k, 128 * (gi % 4), 128 * (gi % 4) + 128))
-
-        if v == 0:
-            ts(A("BL"), B(6, 0, 128), 15.0, add)
-            c(0, "v"), book_new(), a(0), a(1), act(A("ID"), A("IDF"))
-            gat("s", C("XB", 0, 2048), A("TN"), A("BL"))
-            small_constants(), b(0)
-            dma("y", "xb0", C("XT", BOOK, 8192), C("XB", 0, 2048))
-            cp(A("CN"), B(6, 0, 128))
-            book_places(0, 16)
-            c(1, "v"), book_list(), b(1), scores(0), book_live()
-            table1("s", 0, 1), natural_rows(0), a(2), a(3), c(2, "s"), c(3, "s")
-            ts(A("DGM"), A("J16"), col(PM), eq)
-            ts(A("NTC"), A("NTC"), col(PM16), add)
-            passages(0), book_counts()
-            table2(), index(0), d(0, 128), counts(0), natural_rows(1), payload(0), pickers(), b(2)
-            natural_rows(2), offers(0), b(3), natural_rows(3), scores(1)
-            for gi in range(8):
-                dma("y", "rc", P("W", 16 * gi + 4, 16 * gi + 8, 0, 4096), A("RS", slice(0, 64), gi))
-            tt(A("DM"), A("DM"), A("DGM"), mult)
-            single_items()
-            offer_rows(0, 0), offer_rows(0, 1), passages(1), index(1), far(224), payload(1), d(128, 96)
-            same(224), counts(1), lowest(0, 0)
+    def key_table(b, first):
+        n = str(b)
+        move(OPT["ZS"], C("XL" + n, 0, 64), C("Pa" + n, 0, 64))
+        for j, bank in enumerate((lambda k0, k1: A("Pc" + n, al, slice(k0 // 2, k1 // 2)) if k1 - k0 > 1 else A("Pc" + n, al, k0 // 2, slice(4 * (k0 % 2), 4 * (k0 % 2) + 4)),
+                                  lambda k0, k1: C("Pd" + n, 64 * k0, 64 * k1))):
+            row = (bank(0, 8), P("ONEB", 0, 1, 0, 128), P("KR", 0, 1, 512 * j, 512 * j + 512))
+            mms([row] + [(bank(k, k + 1), IDN16, C("XL" + n, 0, 64)) for k in range(8)] + [row])
+            act(A("SG", al, slice(8 * j, 8 * j + 8)), bank(0, 8), 1.0, 0.0, AF.Sign)
+        out = C("Pa" + n, 64, 128)
+        items = [(out, C("USEL", 16 - k, 144 - k), A("SG", al, k)) for k in range(16)]
+        if first:
+            items.append((out, P("ONEB", 0, 1, 0, 128), A("ROWS", slice(0, 1), 4, slice(0, 64))))
         else:
-            c(0, "v"), a(0), a(1), c(1, "s"), a(2), a(3), c(2, "s"), c(3, "s")
-            b(0), table2(), b(1), scores(0), b(2), passages(0), b(3), index(0)
-            scores(1), far(96), d(0, 96), payload(0), same(96)
-            for f in range(4):
-                dma("y", "rows%d" % v, A("W", slice(4 + f, 128, 16), slice(0, 4096)), P("LND%d" % v, 32 * f, 32 * f + 32))
-            passages(1), counts(0), index(1), far(224), payload(1), d(128, 32), offers(0), same(224), d(160, 32), offer_rows(0, 0)
-            d(192, 32), offer_rows(0, 1), counts(1), lowest(0, 0)
+            items[1:1] = [(P("Pa" + n, 64 * hh, 64 * hh + 64, 64, 128), A("SY", slice(0, 64), SPB - hh), P("YS" + n, 0, 64, 64 * hh, 64 * hh + 64)) for hh in (0, 1)]
+        mms(items)
+        ts(A("LS" + n, al, 0), out, 8.0 if first else 0.0, add)
+        gats(OPT["TB"], "TBN" + n, A("XB") if first else A("XW" + n), lambda a, e: A("LS" + n, al, 0, slice(a, e)), 64)
+        tag = "tb%d%d" % (b, len(ops))
+        for hh in (0, 1):
+            for h2 in (0, 1):
+                dma(tag, P("XW" + n, 64 * h2, 64 * h2 + 64, 16 + 1024 * hh, 1040 + 1024 * hh), P("TBN" + n, 64 * hh, 64 * hh + 64))
+        gat(OPT["XL"], A("XL" + n), C("XW" + n, 0, T2), A("NTL" + n))
+        cp(IND(C("XW" + n, T2, XO), A("NTL" + n)), A("XL" + n))
+
+    def turn(b, src, sel, lo, c0=0):
+        for s in range(16):
+            mm(A("Pc%d" % b, al, slice(lo, 3), al, s), C(src, c0 + s, c0 + 2048, 16), A("SELT", al, slice(3 * sel, 3 + 2 * sel)))
+        ts(C("TS%d" % b, 128 * lo, 256), A("Pc%d" % b, al, slice(lo, 2)), -2048.0, add)
+
+    def marks(b, out):
+        n = str(b)
+        act(out(0), A("Pc" + n, al, 2))
+        act(out(2), A("Pc" + n, al, 1), -2.0, 2.0, AF.Relu, False)
+        tt(out(1), C("TS" + n, 128, 256), C("TS" + n, 129, 257), ne)
+
+    def opening(b):
+        n = str(b)
+        W = "W" + n
+        mm(C("Pa" + n, 0, 1), P("MK" + n, 0, 8), P("SMF", 0, 8, 0, 1))
+        tt(A("TI" + n, al, 0, slice(0, 1)), C("Pa" + n, 0, 1), col(PMH), sub)
+        ts(A("JM" + n), A("JI"), A("TI" + n, al, 0, slice(0, 1)), ge, -8192.0, mult)
+        for k in (1, 0):
+            tt(C("Y0" + n, 128 * k, 128 * k + 128), C("PI" + n, 128 * k, 128 * k + 128), A("JM" + n), add)
+            ts(A("OFF" + n, al, 0, slice(128 * k, 128 * k + 128)), C("Y0" + n, 128 * k, 128 * k + 128), -1.0, amax, 16.0, add)
+        ts(P("THX" + n, 0, 8), P("MK" + n, 0, 8), P("SMF", 0, 8, 1, 2), mult, -1.0, mult)
+        act(A("THB" + n, slice(0, 8), 0), P("THX" + n, 0, 8))
+        put(A("THB" + n, slice(0, 32), 1), -8192.0), put(A("THB" + n, slice(0, 32), 1, slice(15, 128, 16)), 8192.0)
+        tt(A("THB" + n, slice(0, 8), 1), P("THX" + n, 0, 8), A("THB" + n, slice(0, 8), 0), sub)
+        for hh in (0, 1):
+            mm(P("Pb" + n, 64 * hh, 64 * hh + 64, 128, 192), C("BTF", 16 + 64 * b, 80 + 64 * b), C("IDF", 64 * hh, 64 * hh + 64))
+        for hh in (0, 1):
+            mm(A("Pb" + n, slice(64 * hh, 64 * hh + 64), 12, slice(0, 8)), C("NTA", 64 * b, 64 * b + 64), SELF)
+        ts(A("LS" + n, al, 1), C("Pb" + n, 128, 192), 16.0, add)
+        cp(A("NTL" + n), A("Pb" + n, al, 12, slice(0, 8)))
+        gats(OPT["XB"], "XB", A("TN" + n), lambda a, e: A("LS" + n, al, 1, slice(a, e)), 64)
+        for hh in (0, 1):
+            mm(P("Pa" + n, 64 * hh, 64 * hh + 64, 0, 64), C("CN", 64 * b, 64 * b + 64), A("IDS", al, 0, slice(64 * hh, 64 * hh + 64)))
+        key_table(b, True)
+        ts(C("Y0" + n, 0, 128), C("Y0" + n, 0, 128), -1.0, amax, 1.0, add)
+        act(C("DU" + n, 0, 128), C("Y0" + n, 0, 128))
+        tt(C("DU" + n, 128, 256), C("Y0" + n, 0, 128), C("DU" + n, 0, 128), sub)
+        for bl in range(4):
+            mm(A("Pb" + n, slice(0, 64), slice(bl, 32, 4)), C("DU" + n, bl, 256, 4), ID1)
+        act(A("RS", slice(0, 64)), A("Pb" + n, slice(0, 64)))
+        gats(OPT["CO"], "CO", C(W, PB - 16, PB + 4096), lambda a, e: A("OFF" + n, al, 0, slice(128 + a, 128 + e)), 128)
+        gats(OPT["CB"], "CB", C(W, PB - 16, PB + 4096), lambda a, e: A("LS" + n, al, 1, slice(a, e)), 64)
+        turn(b, "CO", 1, 1)
+        marks(b, lambda k: A("ATT" + n, al, 0, slice(128 * k, 128 * k + 128)))
+        for hh in (0, 1):
+            for h2 in (0, 1):
+                dma("row0" + n, every(W, h2, 2, PB + 2048 * hh, PB + 2048 * hh + 2048), every("CO", hh, 2, 0, 2048))
+                dma("row0" + n, every(W, h2, 2, 1024 * hh, 1024 * hh + 1024), every("CB", hh, 2, 0, 1024))
+        for k in range(8):
+            p, c0 = 16 * (k % 4), PB + 2048 * (k // 4)
+            dma("row1" + n, A(W, slice(p, p + 16, 8), slice(c0, c0 + 2048)), A("RS", slice(0, 64), k))
+        for f in (0, 1):
+            dma("row1" + n, rows4(W, 0, 8 * f, 0, PB), A("BD", slice(64 * b, 64 * b + 64), f))
+        dma("row2" + n, every(W, 1, 8, 0, PB + 4096), every(W, 0, 8, 0, PB + 4096))
+
+    def visit(v, b):
+        n = str(b)
+        W, XW, TN, Xn, YS, U = "W" + n, "XW" + n, "TN" + n, "X" + n, "YS" + n, "U" + n
+        Pa, Pb, Pc, Pd = ["P" + k + n for k in "abcd"]
+        END, CNT, AC, K, CL, RL = range(6)
+
+        def tf(k, a=0):
+            return A("TF" + n, al, k, slice(a, a + 128))
+
+        def att(a):
+            return A("ATT" + n, al, v, slice(a, a + 128))
+
+        def xc(k, gi=None):
+            return A(Xn, al, al, k) if gi is None else A(Xn, al, gi, slice(k, k + 1))
+
+        def half(name, hh, a, b_):
+            return P(name, 64 * hh, 64 * hh + 64, a, b_)
+
+        def sy(k, hh):
+            return A("SY", slice(0, 64), k)
+
+        def clear(k):
+            fills(U, 16 + 2048 * k, 2064 + 2048 * k, 0)
+
+        nq = OPT["NQ"]
+        w = 128 // nq
+        for q in range(nq):
+            xt = C(XW, XO + 16 * w * q, XO + 16 * w * (q + 1))
+            gat(OPT["XT"], xt, A(TN), A("OFF" + n, al, v, slice(128 + w * q, 128 + w * (q + 1))))
+            tt(C(U, 16 + 16 * w * q, 16 + 16 * w * (q + 1)), IND(A(TN), A("OFF" + n, al, v, slice(w * q, w * (q + 1)))), xt, mult)
         if v < 2:
-            dma("y", "t%d" % (v + 1), C("TB", 2064, 4128), A("N99"))
-        F0, F1 = A("FB", al, 0), A("FB", al, 1)
-        offers(1), offer_rows(1, 0), lowest(0, 1), offer_rows(1, 1)
-        ts(TMP, F0, 32768.0, ge, 1048576.0, mult)
-        ts(F0, F0, -32768.0, add)
-        tt(F0, F0, TMP, add)
-        mm(B(6, 0, 128), A("IDF"), C("LRS", 128, 256), True, False)
-        lowest(1, 0), lowest(1, 1)
-        DL = xk("X3", 9)
-        VI, BB, FS, SEE = [A("TI", al, k) for k in range(4)]
-        tt(VI, F0, F1, amin)
-        ts(BB, VI, 8, AL.arith_shift_right)
-        ts(FS, VI, 4, AL.arith_shift_right, 15, AL.bitwise_and)
-        ts(SEE, VI, 15, AL.bitwise_and)
-        ts(xk("X2", 6), BB, 16.0, mult, 2048.0, add)
-        ts(xk("X1", 2), BB, -16.0, mult, -2048.0, add)
-        ts(xk("X1", 3), FS, -1.0, mult)
-        tt(xk("X2", 7), SEE, LM1, sub)
-        ts(xk("X1", 4), BB, 128.0, ge, -16384.0, mult)
-        tt(xk("X1", 6), xk("X2", 6), ONEL, mult)
-        tt(xk("X1", 7), xk("X2", 7), ONEL, mult)
-        mm(B(0, 0, 128), A("X1"), A("ID"))
-        mm(B(0, 128, 256), A("X2"), A("ID"))
-        act(A("YS"), B(0, 0, 256))
-        for gi in range(8):
-            mm(B(4 + gi // 4, 128 * (gi % 4), 128 * (gi % 4) + 128), A("BS", al, gi), C("YS", 0, 128))
-        ts(TK, BB, 128.0, lt)
-        ts(NTK, BB, 128.0, ge)
-        tt(DL, FS, xk("X2", 7), sub)
-        tt(xk("X3", 0), xk("X2", 6), TK, mult)
-        tt(xk("X3", 1), FS, TK, mult)
-        tt(TMP, DL, TK, mult)
-        ts(xk("X3", 2), NTK, col(C16C), mult)
-        ts(xk("X3", 3), NTK, float(BOOK), mult)
-        tt(xk("X3", 4), LM1, TMP, sub)
-        tt(LM1, LM1, TMP, sub)
-        ts(xk("X3", 5), xk("X3", 4), 0.0, eq, 16384.0, mult)
-        mm(B(1, 0, 128), A("X3"), A("ID"))
-        act(A("Y3"), B(1, 0, 128))
-        mm(B(2, 0, 128), S128(SPOS), C("YS", 0, 128), True, False)
-        mm(B(6, 0, 128), S128(SPOS), C("YS", 0, 128), False, False)
-        for gi in range(8):
-            ts(A("MG", al, gi), B(4 + gi // 4, 128 * (gi % 4), 128 * (gi % 4) + 128), C("X1", 16 * gi + 2, 16 * gi + 3), lt, C("X3", 16 * gi + 9, 16 * gi + 10), mult)
-            for k in (2, 6):
-                mm(B(k, 0, 128), C("V1", 112 - 16 * gi, 240 - 16 * gi), A("MG", al, gi), False, gi == 7)
-            if gi == 3:
-                for i, k in enumerate((SF, SL, SLE)):
-                    mm(B(3, 128 * i, 128 * i + 128), S128(k), A("Y3"))
-        if v < 2:
-            ts(A("FL"), B(3, 0, 128), col(PM), add)
+            for hh in (0, 1):
+                dma("swap%d%d" % (v, b), half(XW, 1 - hh, XO + 2048, XO + 4096), half(XW, hh, XO, XO + 2048))
+        mm(C(Pa, 128, 256), IDM14, att(0))
+        SC = C(Pa, 0, 128)
+        mms([(SC, ID8K, att(128))] + [(SC, P("ONEB", 0, 8, 0, 128), A("THB" + n, slice(0, 8), 0)), (C(Pa, 0, 127), ID8K, A("ATT" + n, al, v, slice(257, 384)))] +
+            [(C(Pa, s, 128, 16), C(U, 16 + s, 2064, 16), A("SEL", al, 0)) for s in range(16)] + [(SC, P("ONEB", 0, 9, 0, 128), A("THB" + n, slice(0, 9), 1))])
+        clear(0)
+        ts(tf(END, 1), SC, 0.0, ge, 16384.0, mult)
+        if OPT["CNT"] == "s":
+            act(tf(CNT), tf(END), -2.0 ** -14, 1.0)
         else:
-            ts(C("SRC", 0, 128), B(3, 128, 256), col(PM), ge)
-            ts(C("SRC", 128, 256), B(3, 0, 128), col(PM), add, -4096.0, add)
-            tt(C("SRC", 0, 128), C("SRC", 0, 128), C("SRC", 128, 256), mult)
-            ts(A("FL"), C("SRC", 0, 128), 4096.0, add)
-        gat("s", A("FO"), A("W"), A("FL"))
+            ts(tf(CNT), tf(END), 0.0, eq)
+        tt(tf(AC), C(Pa, 128, 256), tf(END), mult)
+        scan(tf(K), att(127), tf(CNT), add, mult)
+        scan(tf(CL), tf(CNT), tf(AC), mult, add)
+        scan(tf(RL), C("ONEB", 0, 128), tf(CNT), add, mult)
+        IX = C(Pa, 256, 384)
+        mms([(IX, tf(END, 1), ID129), (IX, tf(K), ID1), (IX, tf(CL), ID1)])
+        cp(A("IDX" + n), IX)
+        one = P("ONEB", 0, 1, 0, 128)
+        PV, Z = C(Pb, 0, 128), C(Pb, 128, 256)
+        mms([(PV, one, A("ROWS", slice(0, 1), 0)), (PV, ID1, tf(END, 1)), (PV, ID16, tf(CL)), (PV, ID32, tf(RL))])
         if v < 2:
-            gat("s", C("XB", 0, 16 * XS), A("XT"), C("FL", 0, XS))
-        tt(C("LV", 0, 128), B(2, 0, 128), C("DM", 0, 128), amin)
-        tt(C("LV", 128, 256), B(6, 0, 128), C("DM", 128, 256), amin)
-        scan(A("LS"), A("CONT16"), A("LV"), 0.0, mult, add)
-        ts(A("EL"), C("LS", 15, 256, 16), 16.0, add)
-        cp(IND(A("SCW"), A("EL")), A("YS"))
+            mms([(Z, one, A("ROWS", slice(0, 1), 2)), (Z, ID1, tf(K)), (Z, IDN16, tf(RL))])
+            act(A("ZP" + n, al, al, slice(48, 64)), Z)
+        for q in range(OPT["NE"]):
+            u = 128 // OPT["NE"]
+            tt(C("EQ" + n, 16 * u * q, 16 * u * (q + 1)), IND(C(XW, 0, XO), C("IDX" + n, u * q, u * (q + 1))), C(XW, XO + 16 * u * q, XO + 16 * u * (q + 1)), eq)
+        CB = C(Pa, 384, 512)
+        mms([(CB, one, A("ROWS", slice(0, 1), 1))] + [(C(Pa, 384 + s, 512, 16), C("EQ" + n, s, 2048, 16), A("SEL", al, 1)) for s in range(16)] +
+            [(CB, one, A("ROWS", slice(0, 1), 1))])
+        MN, VAL, OV, LV = [A("FS" + n, al, k) for k in range(4)]
+        scan(MN, tf(END), CB, amax, amin)
+        tt(VAL, PV, MN, amin)
+        scan(OV, A("CONT"), VAL, mult, amax)
+        best, REM, C1 = A("FS" + n, al, 2, slice(15, 128, 16)), A("TI" + n, al, 1), A("TI" + n, al, 2)
+        ts(A("PAY" + n, al, al, EE), best, 1.5 * 2.0 ** 32, add, -1.5 * 2.0 ** 32, add)
+        tt(REM, best, A("PAY" + n, al, al, EE), sub)
+        ts(C1, REM, 1.5 * 2.0 ** 23, add, -1.5 * 2.0 ** 23, add)
+        for k in range(8):
+            ts(C("OH", 128 * k, 128 * k + 128), A("IOC"), A("TI" + n, al, 2, slice(k, k + 1)), eq)
+        tt(A("PAY" + n, al, al, RR), REM, C1, sub)
+        mm(A(Pc), A("TRI"), C("OH", 0, 512))
+        mms([(A(Pd), A("NEG"), C("OH", 0, 512)), (A(Pd), A("TRI"), C("OH", 512, 1024))])
+        act(C("TK" + n, 0, 512), A(Pc), 1.0, 0.0, AF.Relu)
+        if OPT["TK1"] == "s":
+            act(C("TK" + n, 512, 1024), A(Pd), 1.0, 0.0, AF.Relu)
+        else:
+            ts(C("TK" + n, 512, 1024), A(Pd), 0.0, amax)
+        for gi in range(4):
+            mms([(A(Pb, al, 16 + gi, slice(0, 5)), C("TK" + n, 512 * hh + 128 * gi, 512 * hh + 128 * gi + 128), A("PAY" + n, al, 4 * hh + gi, slice(0, 5))) for hh in (0, 1)])
+        mms([(A(Pc), A("BARX", al, hh), C("TK" + n, 512 * hh, 512 * hh + 512)) for hh in (0, 1)])
+        move(OPT["XC"], A(Xn, al, al, slice(0, 5)), A(Pb, al, slice(16, 20), slice(0, 5)))
+        TMP = A("TI" + n, al, 3, slice(0, 4))
+        tt(TMP, xc(TKN), xc(LM), mult)
+        tt(xc(DL), TMP, xc(RR), sub)
+        tt(xc(CT), xc(TKN), xc(CC), mult)
+        if v == 2:
+            tt(xc(LN), xc(LM), xc(DL), sub)
+        for hh in (0, 1):
+            mm(half(Pb, hh, 320, 448), A(Xn), ID1)
+        move(OPT["YS"], A(YS), C(Pb, 320, 448))
         if v < 2:
-            single_items()
-        for h in (0, 1):
-            o = 2048 * h
-            for s in range(16):
-                mm(B(6 + h, 0, 128), A("UTRI", al, s), C("SCW", 16 + o + s, 16 + o + 2048, 16), s == 0, s == 15)
-            cp(C("LOC", 1 + 128 * h, 129 + 128 * h), B(6 + h, 0, 128))
-        for h in (0, 1):
-            o = 2048 * h
-            mm(B(h, 0, 128), S128(SE), C("SCW", o + 15, o + 2048, 16), True, False)
-            mm(B(h, 0, 128), A("M15"), C("LOC", 128 * h, 128 * h + 128), False, False)
-            mm(B(h, 0, 128), A("IDF"), C("LOC", 1 + 128 * h, 129 + 128 * h), False, True)
-            scan(C("SRC", 128 * h, 128 * h + 128), A("C16F"), B(h, 0, 128), col(INI) if h == 0 else C("SRC", 127, 128), add, add)
-            cp(C("SRU", 128 * h, 128 * h + 128), C("SRC", 128 * h, 128 * h + 128))
-            for eng, lo, hi in ((("s", 0, 128),), (("s", 128, 128 + ES), ("v", 128 + ES, 256)))[h]:
-                if hi > lo:
-                    gat(eng, C("EO", 16 * lo, 16 * hi), A("W"), C("SRU", lo, hi))
+            tt(xc(LM), xc(LM), xc(DL), sub)
+        for gi in range(4):
+            ts(A("MG" + n, al, gi), A(Pc, al, gi), xc(BAR, gi), gt, xc(DL, gi), mult)
+        POS = C(Pd, 0, 128)
+        mms([(POS, C("V1", 48 - 16 * gi, 176 - 16 * gi), A("MG" + n, al, gi)) for gi in range(4)] + [(POS, A("SY", slice(0, 64), slice(SPOS, SPOS + 2)), P(YS, 0, 64))])
+        tt(LV, POS, A("DM"), amin)
+        scan(MN, A("CONT"), LV, mult, add)
+        ts(A("EL" + n), A("FS" + n, al, 0, slice(15, 128, 16)), col(KIND), add)
+        cp(IND(A(U), A("EL" + n)), A(YS))
+        for hh in (0, 1):
+            mms([(A(Pc, al, 0, slice(4 * hh, 4 * hh + 4)), C(U, 16 + 2048 * hh + o, 2064 + 2048 * hh + o, 16), A("SELI", al, al, slice(16 - o, 32 - o))) for o in range(-15, 16)])
         if v < 2:
-            gat("s", C("XB", 16 * XS, 2048), A("XT"), C("FL", XS, 128))
+            clear(1)
+        if OPT["LT"] == "s":
+            act(C("LT" + n, 64, 192), A(Pc, al, 0), 1.0, 16.0)
+        else:
+            ts(C("LT" + n, 64, 192), A(Pc, al, 0), 16.0, add)
+        SRC = C(Pd, 128, 256)
+        mms([(SRC, C("LT" + n, 64, 192), A("UP")), (SRC, C("LT" + n, 0, 128), A("ONE"))])
+        ts(A("SRU" + n), SRC, col(SRC0), add)
+        gats(OPT["EO"], U, A(W), lambda a, e: C("SRU" + n, a, e), 128, EO)
+        for hh in (0, 1):
+            mm(half(Pb, hh, 448, 512), sy(SFL, hh), P(YS, 0, 64, 64 * hh, 64 * hh + 64))
+        FL = A("LS" + n, al, 2)
+        if v < 2:
+            ts(FL, C(Pb, 448, 512), col(PM), add)
+        else:
+            for hh in (0, 1):
+                mm(half(Pb, hh, 0, 64), sy(SLN, hh), P(YS, 0, 64, 64 * hh, 64 * hh + 64))
+            T1, T2_ = A("FS" + n, al, 1, slice(0, 64)), A("FS" + n, al, 1, slice(64, 128))
+            ts(T1, C(Pb, 0, 64), col(PM), lt, 16384.0, mult)
+            tt(T2_, C(Pb, 448, 512), T1, add)
+            ts(FL, T2_, col(PM), add, 8000.0, amin)
+        turn(b, U, 0, 0, EO)
+        for k in (1, 0):
+            mm(C(Pd, 256 + 128 * k, 384 + 128 * k), C("TS" + n, 128 * k, 128 * k + 128), A("IDH"))
+        if v < 2:
+            ts(A("OUT" + n, al, v), C(Pd, 256, 512), 2063.0, add)
+            send(A("OFF" + n, al, v + 1), A("OUT" + n, al, v), "off%d%d" % (v + 1, b), 3)
+            marks(b, lambda k: A("ATO" + n, al, v, slice(128 * k, 128 * k + 128)))
+            send(A("ATT" + n, al, v + 1), A("ATO" + n, al, v), "att%d%d" % (v + 1, b), 3, "off%d%d" % (v + 1, b))
+            dma("stg%d%d" % (v, b), A("STG" + n, al, v, slice(0, 512)), A(U, slice(0, 128, 4), slice(EO, EO + 2048)))
             if v == 0:
-                dma("y", "xb1", C("XT", BOOK, 8192), C("XB", 0, 2048))
-            book_compact(UDF, B(7, 0, 128), "FO", 0)
+                dma("stg%d%d" % (v, b), A("STG" + n, al, v, slice(512, 640)), A(U, slice(10, 128, 16), slice(EO, EO + 2048)))
+            send(A("LND" + n, al, v, slice(0, 640 - 128 * v)), A("STG" + n, al, v, slice(0, 640 - 128 * v)), "lnd%d%d" % (v + 1, b), 3, "att%d%d" % (v + 1, b))
         else:
-            for q in range(8):
-                mm(B(6, 0, 256), C("UZ", 8 - q, 136 - q), C("FO", 256 * q, 256 * q + 256), q == 0, q == 7)
-        for h in (0, 1):
-            for s in range(16):
-                mm(B(4 + h, s, 512, 128, 16), C("EO", 2048 * h + s, 2048 * h + 2048, 16), C("EQF", 32, 64))
+            act(A("Y0" + n), C(Pd, 256, 512), 1.0, 2047.0)
+            for k, dst in enumerate((T.yu, T.yt)):
+                for hh in (0, 1):
+                    dma("yo" + n, X(dst[64 * b:64 * b + 64, 128 * hh:128 * hh + 128]), half("Y0" + n, hh, 128 * k, 128 * k + 128))
+        gats(OPT["FO"], "FO" + n, A(W), lambda a, e: A("LS" + n, al, 2, slice(a, e)), 64)
         if v < 2:
-            book_new()
-        for h in (0, 1):
-            (cp if v == 2 and h == 1 else act)(A("ETS", al, h), B(4 + h, 0, 512))
-            bk = 2 * h
-            for f in range(4):
-                mm(B(bk, 128 * (f // 2), 128 * (f // 2) + 128), H("ETS", h, 128 * f), A("ID"), f % 2 == 0, f % 2 == 1)
-            if v < 2:
-                if h == 0:
-                    cp(A("CN"), B(6, 0, 128))
-                else:
-                    act(A("LRS"), B(3, 128, 384))
-                    book_places(0, 6)
-                o = C("OUT%d" % v, 256 * h, 256 * h + 256)
-                ts(o, B(bk, 0, 256), 15.0, add)
-                send(C("OFF%d" % (v + 1), 256 * h, 256 * h + 256), o, "arr%d%d" % (v + 1, h))
-            else:
-                ts(A("YO", al, h), B(bk, 0, 256), -1.0, add)
-                dma("y", "yo", X(T.yu[:, 128 * h:128 * h + 128]), H("YO", h))
-                dma("y", "yo", X(T.yt[:, 128 * h:128 * h + 128]), H("YO", h, 128))
-        if v < 2:
-            for f in range(4):
-                dma("y", "stg%d" % v, A("STG%d" % v, slice(32 * f, 32 * f + 32)), A("EO", slice(4 + f, 128, 16)))
-            send(A("LND%d" % (v + 1)), A("STG%d" % v), "arw%d" % (v + 1))
-            for f in range(4):
-                dma("y", "fo%d" % v, A("W", slice(4 + f, 128, 16), slice(BOOK, 8192)), A("FO", slice(4 + f, 128, 16)))
-            clear_steps("zs%d" % v)
-            book_places(6, 16), book_live(), book_list(), table1("s", 1, 2), book_counts(), table1("v", 0, 2)
+            for h2 in (0, 1):
+                out = half(Pa, h2, 0, 64)
+                mms([(out, A("ROWS", slice(0, 1), 3, slice(0, 64)), P("ONEB", 0, 1, 0, 64)), (out, sy(SZC, h2), P(YS, 0, 64, 64 * h2, 64 * h2 + 64))] +
+                    [(out, A("ZP" + n, al, k, slice(48 - 16 * (k % 4), 112 - 16 * (k % 4))), C("TK" + n, 128 * k + 64 * h2, 128 * k + 64 * h2 + 64)) for k in range(8)])
+            key_table(b, False)
+            for hh in (0, 1):
+                for h2 in (0, 1):
+                    dma("fo%d%d" % (v, b), every(W, h2, 2 + 2 * v, 1024 * hh, 1024 * hh + 1024), every("FO" + n, hh, 2 + 2 * v, 0, 1024))
+                    dma("rows%d%d" % (v, b), every(W, h2, 4, PB + 2048 * hh, PB + 2048 * hh + 2048), A("LND" + n, slice(64 * hh, 64 * hh + 64), v, slice(0, 512)))
+                    if v == 0:
+                        dma("rows%d%d" % (v, b), rows4(W, h2, 6, PB + 2048 * hh, PB + 2048 * hh + 2048), A("LND" + n, slice(64 * hh, 64 * hh + 64), v, slice(512, 640)))
         else:
-            act(A("ZO"), B(6, 0, 256), 1.0, -1.0)
-            dma("s", "zo", X(T.zu[:]), P("ZO", 0, 64))
-            dma("s", "zo", X(T.zt[:]), P("ZO", 64, 128))
+            ZO = C(Pa, 0, 128)
+            mms([(ZO, C("UZ", 8 - q, 136 - q), C("FO" + n, 128 * q, 128 * q + 128)) for q in range(8)])
+            act(A("JM" + n), ZO, 1.0, -1.0)
+            for k, dst in enumerate((T.zu, T.zt)):
+                dma("zo" + n, X(dst[4 * b:4 * b + 4]), P("JM" + n, 64 * k, 64 * k + 64))
 
+    for b in (0, 1):
+        now[0] = b
+        opening(b)
     for v in range(3):
-        visit(v)
+        for b in (0, 1):
+            now[0] = b
+            visit(v, b)
 
-    know = {e: {} for e in Q}
-    seen, need, pos, cnt = [], set(), [], {e: 0 for e in Q}
-    for i, o in enumerate(ops):
-        e = o["eng"]
-        o["waits"] = []
-        if e == "x":
-            seen.append({}), pos.append(0)
-            continue
-        k = know[e]
-        for j in sorted(o["deps"], reverse=True):
-            gj = ops[j]["grp"]
-            key, val = (gj, 1) if gj is not None else (ops[j]["eng"], pos[j])
-            if k.get(key, 0) >= val:
+    if not planned:
+        for o in ops:
+            o["all"] = set(o["soft"])
+            for j in o["deps"]:
+                o["all"].update(grp[ops[j]["grp"]] if ops[j]["grp"] is not None else [j])
+        for arr, snd in sends.values():
+            ops[arr]["all"].add(snd)
+        succ = [[] for _ in ops]
+        for i, o in enumerate(ops):
+            for j in o["all"]:
+                succ[j].append(i)
+
+        def gap(j, i):
+            return 0.0 if j in ops[i]["soft"] else ops[j]["lat"] + (0.0 if ops[i]["eng"] == "x" else COST["sem"])
+
+        left = [len(o["all"]) for o in ops]
+        topo_order = [i for i in range(len(ops)) if not left[i]]
+        for i in topo_order:
+            for j in succ[i]:
+                left[j] -= 1
+                if not left[j]:
+                    topo_order.append(j)
+        way, taken = [0.0] * len(ops), {}
+        for i in reversed(topo_order):
+            way[i] = (ops[i]["dur"]["s"] if ops[i]["eng"] == "f" else ops[i]["dur"]) + max([gap(i, j) + way[j] for j in succ[i]] + [ops[i]["lat"]])
+        way = [w + (OPT["lead"] if ops[i]["batch"] == 0 else 0.0) for i, w in enumerate(way)]
+        left = [len(o["all"]) for o in ops]
+        ready = {e: [] for e in "gvstyxf"}
+        at = [0.0] * len(ops)
+        for i, o in enumerate(ops):
+            if not left[i]:
+                ready[o["eng"]].append(i)
+        free = {e: 0.0 for e in "gsvtyx"}
+        order = []
+
+        def cost(i, e):
+            return ops[i]["dur"][e] if ops[i]["eng"] == "f" else ops[i]["dur"]
+
+        while len(order) < len(ops):
+            pick = None
+            for e in free:
+                r = ready[e] + ready["f"] if e in "vs" else ready[e]
+                if r:
+                    t = max(free[e], min(at[i] for i in r))
+
+                    def worth(i):
+                        return way[i] - OPT["look"] * max(0.0, at[i] - t) - (OPT["shy"] if e == "v" and ops[i]["eng"] == "f" else 0.0), -i
+
+                    i = max(r, key=worth)
+                    fits = [j for j in r if max(at[j], t) + cost(j, e) <= at[i] + OPT["slack"] and j != i]
+                    if at[i] > t and fits:
+                        i = max(fits, key=worth)
+                    t = max(t, at[i])
+                    if pick is None or t < pick[0]:
+                        pick = (t, e, i)
+            t, e, i = pick
+            ready[ops[i]["eng"]].remove(i)
+            order.append(i)
+            free[e] = t + cost(i, e)
+            if ops[i]["eng"] == "f":
+                ops[i]["eng"], taken[i] = e, e
+            for j in succ[i]:
+                at[j] = max(at[j], free[e] + gap(i, j))
+                left[j] -= 1
+                if not left[j]:
+                    ready[ops[j]["eng"]].append(j)
+        know = {e: {} for e in Q}
+        seen, need, pos, cnt, waits = {}, set(), {}, {e: 0 for e in Q}, {}
+        when = {i: k for k, i in enumerate(order)}
+        for i in order:
+            o = ops[i]
+            e = o["eng"]
+            waits[i] = []
+            if e == "x":
+                seen[i], pos[i] = {}, 0
                 continue
-            members = grp[gj] if gj is not None else [j]
-            assert max(members) < i
-            o["waits"].append(j)
-            need.add(j)
-            k[key] = val
-            for m in members:
-                for kk, vv in seen[m].items():
-                    if k.get(kk, 0) < vv:
-                        k[kk] = vv
-        cnt[e] += 1
-        pos.append(cnt[e])
-        seen.append(dict(k))
+            k = know[e]
+            for j in sorted(o["deps"], key=lambda j: -when[j]):
+                gj = ops[j]["grp"]
+                key, val = (gj, 1) if gj is not None else (ops[j]["eng"], pos[j])
+                if k.get(key, 0) >= val:
+                    continue
+                waits[i].append(j)
+                need.add(j)
+                k[key] = val
+                for m in (grp[gj] if gj is not None else [j]):
+                    for kk, vv in seen[m].items():
+                        if k.get(kk, 0) < vv:
+                            k[kk] = vv
+            cnt[e] += 1
+            pos[i] = cnt[e]
+            seen[i] = dict(k)
+        PLAN.update({"order": order, "waits": waits, "need": need, "span": max(free.values()), "taken": taken})
+    order, waits, need = PLAN["order"], PLAN["waits"], PLAN["need"]
+    for i, e in PLAN["taken"].items():
+        ops[i]["eng"], ops[i]["fn"] = e, ops[i]["fn"][e]
     total = {e: 0 for e in Q}
     val = {}
-    for i, o in enumerate(ops):
-        if o["grp"] is None and i in need:
-            total[o["eng"]] += 1
-            val[i] = total[o["eng"]]
+    for i in order:
+        if ops[i]["grp"] is None and i in need:
+            total[ops[i]["eng"]] += 1
+            val[i] = total[ops[i]["eng"]]
     gsum = {k: sum(ops[m]["inc"] for m in members) for k, members in grp.items()}
-    gsum["sent"] = n_eng * len(grp["sent"])
-    for i, o in enumerate(ops):
+    for i in order:
+        o = ops[i]
         e = o["eng"]
         if e == "x":
             continue
-        for j in o["waits"]:
+        for j in waits[i]:
             gj = ops[j]["grp"]
             if gj is not None:
-                Q[e].wait_ge(T.sem[gj], gsum[gj])
+                Q[e].wait_ge(sem_of(gj), gsum[gj])
             else:
                 Q[e].wait_ge(T.sem["c" + ops[j]["eng"]], val[j])
         ins = o["fn"]()
         if o["grp"] is not None:
-            if o["inc"]:
-                ins.then_inc(T.sem[o["grp"]], 16)
+            if o["grp"] != "sent":
+                ins.then_inc(sem_of(o["grp"]), 16)
         elif i in need:
             ins.then_inc(T.sem["c" + e], 1)
     for e in "vstg":
         if total[e]:
             g.wait_ge(T.sem["c" + e], total[e])
     for k in gsum:
-        g.wait_ge(T.sem[k], gsum[k])
+        g.wait_ge(T.sem["sent"] if k == "sent" else sem_of(k), gsum[k])

from concourse.mybir import AluOpType, AxisListType, ActivationFunctionType

BF, F32, I32, U16, F16 = "bfloat16", "float32", "int32", "uint16", "float16"
PB = 2048
T2, XO = 2064, 4128
DUMMY = 6048
EO = 4112
OPT = {"shy": 3000.0, "slack": 100.0, "XT": "f", "CNT": "s", "TK1": "s", "FO": "ff", "TB": "ff", "XL": "f", "CO": "ffff", "CB": "ff", "XB": "ff", "EO": "ffff", "XC": "f", "ZS": "f", "LT": "s", "YS": "f", "NQ": 4, "NE": 4, "look": 10.0, "lead": 6500.0}


def _s(n, d):
    return ("sbuf", [128] + (list(n) if isinstance(n, (list, tuple)) else [n]), d)


SHARED = {
    "WR": _s([13, 128], BF), "WC": _s(16, F32), "BLK": _s(128, F32), "CO": _s(2048, BF), "CB": _s(1024, BF), "XB": _s(1040, BF), "SG": _s([16, 64], BF), "OH": _s(1024, BF),
    "BKI": _s(256, I32), "RW": _s([3, 256], BF), "LP1": _s(256, BF), "LP2": _s(256, BF),
    "BI": _s(128, I32), "BX": _s(128, F32), "BD": _s([2, 128], BF), "BT": _s(128, I32), "BTF": _s(144, F32),
    "SM": _s(144, I32), "SMF": _s(144, F32), "PMI": _s(2, I32), "COL": _s(8, F32), "JI": _s(128, F32), "SI": _s(128, F32),
    "NEB": _s([2, 128], BF), "CN": _s(128, BF), "NTC": _s(8, F32), "NTA": _s(128, F32), "E16": _s(128, BF), "DG": _s(16, F32),
    "ONE": _s(128, F32), "ONEB": _s(256, BF), "NEG": _s(128, BF), "IDF": _s(128, F32), "IDS": _s([7, 128], BF),
    "TRI": _s(128, BF), "SEL": _s([2, 8], BF), "SELT": _s([5, 8], BF), "IOC": _s(128, BF),
    "CONT": _s(128, F32), "DM": _s(128, F32), "BARX": _s([2, 128], BF), "IDH": _s(128, F16), "V1": _s(176, BF), "ROWS": _s([6, 128], BF), "UP": _s(128, F32), "KR": _s(1024, BF),
    "SY": _s([7, 64], BF), "SELI": _s([4, 48], BF), "USEL": _s(160, BF), "UZ": _s(144, BF), "MK8": _s(128, F32), "RS": _s([8, 4, 16], BF),
}
EACH = {
    "TN": _s(4112, BF), "W": _s(8192, BF), "XW": _s(XO + 4112, BF), "U": _s(6208, BF), "EQ": _s(2048, BF),
    "FO": _s(1024, BF), "TBN": _s(1024, BF), "TK": _s(1024, BF), "MG": _s([4, 128], BF), "ZP": _s([8, 112], BF),
    "OFF": _s([3, 256], U16), "ATT": _s([3, 384], BF), "OUT": _s([2, 256], U16), "ATO": _s([2, 384], BF), "STG": _s([2, 640], BF), "LND": _s([2, 640], BF),
    "PI": _s(256, I32), "Y0": _s(256, F32), "DU": _s(256, BF), "JM": _s(128, F32), "MK": _s(128, F32), "THX": _s(128, F32),
    "TF": _s([6, 144], BF), "IDX": _s(128, U16), "FS": _s([4, 128], F32), "TI": _s([4, 8], F32), "PAY": _s([8, 8], BF), "X": _s([4, 16], BF),
    "YS": _s(128, BF), "EL": _s(8, U16), "LS": _s([4, 64], U16), "LT": _s(192, F32), "SRU": _s(128, U16), "TS": _s(272, F16), "THB": _s([2, 128], BF), "NTL": _s(8, U16), "XL": _s(128, BF),
}
ONCE = ("XL", "MG", "DU", "EL", "THX", "LT", "SRU", "TBN")
SCRATCH = dict(SHARED)
for _b in (0, 1):
    SCRATCH.update({k + str(_b): v for k, v in EACH.items() if _b == 0 or k not in ONCE})
    SCRATCH.update({"P%s%d" % (k, _b): ("psum", [128, 512], F32) for k in "ad"})
    SCRATCH["Pb%d" % _b] = ("psum", [128, 32, 16], F32)
    SCRATCH["Pc%d" % _b] = ("psum", [128, 4, 8, 16], F32)
SEMAPHORES = ["cg", "cv", "cs", "ct", "sent"] + ["d%d" % i for i in range(140)]
SIZE = {F16: 2, BF: 2, F32: 4, I32: 4, U16: 2}
AL = AluOpType
AF = ActivationFunctionType
PLAN = {}
COST = {"act": 100.0, "cyc": 0.9, "gr": 1.5, "sr": 3.5, "pe": 0.5, "sem": 120.0, "dma": 1900.0, "rem": 3000.0, "bw": 250.0, "rbw": 60.0, "iy": 100.0, "ig": 900.0}


def rank_program(g, core, T, topo):
    rank = T.rank_of(core)
    if rank is None:
        return
    n_ranks = len(T.cores)
    Q = {"g": g, "v": g.vector, "s": g.scalar, "t": g.tensor, "y": g.sync}
    ops, acc, grp, sems = [], {}, {}, {}
    planned = "order" in PLAN
    now = [0]
    cyc = COST["cyc"]

    def sem_of(group):
        if group not in sems:
            sems[group] = "d%d" % len(sems)
        return T.sem[sems[group]]

    def A(name, *ix):
        if name[:-1] in ONCE:
            name = name[:-1] + "0"
        where, shape, d = SCRATCH[name]
        ix = list(ix) + [slice(None)] * (len(shape) - len(ix))
        if planned:
            return (T[name][tuple(ix)], [])
        pm = 0
        for i in range(*ix[0].indices(128)):
            pm |= 1 << i
        lo = hi = 0
        stride, em = 1, 1
        for k in range(len(shape) - 1, 0, -1):
            r = range(ix[k], ix[k] + 1) if isinstance(ix[k], int) else range(*ix[k].indices(shape[k]))
            lo += r[0] * stride
            hi += r[-1] * stride
            if stride == 1 and r.step == 1:
                em = ((1 << len(r)) - 1) << r[0]
            else:
                em = sum(em << (i * stride) for i in r)
            stride *= shape[k]
        z = SIZE[d]
        return (T[name][tuple(ix)], [(name, pm, lo * z, (hi + 1) * z, em)])

    al = slice(None)

    def P(name, p0, p1, a=None, b=None, st=None):
        if name[:2] == "Pb":
            return A(name, slice(p0, p1), slice(a // 16, b // 16))
        return A(name, slice(p0, p1), slice(a, b, st))

    def C(name, a, b=None, st=None):
        return P(name, 0, 128, a, b, st)

    def col(j, p1=128):
        return P("COL", 0, p1, j, j + 1)

    def IND(win, off):
        return (win[0].indirect(off[0]), win[1], off[1], 16 * width(off))

    def X(ap):
        return (ap, [])

    def width(x):
        if len(x) > 3:
            return x[3]
        n = 1
        for k in x[0].shape[1:]:
            n *= k
        return n

    def size(x):
        return SIZE[SCRATCH[x[1][0][0]][2]] if x[1] else 4

    def narrow(*xs):
        return all(x[1] and size(x) == 2 for x in xs)

    def in_psum(x):
        return bool(x[1]) and SCRATCH[x[1][0][0]][0] == "psum"

    def rec(eng, fn, outs, ins, dur, group=None, inc=16, lat=0.0):
        me = len(ops)
        op = {"eng": eng, "fn": fn, "deps": set(), "soft": set(), "grp": group, "inc": inc, "dur": dur, "lat": lat, "batch": now[0]}
        ops.append(op)
        if group is not None:
            grp.setdefault(group, []).append(me)
        if planned:
            return me
        rd, wr = [], []
        for o in outs:
            wr += o[1]
            if len(o) > 2:
                rd += o[2]
        for i in ins:
            if isinstance(i, tuple):
                rd += i[1]
                if len(i) > 2:
                    rd += i[2]
        for lst, w in ((rd, False), (wr, True)):
            for (nm, pm, lo, hi, em) in lst:
                ps = SCRATCH[nm][0] == "psum"
                for (o, pm2, lo2, hi2, w2, em2) in acc.setdefault(nm, []):
                    e2, g2 = ops[o]["eng"], ops[o]["grp"]
                    same = e2 == eng != "f" and g2 is None and group is None
                    if ps:
                        if not same:
                            op["deps"].add(o)
                        elif eng == "t":
                            op["soft"].add(o)
                        continue
                    if not (w or w2) or not (pm & pm2):
                        continue
                    if (g2 is None) != (group is None):
                        hit = lo // 16 <= (hi2 - 1) // 16 and lo2 // 16 <= (hi - 1) // 16
                    else:
                        hit = (em & em2) != 0
                    if hit and not (group is not None and g2 == group):
                        op["deps"].add(o)
        for lst, w in ((rd, False), (wr, True)):
            for (nm, pm, lo, hi, em) in lst:
                if SCRATCH[nm][0] == "psum":
                    acc[nm] = [a for a in acc[nm] if ops[a[0]]["eng"] != "t" or eng != "t"]
                acc[nm].append((me, pm, lo, hi, w, em))
        return me

    def ap(x):
        return x[0] if isinstance(x, tuple) else x

    def vec(n, fast=False):
        return max(64, n * (0.5 if fast else 1)) * cyc

    def ts(out, in0, s1, op0, s2=None, op1=None):
        dur = vec(width(in0), narrow(out, in0))
        if op1 is None:
            rec("v", lambda: g.vector.tensor_scalar(out[0], in0[0], ap(s1), None, op0), [out], [in0, s1], dur)
        else:
            rec("v", lambda: g.vector.tensor_scalar(out[0], in0[0], ap(s1), ap(s2), op0, op1), [out], [in0, s1, s2], dur)

    def tt(out, a, b, op):
        dur = 50 + width(a) * COST["gr"] * cyc if len(a) > 2 else vec(width(a) * (1 if in_psum(a) or in_psum(b) else 2))
        rec("v", lambda: g.vector.tensor_tensor(out[0], a[0], b[0], op), [out], [a, b], dur)

    def cp(out, a):
        dur = 50 + width(a) * COST["gr" if len(a) > 2 else "sr"] * cyc if len(a) > 2 or len(out) > 2 else vec(width(a), narrow(out, a))
        rec("v", lambda: g.vector.tensor_copy(out[0], a[0]), [out], [a], dur)

    def ms(out, val):
        rec("v", lambda: g.vector.memset(out[0], val), [out], [], vec(width(out), narrow(out)))

    def scan(out, d0, d1, op0, op1):
        rec("v", lambda: g.vector.tensor_tensor_scan(out[0], d0[0], d1[0], 0.0, op0, op1), [out], [d0, d1], vec(width(out), narrow(out, d0, d1)))

    def act(out, a, scale=None, bias=0.0, func=AF.Identity, either=True):
        dur = 65 + width(a) * COST["gr"] * cyc if len(a) > 2 else COST["act"] + vec(width(a))
        if func == AF.Sign or not either:
            eng = "s"
        else:
            eng, dur = "f", {"s": dur, "v": dur - 15 if len(a) > 2 else vec(width(a), narrow(out, a))}
        if scale is None:
            fn = {"s": lambda: g.scalar.activation(out[0], a[0], AF.Copy), "v": lambda: g.vector.tensor_copy(out[0], a[0])}
        else:
            fn = {"s": lambda: g.scalar.activation(out[0], a[0], func, bias=ap(bias), scale=ap(scale)),
                  "v": lambda: g.vector.tensor_scalar(out[0], a[0], ap(scale), ap(bias), AL.mult, AL.add if func == AF.Identity else AL.max)}
        rec(eng, fn if eng == "f" else fn["s"], [out], [a, bias, scale], dur)

    def move(eng, out, a):
        if eng == "v":
            cp(out, a)
        else:
            act(out, a, either=eng == "f")

    def gat(eng, out, win, off):
        move(eng, out, IND(win, off))

    def gats(engs, out, win, off, n, c0=0):
        w = n // len(engs)
        for q, eng in enumerate(engs):
            gat(eng, C(out, c0 + 16 * w * q, c0 + 16 * w * (q + 1)), win, off(w * q, w * (q + 1)))

    def mm(out, l, r, start=True, stop=True):
        dur = max(min(64, width(l)), width(r)) * COST["pe"] * (4 if size(l) == 4 else 1)
        rec("t", lambda: g.tensor.matmul(out[0], l[0], r[0], start, stop), [out], [l, r], dur)

    def mms(items):
        for i, (out, l, r) in enumerate(items):
            mm(out, l, r, i == 0, i == len(items) - 1)

    def iota(out, pat, base, cm, integer=False):
        dur = 130 + 2 * width(out) * cyc
        if integer:
            rec("g", lambda: g.iota(out[0], pat, base, cm), [out], [], dur)
        else:
            rec("g", lambda: g.iota(out[0], pat, base, cm, allow_small_or_imprecise_dtypes=True), [out], [], dur)

    def fill(out, val):
        iota(out, [[0, width(out)]], val, 0)

    def fills(name, a, e, val):
        for x in range(a, e, 512):
            fill(C(name, x, min(e, x + 512)), val)

    def asel(out, a, pat, op, val, base, cm):
        rec("g", lambda: g.affine_select(out[0], a[0], pat, op, val, base, cm), [out], [a], 170 + 2 * width(out) * cyc)

    def dma(group, out, a, eng="y"):
        sem_of(group)
        move_ns = out[0].shape[0] * width(out) * size(out) / COST["bw"]
        rec(eng, lambda: Q[eng].dma_start(out[0], a[0]), [out], [a], max(COST["iy"], move_ns) if eng == "y" else COST["iy"], group, 16, COST["dma"] + (0.0 if eng == "y" else move_ns))

    sends = {}

    def arrive(out, group, step):
        sem_of(group)
        sends[group] = [rec("x", None, [out], [], 0.0, group, len(topo.engines(T.cores[(rank - step) % n_ranks], core)))]

    def send(out, a, group, step, after=None):
        to = T.cores[(rank + step) % n_ranks]
        rid, pid = topo.addr(to, core)
        mask = topo.mask(core, to)
        sends[group].append(rec("g", lambda: g.remote_dma(out[0], a[0], sem_of(group), T.sem["sent"], pid, rid, mask), [], [a], COST["ig"], "sent",
                                len(topo.engines(core, to)), COST["rem"] + 128 * width(a) * 2 / COST["rbw"]))
        if after is not None:
            ops[-1]["soft"].add(sends[after][1])

    mult, add, sub, amax, amin = AL.mult, AL.add, AL.subtract, AL.max, AL.min
    ge, gt, le, lt, eq, ne = AL.is_ge, AL.is_gt, AL.is_le, AL.is_lt, AL.is_equal, AL.not_equal
    PM, PM256, SRC0, KIND, C16, PMH = range(6)
    BAR, RR, TKN, EE, HB, DL, CC, UNO, LM, CT, LN, CU = range(12)
    SPOS, SZC, SFL, SPB, SLN = 5, 1, 4, 3, 0

    def every(name, hh, st, a, e):
        return A(name, slice(64 * hh, 64 * hh + 64, st), slice(a, e))

    WEIGHTS = [1.0, 8192.0, 2.0 ** -14, 129.0 / 1024, 1.0 / 16, 1.0 / 32, -16.0]
    ID1, ID8K, IDM14, ID129, ID16, ID32, IDN16 = [A("IDS", al, k) for k in range(7)]

    def rows4(name, hh, f, a, b):
        return A(name, slice(64 * hh + f, 64 * hh + 64, 16), slice(a, b))

    arrive(A("LP1"), "lp1", -3)
    arrive(A("LP2"), "lp2", -6)
    for b in (0, 1):
        for v in (1, 2):
            arrive(A("OFF%d" % b, al, v), "off%d%d" % (v, b), 3)
            arrive(A("ATT%d" % b, al, v), "att%d%d" % (v, b), 3)
            arrive(A("LND%d" % b, al, v - 1, slice(0, 128 * (6 - v))), "lnd%d%d" % (v, b), 3)
    dma("bk", A("BKI"), X(T.bk[:]))
    dma("small", P("SM", 0, 8, 0, 1), X(T.pn[:]))
    dma("small", P("SM", 0, 8, 1, 2), X(T.th[:]))
    dma("small", P("SM", 0, 8, 16, 144), X(T.bl[:]))
    for b in (0, 1):
        for hh in (0, 1):
            for k, src in enumerate((T.pu, T.pt)):
                dma("pp%d" % b, P("PI%d" % b, 64 * hh, 64 * hh + 64, 128 * k, 128 * k + 128), X(src[64 * b:64 * b + 64, 128 * hh:128 * hh + 128]))
            dma("tn%d" % b, P("TN%d" % b, 64 * hh, 64 * hh + 64, 16, 4112), X(T.tones[64 * b:64 * b + 64]))
    for gi in range(8):
        dma("bt", C("BT", 16 * gi, 16 * gi + 16), X(T.bt[gi]), "s")
    dma("bb", A("BI"), X(T.bu[:]))

    ms(A("ONE"), 1.0), ms(A("ONEB"), 1.0), ms(A("NEG"), -1.0)

    def put(out, val):
        act(out, A("ONE", slice(0, out[0].shape[0]), slice(0, width(out))), 0.0, val)

    iota(C("PMI", 0, 1), [[0, 1]], 0, 1, True)
    ts(C("PMI", 1, 2), C("PMI", 0, 1), 15, AL.bitwise_and)
    cp(col(PM), C("PMI", 1, 2))
    act(col(PM256), col(PM), 256.0)
    act(col(SRC0), col(PM), 1.0, float(PB - 16))
    iota(col(C16), [[0, 1]], 16, 16)
    for hh in (0, 1):
        act(P("COL", 64 * hh, 64 * hh + 64, KIND, KIND + 1), P("ONE", 64 * hh, 64 * hh + 64, 0, 1), 16.0 + hh)
        act(P("COL", 64 * hh, 64 * hh + 64, PMH, PMH + 1), P("COL", 64 * hh, 64 * hh + 64, PM, PM + 1), 1.0, 2048.0 * hh)
    iota(A("JI"), [[16, 128]], 0, 0)
    asel(A("IDF"), A("ONE"), [[-1, 128]], eq, 0.0, 0, 1)
    iota(A("BARX"), [[128, 2], [0, 128]], 1, 1)
    cp(A("IDH"), A("IDF"))
    for k, w in enumerate(WEIGHTS):
        act(A("IDS", al, k), A("IDF"), w)
    asel(A("UP"), A("ONE"), [[1, 128]], ge, 0.0, 0, -1)
    asel(A("TRI"), A("NEG"), [[1, 128]], ge, 0.0, 0, -1)
    asel(A("TRI"), A("TRI"), [[1, 128]], ne, 1.0, 0, -1)
    asel(A("BLK"), A("ONE"), [[-16, 8], [0, 16]], ge, 0.0, 0, 1)
    asel(A("BLK"), A("BLK"), [[16, 8], [0, 16]], ge, 0.0, 15, -1)
    SELF = C("BLK", 0, 128, 16)
    act(A("SEL", al, 0), SELF)
    act(A("SEL", al, 1), SELF, 32768.0)
    iota(A("IOC"), [[1, 128]], 1, 0)
    iota(A("SI"), [[0, 8], [1, 16]], 0, 0)
    asel(A("CONT"), A("ONE"), [[0, 8], [1, 16]], gt, 0.0, 0, 0)
    for k, (scale, bias) in enumerate(((-512.0, -8192.0), (0.0, -188416.0), (15.0, 0.0), (1.0, 0.0))):
        act(A("ROWS", slice(0, 1), k), P("SI", 0, 1), scale, bias)
    act(A("ROWS", slice(0, 1), 4), P("JI", 0, 1))
    asel(P("E16", 0, 32), P("ONEB", 0, 32, 0, 128), [[0, 8], [-1, 16]], eq, 0.0, 0, 1)
    mm(C("Pb1", 0, 128), P("E16", 0, 16), P("E16", 0, 16))
    iota(A("DM"), [[1, 128]], DUMMY, 0)
    tt(A("DM"), C("Pb1", 0, 128), A("DM"), mult)
    cp(A("DG"), C("Pb1", 0, 16))
    ms(A("V1"), 0.0), put(C("V1", 48, 64), 32.0), put(C("V1", 112, 128), 32.0)
    ms(A("USEL"), 0.0)
    act(C("USEL", 16, 144, 16), SELF, 0.5)
    asel(P("MK8", 0, 32), P("ONE", 0, 32), [[-1, 8], [0, 16]], eq, 0.0, 0, 1)
    place = {BAR: 16.0, EE: -1.0 / 512, RR: -32.0}
    step = {BAR: -16.0, EE: 1.0 / 512, RR: 32.0, CU: 1.0}
    base = {BAR: 16.0, CC: 1.0, CT: -1.0, UNO: 24.0}
    start = {**place, UNO: 8192.0, TKN: -8192.0}
    slots = [{0: 1.0, 8: 1.0}, {4: 1.0, 12: 1.0}, {6: 1.0}, {2: 1.0},
             {LN: 32.0}, {EE: 1.0 / 32, RR: 512.0, TKN: -256.0}, {**base, TKN: XO - 32.0 + 2048, HB: -4096.0}, {**base, TKN: XO - 32.0},
             {**place, TKN: float(PB), CC: 1.0, CT: -1.0}, start, {**start, LM: 32.0},
             {**{f: -w for f, w in step.items()}, DL: -32.0}, step]
    iota(P("KR", 0, 32), [[8, 16], [0, 64]], -4, 0)
    for k0, k1 in ((0, 4), (4, 13)):
        ms(A("WR", slice(0, 1), slice(k0, k1)), 0.0)
    for k, ws in enumerate(slots):
        for f, w in ws.items():
            if k == 0 or slots[k - 1].get(f) != w:
                e = k + 1
                while e < len(slots) and slots[e].get(f) == w:
                    e += 1
                ms(A("WR", slice(0, 1), slice(k, e), slice(f, 128, 16)), w)
    for k0, k1 in ((0, 4), (4, 13)):
        for k in range(k0, k1):
            mm(C("Pd0", k, k + 1), A("WR", slice(0, 1), k), P("ONEB", 0, 1, 0, 1))
        act(C("WC", k0, k1), C("Pd0", k0, k1))
    for j, k in enumerate((0, 1, 2, 1, 3)):
        act(A("SELT", al, j), SELF, C("WC", k, k + 1))
    ms(A("UZ"), 0.0)
    for k in (0, 1):
        for hh in (0, 1):
            act(C("UZ", 8 + 64 * k + 8 * hh, 72 + 64 * k, 16), C("BLK", 64 * hh, 64 * hh + 64, 16), C("WC", k, k + 1))
    for k in range(4, 11):
        act(A("SY", slice(0, 64), k - 4), P("BLK", 0, 64, 0, 64), P("WC", 0, 64, k, k + 1))
    ms(A("SELI"), 0.0)
    for kind in (0, 1):
        act(A("SELI", slice(64 * kind, 64 * kind + 64), al, slice(16, 32)), P("BLK", 64 * kind, 64 * kind + 64, 64 * kind, 64 * kind + 64), P("WC", 64 * kind, 64 * kind + 64, 12 - kind, 13 - kind))
    for b in (0, 1):
        for a in range(PB - 16, PB + 4096, 1028):
            ms(C("W%d" % b, a, a + 1028), 0.0)
        for a in (T2, T2 + 1032):
            act(C("XW%d" % b, a, a + 1032), C("W0", PB - 16, PB + 1016), 0.0, 99.0)
        now[0] = b
        fills("W%d" % b, 0, PB - 16, 0), fills("W%d" % b, PB + 4096, 8192, 0), fills("U%d" % b, 2064, 4112, 0)
    now[0] = 0
    fill(C("XB", 1024, 1040), 0), fill(C("BTF", 0, 16), 0)
    for b in (0, 1):
        n = str(b)
        fill(C("TN" + n, 0, 16), 0), fill(C("XW" + n, 0, 16), 99), fill(C("XW" + n, XO + 4096, XO + 4112), 0), fill(C("U" + n, 0, 16), 0)
        ms(A("ZP" + n), 0.0), fill(C("LT" + n, 0, 64), 0), cp(C("TS" + n, 256, 272), C("ONE", 0, 16))
        fill(A("TF" + n, al, 0, slice(0, 1)), 16384)
        fill(A("X" + n), 0), fill(A("X" + n, al, al, UNO), 1)
        iota(A("X" + n, al, al, CC), [[0, 4]], 0, 16)
        iota(A("X" + n, al, al, CU), [[0, 4]], -PB, 16)
        fill(A("PAY" + n), 1)
        iota(A("PAY" + n, al, al, BAR), [[128, 2], [0, 4]], 1, 1)
        iota(A("PAY" + n, al, al, HB), [[1, 2], [0, 4]], 0, 0)
        asel(P("MK" + n, 0, 32), P("ONE", 0, 32), [[0, 2], [-1, 4], [0, 16]], eq, 0.0, -4 * b, 1)

    ts(A("RW", al, 0), A("BKI"), 1.0, add, 16.0, mult)
    send(A("LP1"), A("RW", al, 0), "lp1", -3)
    send(A("LP2"), A("RW", al, 0), "lp2", -6)
    ts(A("RW", al, 1), A("ONEB"), col(PM256), mult)
    iota(A("RW", al, 2), [[1, 256]], 1, 0)
    for b in (0, 1):
        now[0] = b
        for f, src in enumerate((A("RW", slice(64 * b, 64 * b + 64), 0), P("LP1", 64 * b, 64 * b + 64), P("LP2", 64 * b, 64 * b + 64))):
            for hh in (0, 1):
                dma("tab%d" % b, rows4("W%d" % b, hh, 2 + 4 * f, PB, PB + 4096), src)
        for k in (1, 2):
            dma("tab%d" % b, A("W%d" % b, slice(8 * k - 4, 128, 16), slice(PB, PB + 4096)), A("RW", al, k))
    now[0] = 0
    ts(A("BX"), A("BI"), 1.0, add)
    act(A("BD", al, 0), A("BX"))
    tt(A("BD", al, 1), A("BX"), A("BD", al, 0), sub)
    cp(P("SMF", 0, 8, 0, 2), P("SM", 0, 8, 0, 2))
    cp(P("SMF", 0, 8, 16, 144), P("SM", 0, 8, 16, 144))
    cp(C("BTF", 16, 144), A("BT"))
    LB = C("Pd1", 0, 128)
    mm(LB, P("SMF", 0, 8, 16, 144), P("MK8", 0, 8))
    tt(A("NEB", al, 0), LB, A("SI"), gt)
    for b in (0, 1):
        ts(A("X%d" % b, al, al, LM), C("Pd1", 64 * b, 64 * b + 64, 16), -1.0, add, 1.0 / 32, mult)
    tt(A("NEB", al, 1), C("BTF", 16, 144), C("BTF", 15, 143), ne)
    tt(A("NEB", al, 0), A("NEB", al, 0), A("NEB", al, 1), mult)
    scan(A("CN"), A("NEB", al, 0), A("CONT"), add, mult)
    ts(A("NTC"), C("CN", 15, 128, 16), col(C16), add)
    for gi in range(8):
        ts(C("NTA", 16 * gi, 16 * gi + 16), A("DG"), C("NTC", gi, gi + 1), mult)

    def key_table(b, first):
        n = str(b)
        move(OPT["ZS"], C("XL" + n, 0, 64), C("Pa" + n, 0, 64))
        for j, bank in enumerate((lambda k0, k1: A("Pc" + n, al, slice(k0 // 2, k1 // 2)) if k1 - k0 > 1 else A("Pc" + n, al, k0 // 2, slice(4 * (k0 % 2), 4 * (k0 % 2) + 4)),
                                  lambda k0, k1: C("Pd" + n, 64 * k0, 64 * k1))):
            row = (bank(0, 8), P("ONEB", 0, 1, 0, 128), P("KR", 0, 1, 512 * j, 512 * j + 512))
            mms([row] + [(bank(k, k + 1), IDN16, C("XL" + n, 0, 64)) for k in range(8)] + [row])
            act(A("SG", al, slice(8 * j, 8 * j + 8)), bank(0, 8), 1.0, 0.0, AF.Sign)
        out = C("Pa" + n, 64, 128)
        items = [(out, C("USEL", 16 - k, 144 - k), A("SG", al, k)) for k in range(16)]
        if first:
            items.append((out, P("ONEB", 0, 1, 0, 128), A("ROWS", slice(0, 1), 4, slice(0, 64))))
        else:
            items[1:1] = [(P("Pa" + n, 64 * hh, 64 * hh + 64, 64, 128), A("SY", slice(0, 64), SPB - hh), P("YS" + n, 0, 64, 64 * hh, 64 * hh + 64)) for hh in (0, 1)]
        mms(items)
        ts(A("LS" + n, al, 0), out, 8.0 if first else 0.0, add)
        gats(OPT["TB"], "TBN" + n, A("XB") if first else A("XW" + n), lambda a, e: A("LS" + n, al, 0, slice(a, e)), 64)
        tag = "tb%d%d" % (b, len(ops))
        for hh in (0, 1):
            for h2 in (0, 1):
                dma(tag, P("XW" + n, 64 * h2, 64 * h2 + 64, 16 + 1024 * hh, 1040 + 1024 * hh), P("TBN" + n, 64 * hh, 64 * hh + 64))
        gat(OPT["XL"], A("XL" + n), C("XW" + n, 0, T2), A("NTL" + n))
        cp(IND(C("XW" + n, T2, XO), A("NTL" + n)), A("XL" + n))

    def turn(b, src, sel, lo, c0=0):
        for s in range(16):
            mm(A("Pc%d" % b, al, slice(lo, 3), al, s), C(src, c0 + s, c0 + 2048, 16), A("SELT", al, slice(3 * sel, 3 + 2 * sel)))
        ts(C("TS%d" % b, 128 * lo, 256), A("Pc%d" % b, al, slice(lo, 2)), -2048.0, add)

    def marks(b, out):
        n = str(b)
        act(out(0), A("Pc" + n, al, 2))
        act(out(2), A("Pc" + n, al, 1), -2.0, 2.0, AF.Relu, False)
        tt(out(1), C("TS" + n, 128, 256), C("TS" + n, 129, 257), ne)

    def opening(b):
        n = str(b)
        W = "W" + n
        mm(C("Pa" + n, 0, 1), P("MK" + n, 0, 8), P("SMF", 0, 8, 0, 1))
        tt(A("TI" + n, al, 0, slice(0, 1)), C("Pa" + n, 0, 1), col(PMH), sub)
        ts(A("JM" + n), A("JI"), A("TI" + n, al, 0, slice(0, 1)), ge, -8192.0, mult)
        for k in (1, 0):
            tt(C("Y0" + n, 128 * k, 128 * k + 128), C("PI" + n, 128 * k, 128 * k + 128), A("JM" + n), add)
            ts(A("OFF" + n, al, 0, slice(128 * k, 128 * k + 128)), C("Y0" + n, 128 * k, 128 * k + 128), -1.0, amax, 16.0, add)
        ts(P("THX" + n, 0, 8), P("MK" + n, 0, 8), P("SMF", 0, 8, 1, 2), mult, -1.0, mult)
        act(A("THB" + n, slice(0, 8), 0), P("THX" + n, 0, 8))
        put(A("THB" + n, slice(0, 32), 1), -8192.0), put(A("THB" + n, slice(0, 32), 1, slice(15, 128, 16)), 8192.0)
        tt(A("THB" + n, slice(0, 8), 1), P("THX" + n, 0, 8), A("THB" + n, slice(0, 8), 0), sub)
        for hh in (0, 1):
            mm(P("Pb" + n, 64 * hh, 64 * hh + 64, 128, 192), C("BTF", 16 + 64 * b, 80 + 64 * b), C("IDF", 64 * hh, 64 * hh + 64))
        for hh in (0, 1):
            mm(A("Pb" + n, slice(64 * hh, 64 * hh + 64), 12, slice(0, 8)), C("NTA", 64 * b, 64 * b + 64), SELF)
        ts(A("LS" + n, al, 1), C("Pb" + n, 128, 192), 16.0, add)
        cp(A("NTL" + n), A("Pb" + n, al, 12, slice(0, 8)))
        gats(OPT["XB"], "XB", A("TN" + n), lambda a, e: A("LS" + n, al, 1, slice(a, e)), 64)
        for hh in (0, 1):
            mm(P("Pa" + n, 64 * hh, 64 * hh + 64, 0, 64), C("CN", 64 * b, 64 * b + 64), A("IDS", al, 0, slice(64 * hh, 64 * hh + 64)))
        key_table(b, True)
        ts(C("Y0" + n, 0, 128), C("Y0" + n, 0, 128), -1.0, amax, 1.0, add)
        act(C("DU" + n, 0, 128), C("Y0" + n, 0, 128))
        tt(C("DU" + n, 128, 256), C("Y0" + n, 0, 128), C("DU" + n, 0, 128), sub)
        for bl in range(4):
            mm(A("Pb" + n, slice(0, 64), slice(bl, 32, 4)), C("DU" + n, bl, 256, 4), ID1)
        act(A("RS", slice(0, 64)), A("Pb" + n, slice(0, 64)))
        gats(OPT["CO"], "CO", C(W, PB - 16, PB + 4096), lambda a, e: A("OFF" + n, al, 0, slice(128 + a, 128 + e)), 128)
        gats(OPT["CB"], "CB", C(W, PB - 16, PB + 4096), lambda a, e: A("LS" + n, al, 1, slice(a, e)), 64)
        turn(b, "CO", 1, 1)
        marks(b, lambda k: A("ATT" + n, al, 0, slice(128 * k, 128 * k + 128)))
        for hh in (0, 1):
            for h2 in (0, 1):
                dma("row0" + n, every(W, h2, 2, PB + 2048 * hh, PB + 2048 * hh + 2048), every("CO", hh, 2, 0, 2048))
                dma("row0" + n, every(W, h2, 2, 1024 * hh, 1024 * hh + 1024), every("CB", hh, 2, 0, 1024))
        for k in range(8):
            p, c0 = 16 * (k % 4), PB + 2048 * (k // 4)
            dma("row1" + n, A(W, slice(p, p + 16, 8), slice(c0, c0 + 2048)), A("RS", slice(0, 64), k))
        for f in (0, 1):
            dma("row1" + n, rows4(W, 0, 8 * f, 0, PB), A("BD", slice(64 * b, 64 * b + 64), f))
        dma("row2" + n, every(W, 1, 8, 0, PB + 4096), every(W, 0, 8, 0, PB + 4096))

    def visit(v, b):
        n = str(b)
        W, XW, TN, Xn, YS, U = "W" + n, "XW" + n, "TN" + n, "X" + n, "YS" + n, "U" + n
        Pa, Pb, Pc, Pd = ["P" + k + n for k in "abcd"]
        END, CNT, AC, K, CL, RL = range(6)

        def tf(k, a=0):
            return A("TF" + n, al, k, slice(a, a + 128))

        def att(a):
            return A("ATT" + n, al, v, slice(a, a + 128))

        def xc(k, gi=None):
            return A(Xn, al, al, k) if gi is None else A(Xn, al, gi, slice(k, k + 1))

        def half(name, hh, a, b_):
            return P(name, 64 * hh, 64 * hh + 64, a, b_)

        def sy(k, hh):
            return A("SY", slice(0, 64), k)

        def clear(k):
            fills(U, 16 + 2048 * k, 2064 + 2048 * k, 0)

        nq = OPT["NQ"]
        w = 128 // nq
        for q in range(nq):
            xt = C(XW, XO + 16 * w * q, XO + 16 * w * (q + 1))
            gat(OPT["XT"], xt, A(TN), A("OFF" + n, al, v, slice(128 + w * q, 128 + w * (q + 1))))
            tt(C(U, 16 + 16 * w * q, 16 + 16 * w * (q + 1)), IND(A(TN), A("OFF" + n, al, v, slice(w * q, w * (q + 1)))), xt, mult)
        if v < 2:
            for hh in (0, 1):
                dma("swap%d%d" % (v, b), half(XW, 1 - hh, XO + 2048, XO + 4096), half(XW, hh, XO, XO + 2048))
        mm(C(Pa, 128, 256), IDM14, att(0))
        SC = C(Pa, 0, 128)
        mms([(SC, ID8K, att(128))] + [(SC, P("ONEB", 0, 8, 0, 128), A("THB" + n, slice(0, 8), 0)), (C(Pa, 0, 127), ID8K, A("ATT" + n, al, v, slice(257, 384)))] +
            [(C(Pa, s, 128, 16), C(U, 16 + s, 2064, 16), A("SEL", al, 0)) for s in range(16)] + [(SC, P("ONEB", 0, 9, 0, 128), A("THB" + n, slice(0, 9), 1))])
        clear(0)
        ts(tf(END, 1), SC, 0.0, ge, 16384.0, mult)
        if OPT["CNT"] == "s":
            act(tf(CNT), tf(END), -2.0 ** -14, 1.0)
        else:
            ts(tf(CNT), tf(END), 0.0, eq)
        tt(tf(AC), C(Pa, 128, 256), tf(END), mult)
        scan(tf(K), att(127), tf(CNT), add, mult)
        scan(tf(CL), tf(CNT), tf(AC), mult, add)
        scan(tf(RL), C("ONEB", 0, 128), tf(CNT), add, mult)
        IX = C(Pa, 256, 384)
        mms([(IX, tf(END, 1), ID129), (IX, tf(K), ID1), (IX, tf(CL), ID1)])
        cp(A("IDX" + n), IX)
        one = P("ONEB", 0, 1, 0, 128)
        PV, Z = C(Pb, 0, 128), C(Pb, 128, 256)
        mms([(PV, one, A("ROWS", slice(0, 1), 0)), (PV, ID1, tf(END, 1)), (PV, ID16, tf(CL)), (PV, ID32, tf(RL))])
        if v < 2:
            mms([(Z, one, A("ROWS", slice(0, 1), 2)), (Z, ID1, tf(K)), (Z, IDN16, tf(RL))])
            act(A("ZP" + n, al, al, slice(48, 64)), Z)
        for q in range(OPT["NE"]):
            u = 128 // OPT["NE"]
            tt(C("EQ" + n, 16 * u * q, 16 * u * (q + 1)), IND(C(XW, 0, XO), C("IDX" + n, u * q, u * (q + 1))), C(XW, XO + 16 * u * q, XO + 16 * u * (q + 1)), eq)
        CB = C(Pa, 384, 512)
        mms([(CB, one, A("ROWS", slice(0, 1), 1))] + [(C(Pa, 384 + s, 512, 16), C("EQ" + n, s, 2048, 16), A("SEL", al, 1)) for s in range(16)] +
            [(CB, one, A("ROWS", slice(0, 1), 1))])
        MN, VAL, OV, LV = [A("FS" + n, al, k) for k in range(4)]
        scan(MN, tf(END), CB, amax, amin)
        tt(VAL, PV, MN, amin)
        scan(OV, A("CONT"), VAL, mult, amax)
        best, REM, C1 = A("FS" + n, al, 2, slice(15, 128, 16)), A("TI" + n, al, 1), A("TI" + n, al, 2)
        ts(A("PAY" + n, al, al, EE), best, 1.5 * 2.0 ** 32, add, -1.5 * 2.0 ** 32, add)
        tt(REM, best, A("PAY" + n, al, al, EE), sub)
        ts(C1, REM, 1.5 * 2.0 ** 23, add, -1.5 * 2.0 ** 23, add)
        for k in range(8):
            ts(C("OH", 128 * k, 128 * k + 128), A("IOC"), A("TI" + n, al, 2, slice(k, k + 1)), eq)
        tt(A("PAY" + n, al, al, RR), REM, C1, sub)
        mm(A(Pc), A("TRI"), C("OH", 0, 512))
        mms([(A(Pd), A("NEG"), C("OH", 0, 512)), (A(Pd), A("TRI"), C("OH", 512, 1024))])
        act(C("TK" + n, 0, 512), A(Pc), 1.0, 0.0, AF.Relu)
        if OPT["TK1"] == "s":
            act(C("TK" + n, 512, 1024), A(Pd), 1.0, 0.0, AF.Relu)
        else:
            ts(C("TK" + n, 512, 1024), A(Pd), 0.0, amax)
        for gi in range(4):
            mms([(A(Pb, al, 16 + gi, slice(0, 5)), C("TK" + n, 512 * hh + 128 * gi, 512 * hh + 128 * gi + 128), A("PAY" + n, al, 4 * hh + gi, slice(0, 5))) for hh in (0, 1)])
        mms([(A(Pc), A("BARX", al, hh), C("TK" + n, 512 * hh, 512 * hh + 512)) for hh in (0, 1)])
        move(OPT["XC"], A(Xn, al, al, slice(0, 5)), A(Pb, al, slice(16, 20), slice(0, 5)))
        TMP = A("TI" + n, al, 3, slice(0, 4))
        tt(TMP, xc(TKN), xc(LM), mult)
        tt(xc(DL), TMP, xc(RR), sub)
        tt(xc(CT), xc(TKN), xc(CC), mult)
        if v == 2:
            tt(xc(LN), xc(LM), xc(DL), sub)
        for hh in (0, 1):
            mm(half(Pb, hh, 320, 448), A(Xn), ID1)
        move(OPT["YS"], A(YS), C(Pb, 320, 448))
        if v < 2:
            tt(xc(LM), xc(LM), xc(DL), sub)
        for gi in range(4):
            ts(A("MG" + n, al, gi), A(Pc, al, gi), xc(BAR, gi), gt, xc(DL, gi), mult)
        POS = C(Pd, 0, 128)
        mms([(POS, C("V1", 48 - 16 * gi, 176 - 16 * gi), A("MG" + n, al, gi)) for gi in range(4)] + [(POS, A("SY", slice(0, 64), slice(SPOS, SPOS + 2)), P(YS, 0, 64))])
        tt(LV, POS, A("DM"), amin)
        scan(MN, A("CONT"), LV, mult, add)
        ts(A("EL" + n), A("FS" + n, al, 0, slice(15, 128, 16)), col(KIND), add)
        cp(IND(A(U), A("EL" + n)), A(YS))
        for hh in (0, 1):
            mms([(A(Pc, al, 0, slice(4 * hh, 4 * hh + 4)), C(U, 16 + 2048 * hh + o, 2064 + 2048 * hh + o, 16), A("SELI", al, al, slice(16 - o, 32 - o))) for o in range(-15, 16)])
        if v < 2:
            clear(1)
        if OPT["LT"] == "s":
            act(C("LT" + n, 64, 192), A(Pc, al, 0), 1.0, 16.0)
        else:
            ts(C("LT" + n, 64, 192), A(Pc, al, 0), 16.0, add)
        SRC = C(Pd, 128, 256)
        mms([(SRC, C("LT" + n, 64, 192), A("UP")), (SRC, C("LT" + n, 0, 128), A("ONE"))])
        ts(A("SRU" + n), SRC, col(SRC0), add)
        gats(OPT["EO"], U, A(W), lambda a, e: C("SRU" + n, a, e), 128, EO)
        for hh in (0, 1):
            mm(half(Pb, hh, 448, 512), sy(SFL, hh), P(YS, 0, 64, 64 * hh, 64 * hh + 64))
        FL = A("LS" + n, al, 2)
        if v < 2:
            ts(FL, C(Pb, 448, 512), col(PM), add)
        else:
            for hh in (0, 1):
                mm(half(Pb, hh, 0, 64), sy(SLN, hh), P(YS, 0, 64, 64 * hh, 64 * hh + 64))
            T1, T2_ = A("FS" + n, al, 1, slice(0, 64)), A("FS" + n, al, 1, slice(64, 128))
            ts(T1, C(Pb, 0, 64), col(PM), lt, 16384.0, mult)
            tt(T2_, C(Pb, 448, 512), T1, add)
            ts(FL, T2_, col(PM), add, 8000.0, amin)
        turn(b, U, 0, 0, EO)
        for k in (1, 0):
            mm(C(Pd, 256 + 128 * k, 384 + 128 * k), C("TS" + n, 128 * k, 128 * k + 128), A("IDH"))
        if v < 2:
            ts(A("OUT" + n, al, v), C(Pd, 256, 512), 2063.0, add)
            send(A("OFF" + n, al, v + 1), A("OUT" + n, al, v), "off%d%d" % (v + 1, b), 3)
            marks(b, lambda k: A("ATO" + n, al, v, slice(128 * k, 128 * k + 128)))
            send(A("ATT" + n, al, v + 1), A("ATO" + n, al, v), "att%d%d" % (v + 1, b), 3, "off%d%d" % (v + 1, b))
            dma("stg%d%d" % (v, b), A("STG" + n, al, v, slice(0, 512)), A(U, slice(0, 128, 4), slice(EO, EO + 2048)))
            if v == 0:
                dma("stg%d%d" % (v, b), A("STG" + n, al, v, slice(512, 640)), A(U, slice(10, 128, 16), slice(EO, EO + 2048)))
            send(A("LND" + n, al, v, slice(0, 640 - 128 * v)), A("STG" + n, al, v, slice(0, 640 - 128 * v)), "lnd%d%d" % (v + 1, b), 3, "att%d%d" % (v + 1, b))
        else:
            act(A("Y0" + n), C(Pd, 256, 512), 1.0, 2047.0)
            for k, dst in enumerate((T.yu, T.yt)):
                for hh in (0, 1):
                    dma("yo" + n, X(dst[64 * b:64 * b + 64, 128 * hh:128 * hh + 128]), half("Y0" + n, hh, 128 * k, 128 * k + 128))
        gats(OPT["FO"], "FO" + n, A(W), lambda a, e: A("LS" + n, al, 2, slice(a, e)), 64)
        if v < 2:
            for h2 in (0, 1):
                out = half(Pa, h2, 0, 64)
                mms([(out, A("ROWS", slice(0, 1), 3, slice(0, 64)), P("ONEB", 0, 1, 0, 64)), (out, sy(SZC, h2), P(YS, 0, 64, 64 * h2, 64 * h2 + 64))] +
                    [(out, A("ZP" + n, al, k, slice(48 - 16 * (k % 4), 112 - 16 * (k % 4))), C("TK" + n, 128 * k + 64 * h2, 128 * k + 64 * h2 + 64)) for k in range(8)])
            key_table(b, False)
            for hh in (0, 1):
                for h2 in (0, 1):
                    dma("fo%d%d" % (v, b), every(W, h2, 2 + 2 * v, 1024 * hh, 1024 * hh + 1024), every("FO" + n, hh, 2 + 2 * v, 0, 1024))
                    dma("rows%d%d" % (v, b), every(W, h2, 4, PB + 2048 * hh, PB + 2048 * hh + 2048), A("LND" + n, slice(64 * hh, 64 * hh + 64), v, slice(0, 512)))
                    if v == 0:
                        dma("rows%d%d" % (v, b), rows4(W, h2, 6, PB + 2048 * hh, PB + 2048 * hh + 2048), A("LND" + n, slice(64 * hh, 64 * hh + 64), v, slice(512, 640)))
        else:
            ZO = C(Pa, 0, 128)
            mms([(ZO, C("UZ", 8 - q, 136 - q), C("FO" + n, 128 * q, 128 * q + 128)) for q in range(8)])
            act(A("JM" + n), ZO, 1.0, -1.0)
            for k, dst in enumerate((T.zu, T.zt)):
                dma("zo" + n, X(dst[4 * b:4 * b + 4]), P("JM" + n, 64 * k, 64 * k + 64))

    for b in (0, 1):
        now[0] = b
        opening(b)
    for v in range(3):
        for b in (0, 1):
            now[0] = b
            visit(v, b)

    if not planned:
        for o in ops:
            o["all"] = set(o["soft"])
            for j in o["deps"]:
                o["all"].update(grp[ops[j]["grp"]] if ops[j]["grp"] is not None else [j])
        for arr, snd in sends.values():
            ops[arr]["all"].add(snd)
        succ = [[] for _ in ops]
        for i, o in enumerate(ops):
            for j in o["all"]:
                succ[j].append(i)

        def gap(j, i):
            return 0.0 if j in ops[i]["soft"] else ops[j]["lat"] + (0.0 if ops[i]["eng"] == "x" else COST["sem"])

        left = [len(o["all"]) for o in ops]
        topo_order = [i for i in range(len(ops)) if not left[i]]
        for i in topo_order:
            for j in succ[i]:
                left[j] -= 1
                if not left[j]:
                    topo_order.append(j)
        way, taken = [0.0] * len(ops), {}
        for i in reversed(topo_order):
            way[i] = (ops[i]["dur"]["s"] if ops[i]["eng"] == "f" else ops[i]["dur"]) + max([gap(i, j) + way[j] for j in succ[i]] + [ops[i]["lat"]])
        way = [w + (OPT["lead"] if ops[i]["batch"] == 0 else 0.0) for i, w in enumerate(way)]
        left = [len(o["all"]) for o in ops]
        ready = {e: [] for e in "gvstyxf"}
        at = [0.0] * len(ops)
        for i, o in enumerate(ops):
            if not left[i]:
                ready[o["eng"]].append(i)
        free = {e: 0.0 for e in "gsvtyx"}
        order = []

        def cost(i, e):
            return ops[i]["dur"][e] if ops[i]["eng"] == "f" else ops[i]["dur"]

        while len(order) < len(ops):
            pick = None
            for e in free:
                r = ready[e] + ready["f"] if e in "vs" else ready[e]
                if r:
                    t = max(free[e], min(at[i] for i in r))

                    def worth(i):
                        return way[i] - OPT["look"] * max(0.0, at[i] - t) - (OPT["shy"] if e == "v" and ops[i]["eng"] == "f" else 0.0), -i

                    i = max(r, key=worth)
                    fits = [j for j in r if max(at[j], t) + cost(j, e) <= at[i] + OPT["slack"] and j != i]
                    if at[i] > t and fits:
                        i = max(fits, key=worth)
                    t = max(t, at[i])
                    if pick is None or t < pick[0]:
                        pick = (t, e, i)
            t, e, i = pick
            ready[ops[i]["eng"]].remove(i)
            order.append(i)
            free[e] = t + cost(i, e)
            if ops[i]["eng"] == "f":
                ops[i]["eng"], taken[i] = e, e
            for j in succ[i]:
                at[j] = max(at[j], free[e] + gap(i, j))
                left[j] -= 1
                if not left[j]:
                    ready[ops[j]["eng"]].append(j)
        know = {e: {} for e in Q}
        seen, need, pos, cnt, waits = {}, set(), {}, {e: 0 for e in Q}, {}
        when = {i: k for k, i in enumerate(order)}
        for i in order:
            o = ops[i]
            e = o["eng"]
            waits[i] = []
            if e == "x":
                seen[i], pos[i] = {}, 0
                continue
            k = know[e]
            for j in sorted(o["deps"], key=lambda j: -when[j]):
                gj = ops[j]["grp"]
                key, val = (gj, 1) if gj is not None else (ops[j]["eng"], pos[j])
                if k.get(key, 0) >= val:
                    continue
                waits[i].append(j)
                need.add(j)
                k[key] = val
                for m in (grp[gj] if gj is not None else [j]):
                    for kk, vv in seen[m].items():
                        if k.get(kk, 0) < vv:
                            k[kk] = vv
            cnt[e] += 1
            pos[i] = cnt[e]
            seen[i] = dict(k)
        PLAN.update({"order": order, "waits": waits, "need": need, "span": max(free.values()), "taken": taken})
    order, waits, need = PLAN["order"], PLAN["waits"], PLAN["need"]
    for i, e in PLAN["taken"].items():
        ops[i]["eng"], ops[i]["fn"] = e, ops[i]["fn"][e]
    total = {e: 0 for e in Q}
    val = {}
    for i in order:
        if ops[i]["grp"] is None and i in need:
            total[ops[i]["eng"]] += 1
            val[i] = total[ops[i]["eng"]]
    gsum = {k: sum(ops[m]["inc"] for m in members) for k, members in grp.items()}
    for i in order:
        o = ops[i]
        e = o["eng"]
        if e == "x":
            continue
        for j in waits[i]:
            gj = ops[j]["grp"]
            if gj is not None:
                Q[e].wait_ge(sem_of(gj), gsum[gj])
            else:
                Q[e].wait_ge(T.sem["c" + ops[j]["eng"]], val[j])
        ins = o["fn"]()
        if o["grp"] is not None:
            if o["grp"] != "sent":
                ins.then_inc(sem_of(o["grp"]), 16)
        elif i in need:
            ins.then_inc(T.sem["c" + e], 1)
    for e in "vstg":
        if total[e]:
            g.wait_ge(T.sem["c" + e], total[e])
    for k in gsum:
        g.wait_ge(T.sem["sent"] if k == "sent" else sem_of(k), gsum[k])
